import numpy as np, ml_dtypes
CORES = [35,38,43,46]
N = 4
import mx_ref
BF = ml_dtypes.bfloat16
def gcols(t, e):
    v = np.concatenate([t.reshape(8, 16, -1, 4), np.zeros((8, 16, 1, 4), BF)], axis=2)
    return np.ascontiguousarray(np.stack([v[g][:, e[g]] for g in range(8)])).reshape(128, -1)
def tile(rs):
    return np.stack(rs, axis=2).reshape(128, -1).astype(BF)
def pick(q, e):
    c = np.concatenate([q[0].reshape(128, -1, 4), np.zeros((128, 1, 4), np.uint8)], axis=1); s = np.concatenate([q[1], np.ones((16, 1), np.uint8)], axis=1)
    return (np.ascontiguousarray(c[:, e].reshape(128, -1)), np.ascontiguousarray(s[:, e]))
def join(*qs):
    return (np.concatenate([q[0] for q in qs], axis=1), np.concatenate([q[1] for q in qs], axis=1))
def put(q, e, v):
    c, s = q[0].reshape(128, -1, 4).copy(), q[1].copy(); c[:, e] = v[0].reshape(128, -1, 4); s[:, e] = v[1]
    return (c.reshape(128, -1), s)
def pk(c, s):
    return (np.ascontiguousarray(c), mx_ref.live(s))
def emit(q):
    return q[0], q[1]
def packed(v, rng):
    q = [mx_ref.quantize(np.ascontiguousarray(v[r])) for r in range(N)]
    return np.stack([a for a, b in q]), np.stack([mx_ref.plane(b, rng) for a, b in q])
def values_of_codes():
    e, c = np.zeros((128, 128, 4), np.float32), np.zeros((128, 2, 4), np.uint8)
    e[np.arange(128), np.arange(128), 0] = 1
    c[:127, :, 0] = np.arange(256).reshape(2, 128).T[:127]
    return mx_ref.matmul(mx_ref.quantize(e.reshape(128, 512).astype(BF)), (c.reshape(128, 8), np.full((16, 2), 127, np.uint8))).T.reshape(-1).astype(np.float64)
CODE_VALUE, SCALE_VALUE = values_of_codes(), 2.0 ** (np.arange(256) - 127.0)
def decode(q):
    return (CODE_VALUE[q[0]].reshape(16, 8, -1, 4) * SCALE_VALUE[q[1]][:, None, :, None] + 0.0).reshape(128, -1).astype(np.float32)
def f(rng, *shape):
    return mx_ref.flush((rng.standard_normal(shape, dtype=np.float32) * np.exp2(rng.integers(-2, 3, shape[:-1] + (1,)))).astype(BF))
def wide(rng, *shape, cols=0):
    v = rng.standard_normal(shape, dtype=np.float32) * np.exp2(rng.integers(-12, 13, shape)).astype(np.float32)
    if cols: v *= np.repeat(np.exp2(rng.integers(-cols, cols + 1, shape[:-2] + (1, shape[-1] // 4))) * (rng.random(shape[:-2] + (1, shape[-1] // 4)) > 0.0625), 4, axis=-1).astype(np.float32)
    return mx_ref.flush(v.astype(BF))
C, H, B, P, R = 320, 160, 64, 3, 3
def addresses(s, c):
    key = np.sum((s > 0).reshape(8, 16, -1) * (1 << np.arange(16))[:, None], axis=1)
    return B * np.arange(3)[:, None] + ((key[:, None] * c.astype(np.int64)[:, None] >> 8) & (B - 1))
def written(d, a):
    left, peel, own = np.ones((8, H), bool), np.full((8, H), -1), np.zeros((8, H), int)
    for p in range(P):
        alone = np.zeros((8, 3, H), bool)
        for g in range(8): alone[g] = np.bincount(a[g][:, left[g]].reshape(-1), minlength=3 * B)[a[g]] == 1
        taken = left & alone.any(axis=1)
        peel[taken] = p
        own[taken] = np.argmax(alone, axis=1)[taken]
        left = left & ~taken
    cell, one, two = [np.take_along_axis(a, k[:, None], axis=1)[:, 0] for k in (own, np.where(own == 0, 1, 0), np.where(own == 2, 1, 2))]
    z = np.zeros((128, 12 * B), BF)
    for p in range(P - 1, -1, -1):
        n = ((d.astype(np.float32) - gcols(z, one).astype(np.float32)) - gcols(z, two).astype(np.float32)).astype(BF).reshape(8, 16, H, 4)
        w = z.reshape(8, 16, 3 * B, 4)
        for g in range(8): w[g][:, cell[g, peel[g] == p]] = n[g][:, peel[g] == p]
    return z
def big(v):
    v = v.astype(np.float32)
    v[np.abs(v) < np.float32(2.0 ** -16)] = 0
    return v.astype(BF)
def same(v):
    return np.repeat(v[None], N, axis=0)
def numbers_of(rng):
    return {"x": big(f(rng, N, 128, 4 * C)), "u": same(np.array(f(rng, 128, 512))), "v": np.array(f(rng, N, 128, 512))}
def weights(rng, still=0):
    w = big(f(rng, N, 128, 2048)).reshape(N, 8, 16, 4, 8, 16, 4)
    w[:, :, :, :, :, :still] = 0
    c, p = packed(w.reshape(N, 128, 2048), rng)
    return {"wc": c, "ws": p}
def factors(c):
    return {"hc": np.zeros((N, 128, 3), np.int32) + np.asarray(c).astype(np.int32)}
def odd(rng):
    return rng.permutation(128)[:3] * 2 + 1
def three(a, b):
    c = -a - b
    return np.array([[a, b, c], [b, c, a]]).reshape(2, -1)
def marked(rng, keys, size, k, fine=False):
    d = numbers_of(rng)
    x = d["x"].reshape(N, 8, 16, C, 4)
    x[:, :, :8] = 0
    u = np.zeros((128, 128, 4), np.float32)
    for i in range(16):
        m = np.where((keys >> i) & 1 == 1, 1, -rng.integers(0, 2, keys.shape)) * size
        x[:, :, i // 4, :, i % 4] = (m * np.where(fine, -1.25, 1.0) + 0.0).astype(np.float32).astype(BF)
        x[:, :, 4 + i // 4, :, i % 4] = (m * np.where(fine, 1.125, 0.0) + 0.0).astype(np.float32).astype(BF)
        for h in range(0, 128, 16):
            u[h + i // 4, h + i, i % 4] = k
            u[h + 4 + i // 4, h + i, i % 4] = 1.125 * k
    return {"x": x.reshape(N, 128, 4 * C), "u": same(u.reshape(128, 512).astype(BF)), "v": d["v"], **weights(rng, 8)}
def setup_inputs(rng):
    return {**numbers_of(rng), **weights(rng), **factors(odd(rng))}
def setup_inputs_near(rng):
    size = np.where(rng.permutation(N) < N // 2, 2.0 ** -30, 1.0)
    return {**marked(rng, rng.integers(0, 65536, (N, 8, C)), size[:, None, None], 2.0 ** -30), **factors(odd(rng))}
def setup_inputs_loads(rng):
    keys = rng.integers(0, 65536, (N, 8, C))
    size, fine = np.ones((N, 8, C)), np.zeros((N, 8, C), bool)
    n, last, j, cell = np.arange(H), np.full(H, B - 1), np.arange(28), np.arange(64)
    y = cell[cell % 8 > 0]
    q = y[y < 57]
    own = np.concatenate([[cell[8:], -cell[8:] & 56], [-y & 7, y], [q & 7, q & 56]], axis=1)
    second = np.concatenate([three(9 + 2 * j[:14], 37 + 2 * j[:14]), three(j // 4 * 8, j % 4 * 2 + 1), [[8, 4], [0, 4]]], axis=1)
    deep = np.concatenate([three(6 - 4 * j[:6], -18 - 4 * j[:6]), three(17 + 2 * j[:12], 41 + 2 * j[:12]), three(j[:24] // 4 * 8, j[:24] % 4 * 2 + 1)], axis=1)
    chains = [np.pad(k, ((0, 0), (0, H - k.shape[1]))) for k in (second, deep)]
    sign = np.concatenate([np.tile([1, 1, 1, -1, -1, -1], 3), np.tile([1, 1, 1, 0, 0, 0, 0, 0, 0, -1, -1, -1], 3), np.zeros(H - 54, int)])
    large = (6 - 4 * np.array([0, 1, 2, 9, 10, 11])) & 63
    asks = np.array([(s[i], s[k]) for s in ((6, -34, 28), (2, -30, 28), (2, -38, 36), (-2, -34, 36)) for i in range(3) for k in range(3) if i != k]).T
    first = [rng.permutation(8) for r in range(N)]
    shift = rng.integers(0, 64, (N, 2, 2, 2, 1))
    spot = []
    for r in range(N):
        for h in range(2):
            lo = H * h
            m = np.where(n < 128, n, rng.integers(10, 51, H))
            l = m.copy()
            l[0] = rng.integers(10, 51)
            s = last.copy()
            s[0] = 5
            o = first[r]
            if h == 1:
                e = first[r - 1][[2, 5, 6]]
                o = np.zeros(8, int)
                o[[3, 4, 7]] = e
                o[[0, 1, 2, 5, 6]] = rng.permutation(np.setdiff1d(np.arange(8), e))
            most = own[:, rng.permutation(161)[:H]]
            for i, (a, b) in enumerate([(last, last), (s, last), most, ((m + 1) // 2, m // 2), ((l + 1) // 2, l // 2)] + [chains[k] + shift[r, h, k] for k in range(2)]):
                e = rng.permutation(H)
                keys[r, o[i], lo + e] = ((a & 63) << 8) + ((b & 63) << 2) + (rng.integers(0, 4, H) << 14)
            fine[r, o[2], lo:lo + H] = True
            size[r, o[2], lo:lo + H] = 2.0 ** -30
            if h == 0: spot.append(e)
            if h == 1:
                k = keys[r, o[7], H:].copy()
                p, t = shift[r - 1, 0, 1]
                hit = np.isin(((k >> 8) - p) & 63, large) | np.isin(((k >> 2) - t) & 63, large) | np.isin((p + t - (k * 65 >> 8)) & 63, large)
                hit[rng.permutation(H)[:24]] = True
                i = np.flatnonzero(hit)
                a, b = asks[:, np.arange(len(i)) % 24]
                keys[r, o[7], H + i] = (((a + p) & 63) << 8) + (((b + t) & 63) << 2) + (rng.integers(0, 4, len(i)) << 14)
    d = marked(rng, keys, size, 2.0 ** -30, fine)
    x = d["x"].reshape(N, 8, 16, C, 4)
    i = np.flatnonzero(sign)
    for r in range(N):
        v = rng.choice([-1.0, 1.0], (8, 1, 4)) * 2.0 ** 28
        x[r, first[r][6], 8:][:, spot[r][i]] = (v * sign[i][:, None]).astype(np.float32).astype(BF)
    return {"x": x.reshape(N, 128, 4 * C), "u": d["u"], "v": d["v"], "wc": d["wc"], "ws": d["ws"], **factors(rng.permutation([1, 64, 65]))}
def setup_inputs_huge(rng):
    d = numbers_of(rng)
    x = rng.choice([-1.0, 1.0], (N, 128, C, 4)) * (0.6 + 0.2 * rng.random((N, 128, C, 4))) * 2.0 ** 24
    u = rng.choice([-1.0, 1.0], (128, 128, 4)) * (0.75 + 0.25 * rng.random((128, 128, 4))) * 2.0 ** 30
    for r in range(N):
        for lo in (0, H):
            e = lo + rng.permutation(H)
            for i in range(16): x[r][:, e[2 * i:2 * i + 2]] = (u[:, rng.integers(128)] * (0.5 if i % 2 else -0.5))[:, None]
    w = np.zeros((N, 128, 4, 128, 4), np.float32)
    i = np.arange(128)
    for b in range(4): w[:, i, b, i, b] = 1
    c, p = packed(w.reshape(N, 128, 2048).astype(BF), rng)
    return {"x": x.astype(np.float32).reshape(N, 128, 4 * C).astype(BF), "u": same(u.astype(np.float32).reshape(128, 512).astype(BF)), "v": d["v"], "wc": c, "ws": p, **factors(odd(rng))}
def setup_inputs_copies(rng):
    d = numbers_of(rng)
    x = d["x"].reshape(N, 128, C, 4)
    s, o = int(rng.integers(N)), rng.permutation(N)
    for r in range(N):
        for h in range(2):
            if r == s and h == 0: continue
            i = H * h + rng.permutation(H)[:[2, 16, H // 2, H][(o[r] + h) % 4]]
            x[r][:, i] = x[r][:, i[:1]]
    x[(s + 1) % N, :, H:] = x[s, :, :H]
    x[(s + 2) % N, :, :H] = 0
    x[(s + 3) % N, :, H:] = 0
    return {"x": x.reshape(N, 128, 4 * C), "u": d["u"], "v": d["v"], **weights(rng), **factors(odd(rng))}
def setup_inputs_spread(rng):
    d = setup_inputs(rng)
    d["x"] = big(wide(rng, N, 128, 4 * C, cols=6))
    d["hc"] = factors(rng.integers(1, 256, 3))["hc"]
    return d
def check_inputs(d):
    b = []
    for k in ("x", "u", "v"):
        a = np.abs(d[k].astype(np.float32))
        if not (np.isfinite(a).all() and ((a == 0) | (a >= 2.0 ** -30) & (a <= 2.0 ** 30)).all()): b.append("a value of " + k)
    if (d["u"] != d["u"][:1]).any(): b.append("u: not the same on all ranks")
    if (d["hc"] != d["hc"][:1, :1]).any(): b.append("hc: not the same in all rows and on all ranks")
    if ((d["hc"] < 1) | (d["hc"] > 255)).any(): b.append("hc: out of range")
    none, least, most = [emit(mx_ref.quantize(np.full((128, 16), k, np.float32).astype(BF)))[1][0, 0] for k in (0.0, 2.0 ** -30, 2.0 ** 30)]
    for r in range(N):
        if ((d["wc"][r] == 0x7F) | (d["wc"][r] == 0xFF)).any(): b.append("wc: a code that is no number")
        s = mx_ref.live(d["ws"][r])
        if ((s != none) & ((s < least) | (s > most))).any(): b.append("ws: a scale out of range")
        c = d["wc"][r].reshape(128, -1, 4)
        if ((c != 0) & (c != 0x80) & np.repeat(s == none, 8, axis=0)[:, :, None]).any(): b.append("wc: a number under the scale of zeros")
    return b
def reference(x, u, v, wc, ws, hc):
    qu = [mx_ref.quantize(u[r]) for r in range(N)]
    lay = [pk(wc[r], ws[r]) for r in range(N)]
    now = [x[r] for r in range(N)]
    for t in range(R):
        w = H * (t % 2)
        o = H - w
        num, adr, came = [], [], []
        for r in range(N):
            q = mx_ref.quantize(now[r])
            d = decode(q).astype(BF)
            a = addresses(mx_ref.matmul(qu[r], q), hc[r][0])
            z = written(np.ascontiguousarray(d[:, 4 * w:4 * w + 4 * H]), a[:, :, w:w + H])
            came.append(decode(mx_ref.quantize(z)).astype(BF))
            num.append(d)
            adr.append(a)
        for r in range(N):
            e = [gcols(came[(r - 1) % N], adr[r][:, k, o:o + H]).astype(np.float32) for k in range(3)]
            q = mx_ref.quantize(((e[0] + e[1]) + e[2]).astype(BF))
            new = now[r].copy()
            new[:, 4 * o:4 * o + 4 * H] = tile([mx_ref.matmul(pick(lay[r], np.arange(128 * b, 128 * b + 128)), q) * np.float32(0.015625) + num[r][:, 4 * o + b:4 * o + 4 * H:4].astype(np.float32) for b in range(4)])
            now[r] = new
    y = np.zeros((N, 128, C), np.float32)
    oc, osc = np.zeros((N, 128, 4 * C), np.uint8), np.zeros((N, 16, C), np.uint8)
    for r in range(N):
        q = mx_ref.quantize(now[r])
        y[r] = mx_ref.matmul(mx_ref.quantize(v[r]), q)
        oc[r], osc[r] = emit(q)
    return {"y": y, "oc": oc, "osc": osc}

@@ -1,0 +1,417 @@
+from concourse.bass import DstId, RemoteDMATransfer
+from concourse.mybir import dt, AluOpType as A, ActivationFunctionType as AF
+
+H, R = 160, 3
+BIG, M = float(2 ** 20), float(2 ** 17)
+F32, BF, I32, U16, QC, U8 = "float32", "bfloat16", "int32", "uint16", "float8_e4m3fn_x4", "uint8"
+
+SCRATCH = {"ps": ("psum", [128, 4096], F32)}
+for _d, _l in (
+    (BF, "xt 1280 ut 512 vt 512 rowg 128 ck 512 cv 512 ez 520 wtab 64 rs 480 sg 512 wm 480 fl 640 rem 160 "
+         "tw 644 tx 640 v1 644 v2 640 et 644 e0 640 ft 640 xn 640"),
+    (F32, "hcf 4 pc 8 jrow 17 pw0 16 pw1 16 zr 16 pa1 16 pa2 16 pat4 16 pb1 16 pb2 16 pat16 16 d4 480 d16 160 ph 12 cl 30 "
+          "k64 30 dump 10 idrow 160 ks 40 hb 40 dd 30 sc 480 s1 40 tab 40 vs 160 mm 30 tt 30 sel 30 w2 10 pab 320 pabs 320 "
+          "tmp 640 yb 320 cg 480 cs 480 ot0 352 ot1 352 ot2 352 oz0 128 oz1 128 oz2 128 lo0 64 lo1 64 lo2 64"),
+    (I32, "hci 4 pi 1 pci 4 yk 30 hd 60 xi 12 ex 48 oi 64 otr 192"),
+    (U16, "opt 30 opm 10 trip 30 hu0 60 hu1 60 hu2 60 hu3 60 selu 30 pabu 80 cu 120"),
+    (QC, "qx 320 qu 128 qv 128 qw 512 qck 128 qcv 128 qe 512 qs 128 qf 160 qg 160 qz0 160 qz1 160 qz2 160 lq0 160 lq1 160 lq2 160"),
+    (U8, "sx 320 su 128 sv 128 sw 512 sck 128 scv 128 se 512 ss 128 sf 160 sq 160 sz0 160 sz1 160 sz2 160 ls0 160 ls1 160 ls2 160"),
+):
+    _w = _l.split()
+    for _i in range(0, len(_w), 2):
+        SCRATCH[_w[_i]] = ("sbuf", [128, int(_w[_i + 1])], _d)
+
+POOL = {"V": 14, "A": 10, "P": 16, "G": 24}
+NDMA = 16
+SEMAPHORES = ([q + "%d" % i for q in POOL for i in range(POOL[q])] + ["D%d" % i for i in range(NDMA)]
+              + ["ro%d" % t for t in range(R)] + ["rq%d" % t for t in range(R)] + ["sent"])
+
+
+def rank_program(g, core, T, topo):
+    rank = T.rank_of(core)
+    if rank is None:
+        return
+    n = len(T.cores)
+    nxt, prv = T.cores[(rank + 1) % n], T.cores[(rank - 1) % n]
+    rid, pid = topo.addr(nxt)[0], topo.addr(nxt)[1]
+    mask, nout, nin = topo.mask(core, nxt), len(topo.engines(core, nxt)), len(topo.engines(prv, core))
+
+    Q = {"V": g.vector, "A": g.scalar, "P": g.tensor, "G": g, "S": g.sync}
+    known = {q: set() for q in Q}
+    lastw, readers, last, count = {}, {}, {}, {}
+    nid, ndma, sent = [0], [0], [0]
+
+    def wait(q, grp):
+        if grp["id"] in known[q]:
+            return
+        Q[q].wait_ge(T.sem[grp["sem"]], grp["val"])
+        grp["closed"] = True
+        known[q] |= grp["known"]
+        known[q].add(grp["id"])
+
+    def need(q, r, w, join=None, acc=False):
+        deps = []
+        for k in r:
+            if k in lastw:
+                deps.append(lastw[k])
+            if k[0] == "B":
+                deps += [x for x in readers.get(k, []) if x["q"] != q]
+        for k in w:
+            if k in lastw and not (acc and lastw[k]["q"] == q):
+                deps.append(lastw[k])
+            deps += readers.get(k, [])
+        for d in sorted(deps, key=lambda x: -x["id"]):
+            if d is not join:
+                wait(q, d)
+
+    def op(q, fn, r=(), w=(), join=None, dma=False, acc=False):
+        need(q, r, w, join, acc)
+        if join is not None and not join["closed"]:
+            grp = join
+        else:
+            if dma:
+                sem = "D%d" % ndma[0]
+                ndma[0] += 1
+            else:
+                names = [q + "%d" % i for i in range(POOL[q])]
+                free = [s for s in names if s not in last or last[s]["id"] in known[q]]
+                if not free:
+                    old = min(names, key=lambda s: last[s]["id"])
+                    wait(q, last[old])
+                    free = [old]
+                sem = free[0]
+                if sem in last:
+                    last[sem]["closed"] = True
+            nid[0] += 1
+            grp = {"id": nid[0], "sem": sem, "val": count.get(sem, 0), "known": set(), "closed": False, "q": q}
+            last[sem] = grp
+        inc = 16 if dma else 1
+        fn().then_inc(T.sem[grp["sem"]], inc)
+        grp["val"] += inc
+        count[grp["sem"]] = grp["val"]
+        grp["known"] |= known[q]
+        for k in r:
+            readers.setdefault(k, []).append(grp)
+        for k in w:
+            lastw[k] = grp
+            readers[k] = []
+        return grp
+
+    def arrival(sem, val, keys):
+        nid[0] += 1
+        grp = {"id": nid[0], "sem": sem, "val": val, "known": set(), "closed": True, "q": "X"}
+        last[sem] = grp
+        for k in keys:
+            lastw[k] = grp
+
+    V, S = g.vector, g.scalar
+
+    def bank(b, w=H):
+        return T.ps[:, 512 * b:512 * b + w]
+
+    def ts(out, in0, s1, s2, o0, o1, r, w, join=None):
+        if o1 is None:
+            return op("V", lambda: V.tensor_scalar(out, in0, s1, None, o0), r, w, join)
+        return op("V", lambda: V.tensor_scalar(out, in0, s1, s2, o0, o1), r, w, join)
+
+    def tt(out, a, b, o, r, w, join=None):
+        return op("V", lambda: V.tensor_tensor(out, a, b, o), r, w, join)
+
+    def cp(out, a, r, w, join=None):
+        return op("V", lambda: V.tensor_copy(out, a), r, w, join)
+
+    def ms(out, c, w, join=None):
+        return op("V", lambda: V.memset(out, c), (), w, join)
+
+    def scan(out, d0, d1, init, o0, o1, r, w):
+        return op("V", lambda: V.tensor_tensor_scan(out, d0, d1, init, o0, o1), r, w)
+
+    def qz(c, s, t, r, w, join=None):
+        return op("V", lambda: V.quantize_mx(c, s, t), r, w, join)
+
+    def act(out, a, r, w, scale=1.0, join=None):
+        return op("A", lambda: S.activation(out, a, AF.Copy, scale=scale), r, w, join)
+
+    def mx(b, lc, ls, rc, rs, r, start=True, stop=True, w=H):
+        return op("P", lambda: g.tensor.matmul_mx(bank(b, w), lc, ls, rc, rs, start, stop), r, ["B%d" % b], acc=not start)
+
+    def dma(q, out, a, r, w, join=None):
+        return op(q, lambda: Q[q].dma_start(out, a), r, w, join, dma=True)
+
+    def iota(out, pat, base, cm, w, flt=True, join=None):
+        if flt:
+            return op("G", lambda: g.iota(out, pat, base, cm, allow_small_or_imprecise_dtypes=True), (), w, join)
+        return op("G", lambda: g.iota(out, pat, base, cm), (), w, join)
+
+    def half(h):
+        return T.qx[:, H * h:H * h + H], T.sx[:, H * h:H * h + H]
+
+    def eb(b):
+        return T.qe[:, 128 * b:128 * b + 128], T.se[:, 128 * b:128 * b + 128]
+
+    PM, PG, PT, PA, C4, K4, C16 = [T.pc[:, j:j + 1] for j in range(7)]
+
+    dma("S", T.xt[:, 0:640], T.x[:, 0:640], (), ["xt0"])
+    dma("A", T.ut[:], T.u[:], (), ["ut"])
+    dma("S", T.hci[:, 0:3], T.hc[:], (), ["hci"])
+    dma("S", T.xt[:, 640:1280], T.x[:, 640:1280], (), ["xt1"])
+    j = dma("S", T.qw[:].bitcast(dt.uint8), T.wc[:], (), ["qw"])
+    dma("S", T.sw[:], T.ws[:], (), ["sw"], join=j)
+    dma("S", T.vt[:], T.v[:], (), ["vt"])
+
+    iota(T.pi[:], [[0, 1]], 0, 1, ["pi"], flt=False)
+    iota(T.jrow[:], [[1, 17]], -1, 0, ["jrow"])
+    iota(T.rowg[:], [[1, 8], [0, 16]], 0, 0, ["rowg"])
+    iota(T.sg[:, H:512], [[0, 512 - H]], 0, 0, ["sgz"])
+    j = iota(T.rs[:], [[0, 480]], 1, 0, ["rs"])
+    iota(T.ph[:], [[0, 12]], 0, 0, ["ph"], join=j)
+    iota(T.fl[:, 3:640:4], [[0, H]], 0, 0, ["flz"], join=j)
+    j = iota(T.rs[:, 0:480:40], [[0, 12]], 0, 0, ["rs"])
+    iota(T.ph[:, 0:12:4], [[0, 3]], 2 + 2 ** 7 + 2 ** 13 + 2 ** 19, 0, ["ph"], join=j)
+    j = iota(T.cl[:], [[0, 3], [16, 10]], 0, 0, ["cl"])
+    iota(T.k64[:], [[64, 3], [0, 10]], 0, 0, ["k64"], join=j)
+    iota(T.ez[:], [[0, 520]], 64, 0, ["ez"])
+    op("G", lambda: g.affine_select(T.ez[:], T.ez[:], [[-1, 520]], A.is_equal, 0.0, 3, 4), ["ez"], ["ez"])
+    j = iota(T.idrow[:], [[1, H]], 0, 0, ["idrow"])
+    for b in ("tw", "v1", "et"):
+        iota(T[b][:, 640:644], [[0, 4]], 0, 0, [b + "z"], join=j)
+    for t in range(R):
+        iota(T["ot%d" % t][:, 0:192], [[0, 192]], H, 0, ["ot%d" % t], join=j)
+
+    j = ms(T.ck[:], 0.0, ["ck"])
+    ms(T.zr[:], 0.0, ["zr"], j)
+    j = ts(T.pci[:, 0:1], T.pi[:], 15, None, A.bitwise_and, None, ["pi"], ["pci0"])
+    ts(T.pci[:, 1:2], T.pi[:], 4, None, A.logical_shift_right, None, ["pi"], ["pci1"], j)
+    ts(T.pci[:, 2:3], T.pi[:], 3, None, A.bitwise_and, None, ["pi"], ["pci2"], j)
+    ts(T.pci[:, 3:4], T.pi[:], 2, 3, A.logical_shift_right, A.bitwise_and, ["pi"], ["pci3"], j)
+    cp(T.pc[:, 0:4], T.pci[:], ["pci0"], ["pc"])
+    j = ts(T.pw0[:], T.jrow[:, 1:17], PM, 1.0, A.is_le, A.add, ["jrow", "pc"], ["pw0"])
+    ts(T.pa1[:], T.jrow[:, 1:17], PA, BIG, A.is_equal, A.mult, ["jrow", "pc"], ["pa1"], j)
+    ts(T.pa2[:], T.jrow[:, 0:16], PA, -M, A.is_equal, A.mult, ["jrow", "pc"], ["pa2"], j)
+    ts(T.opt[:], T.rowg[:, 0:30], 0.0, PT, A.mult, A.add, ["rowg", "pc"], ["opt"], j)
+    ts(C4, PA, 3.0, M, A.is_lt, A.mult, ["pc"], ["c4"], j)
+    j = scan(T.pw1[:], T.pw0[:], T.zr[:], 0.5, A.mult, A.add, ["pw0", "zr"], ["pw1"])
+    tt(T.pat4[:], T.pa1[:], T.pa2[:], A.add, ["pa1", "pa2"], ["pat4"], j)
+    act(T.d4[:], T.pat4[:].indirect(T.opt[:]), ["pat4", "opt"], ["d4"])
+    j = None
+    for t in range(4):
+        j = ts(T.ck[:, 5 * t:512:16], T.rowg[:, t:128:4], PG, T.pw1[:, 15:16], A.is_equal, A.mult,
+               ["rowg", "pc", "pw1", "ck"], ["ck%d" % t], j)
+    for d in range(4):
+        ts(T.wtab[:, 16 * d:16 * d + 16], T.jrow[:, 1:17], PM, float(2 ** (6 * d + 1)), A.is_equal, A.mult,
+           ["jrow", "pc"], ["wtab%d" % d], j)
+    qz(T.qck[:], T.sck[:], T.ck[:], ["ck0"], ["qck"])
+    j = qz(half(0)[0], half(0)[1], T.xt[:, 0:640], ["xt0"], ["qx0"])
+    qz(T.qu[:], T.su[:], T.ut[:], ["ut"], ["qu"], j)
+
+    def more_constants_1():
+        j = cp(T.hcf[:, 0:3], T.hci[:, 0:3], ["hci"], ["hcf"])
+        for t in range(4):
+            ts(T.cv[:, t:512:4], T.rowg[:], PG, float(4 >> t), A.is_equal, A.mult, ["rowg", "pc"], ["cv%d" % t], j)
+
+    def more_constants_2():
+        j = qz(T.qcv[:], T.scv[:], T.cv[:], ["cv0"], ["qcv"])
+        ts(T.pb1[:], T.jrow[:, 1:17], PM, BIG, A.is_equal, A.mult, ["jrow", "pc"], ["pb1"], j)
+        ts(T.pb2[:], T.jrow[:, 0:16], PM, -M, A.is_equal, A.mult, ["jrow", "pc"], ["pb2"], j)
+        ts(T.opm[:], T.rowg[:, 0:10], 0.0, PM, A.mult, A.add, ["rowg", "pc"], ["opm"], j)
+
+    def more_constants_3():
+        j = ts(T.trip[:], T.cl[:], PM, None, A.add, None, ["cl", "pc"], ["trip"])
+        for b in range(4):
+            qz(eb(b)[0], eb(b)[1], T.ez[:, 3 - b:515 - b], ["ez"], ["qe%d" % b], j)
+
+    def more_constants_4():
+        j = ts(T.dump[:], T.cl[:, 0:10], PM, 192.0, A.add, A.add, ["cl", "pc"], ["dump"])
+        ts(K4, C4, 4.0, PT, A.mult, A.add, ["c4", "pc"], ["k4"], j)
+        ts(C16, PM, 15.0, M, A.is_lt, A.mult, ["pc"], ["c16"], j)
+        tt(T.pat16[:], T.pb1[:], T.pb2[:], A.add, ["pb1", "pb2"], ["pat16"], j)
+        act(T.d16[:], T.pat16[:].indirect(T.opm[:]), ["pat16", "opm"], ["d16"])
+
+    TW = ["tw0", "tw1", "tw2", "tw3"]
+    ET = ["et0", "et1", "et2", "et3", "etz"]
+
+    def scores(h, b):
+        mx(b, T.qu[:], T.su[:], half(h)[0], half(h)[1], ["qu", "qx%d" % h])
+
+    def signs(b, kb):
+        ts(T.sg[:, 0:H], bank(b), 0.0, None, A.is_gt, None, ["B%d" % b], ["sg"])
+        qz(T.qs[:], T.ss[:], T.sg[:], ["sg", "sgz"], ["qs"])
+        mx(kb, T.qck[:], T.sck[:], T.qs[:], T.ss[:], ["qck", "qs"], w=128)
+
+    def addresses(kb, hu):
+        scan(T.ks[:], T.d4[:, 0:40], bank(kb, 40), 0.0, A.add, A.min, ["d4", "B%d" % kb], ["ks"])
+        j = None
+        for k in range(3):
+            j = ts(T.yk[:, 10 * k:10 * k + 10], T.ks[:, 3:40:4], C4, T.hcf[:, k:k + 1], A.add, A.mult,
+                   ["ks", "c4", "hcf"], ["yk%d" % k], j)
+        j = ts(T.hd[:, 0:30], T.yk[:], 8, 63, A.logical_shift_right, A.bitwise_and, ["yk0", "yk1", "yk2"], ["hd0"])
+        ts(T.hd[:, 30:60], T.yk[:], 12, 3, A.logical_shift_right, A.bitwise_and, ["yk0", "yk1", "yk2"], ["hd1"], j)
+        cp(T[hu][:], T.hd[:], ["hd0", "hd1"], [hu])
+
+    def decode(h, stop):
+        for b in range(4):
+            mx(4 + b, eb(b)[0], eb(b)[1], half(h)[0], half(h)[1], ["qe%d" % b, "qx%d" % h], stop=stop)
+
+    def writers_numbers():
+        for b in range(4):
+            act(T.tw[:, b:640:4], bank(4 + b), ["B%d" % (4 + b)], ["tw%d" % b], scale=0.015625)
+        act(T.tx[:], T.tw[:, 0:640], TW, ["tx"])
+
+    def choices():
+        j = tt(T.hb[:, 10:40], T.hd[:, 0:30], T.k64[:], A.add, ["hd0", "k64"], ["hb"])
+        cp(T.hb[:, 0:10], T.dump[:], ["dump"], ["hb0"], j)
+        j = tt(T.dd[:, 0:10], T.hb[:, 30:40], T.dump[:], A.subtract, ["hb", "dump"], ["dd0"])
+        tt(T.dd[:, 10:30], T.hb[:, 20:40], T.hb[:, 10:30], A.subtract, ["hb"], ["dd1"], j)
+
+    def peel(p, hu):
+        wk = ["wm0", "wm1"]
+        scan(T.sc[:], T.rs[:], T.wm[:], 0.0, A.mult, A.add, ["rs"] + wk, ["sc"])
+        tt(T.xi[:], T.sc[:, 39:480:40], T.ph[:], A.add, ["sc", "ph"], ["xi"])
+        j = None
+        for d in range(4):
+            j = ts(T.ex[:, d:48:4], T.xi[:], 1, 63 << (6 * d), A.logical_shift_right, A.bitwise_and, ["xi"], ["ex%d" % d], j)
+        tt(T.s1[:], T.ex[:, 0:40], T.ex[:, 8:48], A.add, ["ex0", "ex1", "ex2", "ex3"], ["s1"])
+        tt(T.tab[:, 0:36], T.s1[:, 0:36], T.s1[:, 4:40], A.add, ["s1"], ["tab"])
+        j = None
+        for k in range(3):
+            j = tt(T.fl[:, k:640:4], T.tab[:, 16 * k:16 * k + 4].indirect(T[hu][:, 30 + 10 * k:40 + 10 * k]),
+                   T.wm[:, H * k:H * k + H], A.is_equal, ["tab", hu] + wk, ["fl%d" % k], j)
+        qz(T.qf[:], T.sf[:], T.fl[:], ["fl0", "fl1", "fl2", "flz"], ["qf"])
+        if p < 2:
+            mx(1, T.qcv[:], T.scv[:], T.qf[:], T.sf[:], ["qcv", "qf"])
+        mx(2, T.qcv[:], T.scv[:], T.qf[:], T.sf[:], ["qcv", "qf"], start=p == 0, stop=p == 2)
+
+    def remove():
+        ts(T.rem[:], bank(1), 0.0, None, A.is_equal, None, ["B1"], ["rem"])
+        tt(T.wm[:], T.rem[:].indirect(T.trip[:]), T.wm[:], A.mult, ["rem", "trip", "wm0", "wm1"], ["wm0", "wm1"])
+
+    def store(h, qs):
+        lo = H * h
+        j = dma(qs[0], T.oc[:, 4 * lo:4 * lo + 4 * H], half(h)[0].bitcast(dt.uint8), ["qx%d" % h], ())
+        js = {qs[0]: j}
+        for k in range(4):
+            q = qs[1 + k]
+            js[q] = dma(q, T.osc[4 * k:4 * k + 4, lo:lo + H], T.sx[32 * k:32 * k + 4, lo:lo + H], ["qx%d" % h], (), js.get(q))
+        return js
+
+    for t in range(R):
+        w, o = t % 2, 1 - t % 2
+        hu, hr = "hu%d" % t, "hu%d" % ((t - 1) % 4)
+        ot, oz = T["ot%d" % t], T["oz%d" % t]
+        scores(w, 0)
+        if t == 0:
+            more_constants_1()
+        signs(0, 1)
+        if t == 0:
+            more_constants_2()
+        else:
+            decode(w, True)
+        if t == 2:
+            store(0, "SSSSS")
+            mx(3, T.qv[:], T.sv[:], half(0)[0], half(0)[1], ["qv", "qx0"])
+        addresses(1, hu)
+        cp(T.wm[:, 0:256], T.wtab[:].indirect(T[hu][:, 0:16]), ["wtab0", hu], ["wm0"])
+        act(T.wm[:, 256:480], T.wtab[:].indirect(T[hu][:, 16:30]), ["wtab0", hu], ["wm1"])
+        if t > 0:
+            writers_numbers()
+        if t == 2:
+            act(T.yb[:, 0:H], bank(3), ["B3"], ["yb0"])
+            dma("S", T.y[:, 0:H], T.yb[:, 0:H], ["yb0"], ())
+        peel(0, hu)
+        if t == 0:
+            more_constants_3()
+            decode(0, True)
+            writers_numbers()
+        else:
+            choices()
+        remove()
+        peel(1, hu)
+        if t == 0:
+            more_constants_4()
+            qz(half(1)[0], half(1)[1], T.xt[:, 640:1280], ["xt1"], ["qx1"])
+            scores(1, 3)
+        if t == 1:
+            qz(T.qv[:], T.sv[:], T.vt[:], ["vt"], ["qv"])
+        remove()
+        peel(2, hu)
+        if t == 0:
+            choices()
+        scan(T.vs[:], T.d16[:], bank(2), 0.0, A.add, A.min, ["d16", "B2"], ["vs"])
+        j = None
+        for i, th in enumerate((1.0, 4.0, 2.0)):
+            j = ts(T.mm[:, 10 * i:10 * i + 10], T.vs[:, 15:H:16], C16, th, A.add, A.is_ge, ["vs", "c16"], ["mm%d" % i], j)
+        tt(T.tt[:], T.mm[:], T.dd[:], A.mult, ["mm0", "mm1", "mm2", "dd0", "dd1"], ["tt"])
+        j = tt(T.sel[:], T.tt[:], T.hb[:, 0:30], A.add, ["tt", "hb", "hb0"], ["sel"])
+        tt(T.w2[:], T.tt[:, 10:20], T.tt[:, 20:30], A.add, ["tt"], ["w2"], j)
+        tt(T.sel[:, 0:10], T.sel[:, 0:10], T.w2[:], A.subtract, ["sel", "w2"], ["sel"])
+        cp(T.selu[:], T.sel[:], ["sel"], ["selu"])
+        okey = "ot%d" % t
+        cp(ot[:].indirect(T.selu[:, 0:10]), T.idrow[:], ["selu", "idrow"], [okey])
+        cp(T.pab[:, 0:H], ot[:, 0:192].indirect(T.selu[:, 10:20]), [okey, "selu"], ["pab0"])
+        act(T.pab[:, H:2 * H], ot[:, 0:192].indirect(T.selu[:, 20:30]), [okey, "selu"], ["pab1"])
+        j = act(oz[:, 0:64], ot[:, 64:128], [okey], ["oza%d" % t], scale=256.0)
+        act(oz[:, 64:128], ot[:, 128:192], [okey], ["ozb%d" % t], scale=65536.0, join=j)
+        need("G", [okey, "oza%d" % t, "ozb%d" % t], ())
+        g.remote_dma_fused([RemoteDMATransfer(dst_ids=[DstId(rid=rid, pnc=pid)], dma_engine_mask=mask,
+                                              remote_sem=T.sem["ro%d" % t], srcs=[ot[:, 0:64], oz[:, 0:64], oz[:, 64:128]],
+                                              dsts=[T["lo%d" % t][:]], alu_op=1)], local_sem=T.sem.sent)
+        sent[0] += nout
+        scan(T.pabs[:], T.d4[:, 0:320], T.pab[:], 0.0, A.add, A.min, ["d4", "pab0", "pab1"], ["pabs"])
+        ts(T.pabu[:], T.pabs[:, 3:320:4], 4.0, K4, A.mult, A.add, ["pabs", "k4"], ["pabu"])
+        decode(o, False)
+        oa, ob = T.pabu[:, 0:40], T.pabu[:, 40:80]
+        tt(T.tmp[:], T.tw[:].indirect(oa), T.tx[:], A.subtract, TW + ["twz", "tx", "pabu"], ["tmp0", "tmp1"])
+        tt(T.v1[:, 0:640], T.tw[:].indirect(ob), T.tmp[:], A.add, TW + ["pabu", "tmp0", "tmp1"], ["v1"])
+        tt(T.tmp[:], T.v1[:].indirect(oa), T.tx[:], A.add, ["tx", "pabu", "v1", "v1z"], ["tmp0", "tmp1"])
+        tt(T.v2[:], T.v1[:].indirect(ob), T.tmp[:], A.add, ["pabu", "v1", "v1z", "tmp0", "tmp1"], ["v2"])
+        qz(T["qz%d" % t][:], T["sz%d" % t][:], T.v2[:], ["v2"], ["qz%d" % t])
+        need("G", ["qz%d" % t], ())
+        g.remote_dma(T["lq%d" % t][:].bitcast(dt.uint8), T["qz%d" % t][:].bitcast(dt.uint8), T.sem["rq%d" % t], T.sem.sent, pid, rid, mask)
+        g.remote_dma(T["ls%d" % t][:], T["sz%d" % t][:], T.sem["rq%d" % t], T.sem.sent, pid, rid, mask)
+        sent[0] += 2 * nout
+        if t == 0:
+            signs(3, 3)
+        arrival("ro%d" % t, nin, ["lo%d" % t])
+        cp(T.oi[:], T["lo%d" % t][:], ["lo%d" % t], ["oi"])
+        j = ts(T.otr[:, 0:64], T.oi[:], 255, None, A.bitwise_and, None, ["oi"], ["otr0"])
+        ts(T.otr[:, 64:128], T.oi[:], 8, 255, A.logical_shift_right, A.bitwise_and, ["oi"], ["otr1"], j)
+        ts(T.otr[:, 128:192], T.oi[:], 16, None, A.logical_shift_right, None, ["oi"], ["otr2"], j)
+        if t == 0:
+            addresses(3, hr)
+        j = None
+        for k in range(3):
+            j = cp(T.cg[:, H * k:H * k + H], T.otr[:, 64 * k:64 * k + 64].indirect(T[hr][:, 10 * k:10 * k + 10]),
+                   ["otr0", "otr1", "otr2", hr], ["cg%d" % k], j)
+        scan(T.cs[:], T.d4[:], T.cg[:], 0.0, A.add, A.min, ["d4", "cg0", "cg1", "cg2"], ["cs"])
+        ts(T.cu[:], T.cs[:, 3:480:4], 4.0, K4, A.mult, A.add, ["cs", "k4"], ["cu"])
+        arrival("rq%d" % t, 2 * nin, ["lq%d" % t])
+        for b in (0, 2, 1, 3):
+            mx(b, eb(b)[0], eb(b)[1], T["lq%d" % t][:], T["ls%d" % t][:], ["qe%d" % b, "lq%d" % t])
+        for b in (0, 1):
+            ts(T.et[:, b:640:4], bank(b), 0.015625, None, A.mult, None, ["B%d" % b], ["et%d" % b])
+            act(T.et[:, b + 2:640:4], bank(b + 2), ["B%d" % (b + 2)], ["et%d" % (b + 2)], scale=0.015625)
+        act(T.e0[:, H:640], T.et[:].indirect(T.cu[:, 10:40]), ET + ["cu"], ["e01"])
+        cp(T.e0[:, 0:H], T.et[:].indirect(T.cu[:, 0:10]), ET + ["cu"], ["e00"])
+        for i, (a, b) in enumerate(((0, 10), (10, 40))):
+            tt(T.tmp[:, 16 * a:16 * b], T.et[:].indirect(T.cu[:, 40 + a:40 + b]), T.e0[:, 16 * a:16 * b], A.add,
+               ET + ["cu", "e0%d" % i], ["tmp%d" % i])
+            tt(T.ft[:, 16 * a:16 * b], T.et[:].indirect(T.cu[:, 80 + a:80 + b]), T.tmp[:, 16 * a:16 * b], A.add,
+               ET + ["cu", "tmp%d" % i], ["ft%d" % i])
+        qz(T.qg[:], T.sq[:], T.ft[:], ["ft0", "ft1"], ["qg"])
+        for b in (0, 2, 1, 3):
+            mx(4 + b, T.qw[:, 128 * b:128 * b + 128], T.sw[:, 128 * b:128 * b + 128], T.qg[:], T.sq[:], ["qw", "sw", "qg"], start=False)
+        for b in (0, 1):
+            ts(T.xn[:, b:640:4], bank(4 + b), 0.015625, None, A.mult, None, ["B%d" % (4 + b)], ["xn%d" % b])
+            act(T.xn[:, b + 2:640:4], bank(6 + b), ["B%d" % (6 + b)], ["xn%d" % (b + 2)], scale=0.015625)
+        if t == R - 1:
+            g.wait_ge(T.sem.sent, sent[0])
+            for grp in sorted(last.values(), key=lambda x: -x["id"]):
+                wait("G", grp)
+        qz(half(o)[0], half(o)[1], T.xn[:], ["xn0", "xn1", "xn2", "xn3"], ["qx%d" % o])
+
+    mx(0, T.qv[:], T.sv[:], half(1)[0], half(1)[1], ["qv", "qx1"])
+    js = store(1, "SSAAA")
+    cp(T.yb[:, H:2 * H], bank(0), ["B0"], ["yb1"])
+    dma("S", T.y[:, H:2 * H], T.yb[:, H:2 * H], ["yb1"], (), js["S"])
+    for q in js:
+        wait(q, js[q])

@@ -3,17 +3,18 @@ from concourse.mybir import dt, AluOpType as A, ActivationFunctionType as AF
 
 H, R = 160, 3
 BIG, M = float(2 ** 20), float(2 ** 17)
+U, BIG2, M2 = float(2 ** 20), float(2 ** 26), float(2 ** 24)
 F32, BF, I32, U16, QC, U8 = "float32", "bfloat16", "int32", "uint16", "float8_e4m3fn_x4", "uint8"
 
 SCRATCH = {"ps": ("psum", [128, 4096], F32)}
 for _d, _l in (
-    (BF, "xt 1280 ut 512 vt 512 rowg 128 ck 512 cv 512 ez 520 wtab 64 rs 480 sg 512 wm 480 fl 640 rem 160 "
+    (BF, "xt 1280 ut 512 vt 512 rowg 128 ck 512 cv 512 ez 520 wtab 64 rs 160 sg 512 wm 480 wx 480 fl 640 "
          "tw 644 tx 640 v1 644 v2 640 et 644 e0 640 ft 640 xn 640"),
-    (F32, "hcf 4 pc 8 jrow 17 pw0 16 pw1 16 zr 16 pa1 16 pa2 16 pat4 16 pb1 16 pb2 16 pat16 16 d4 480 d16 160 ph 12 cl 30 "
-          "k64 30 dump 10 idrow 160 ks 40 hb 40 dd 30 sc 480 s1 40 tab 40 vs 160 mm 30 tt 30 sel 30 w2 10 pab 320 pabs 320 "
+    (F32, "hcf 4 pc 8 jrow 17 pw0 16 pw1 16 zr 16 pa1 16 pa2 16 pat4 16 pb1 16 pb2 16 pat16 16 d4 480 d16 160 ph 12 cl 10 "
+          "k64 30 idrow 160 ks 40 hb 40 dd 30 sc 480 s1 40 tab 40 vs 160 mm 30 tt 30 sel 30 w2 10 pab 320 pabs 320 "
           "tmp 640 yb 320 cg 480 cs 480 ot0 352 ot1 352 ot2 352 oz0 128 oz1 128 oz2 128 lo0 64 lo1 64 lo2 64"),
     (I32, "hci 4 pi 1 pci 4 yk 30 hd 60 xi 12 ex 48 oi 64 otr 192"),
-    (U16, "opt 30 opm 10 trip 30 hu0 60 hu1 60 hu2 60 hu3 60 selu 30 pabu 80 cu 120"),
+    (U16, "opt 30 opm 10 hu0 60 hu1 60 hu2 60 hu3 60 selu 30 pabu 80 cu 120"),
     (QC, "qx 320 qu 128 qv 128 qw 512 qck 128 qcv 128 qe 512 qs 128 qf 160 qg 160 qz0 160 qz1 160 qz2 160 lq0 160 lq1 160 lq2 160"),
     (U8, "sx 320 su 128 sv 128 sw 512 sck 128 scv 128 se 512 ss 128 sf 160 sq 160 sz0 160 sz1 160 sz2 160 ls0 160 ls1 160 ls2 160"),
 ):
@@ -21,7 +22,7 @@ for _d, _l in (
     for _i in range(0, len(_w), 2):
         SCRATCH[_w[_i]] = ("sbuf", [128, int(_w[_i + 1])], _d)
 
-POOL = {"V": 14, "A": 10, "P": 16, "G": 24}
+POOL = {"V": 24, "A": 12, "P": 16, "G": 24}
 NDMA = 16
 SEMAPHORES = ([q + "%d" % i for q in POOL for i in range(POOL[q])] + ["D%d" % i for i in range(NDMA)]
               + ["ro%d" % t for t in range(R)] + ["rq%d" % t for t in range(R)] + ["sent"])
@@ -123,14 +124,14 @@ def rank_program(g, core, T, topo):
     def ms(out, c, w, join=None):
         return op("V", lambda: V.memset(out, c), (), w, join)
 
-    def scan(out, d0, d1, init, o0, o1, r, w):
-        return op("V", lambda: V.tensor_tensor_scan(out, d0, d1, init, o0, o1), r, w)
+    def scan(out, d0, d1, init, o0, o1, r, w, join=None):
+        return op("V", lambda: V.tensor_tensor_scan(out, d0, d1, init, o0, o1), r, w, join)
 
     def qz(c, s, t, r, w, join=None):
         return op("V", lambda: V.quantize_mx(c, s, t), r, w, join)
 
-    def act(out, a, r, w, scale=1.0, join=None):
-        return op("A", lambda: S.activation(out, a, AF.Copy, scale=scale), r, w, join)
+    def act(out, a, r, w, scale=1.0, join=None, f=AF.Copy):
+        return op("A", lambda: S.activation(out, a, f, scale=scale), r, w, join)
 
     def mx(b, lc, ls, rc, rs, r, start=True, stop=True, w=H):
         return op("P", lambda: g.tensor.matmul_mx(bank(b, w), lc, ls, rc, rs, start, stop), r, ["B%d" % b], acc=not start)
@@ -149,6 +150,9 @@ def rank_program(g, core, T, topo):
     def eb(b):
         return T.qe[:, 128 * b:128 * b + 128], T.se[:, 128 * b:128 * b + 128]
 
+    def third(buf, k):
+        return buf[:, H * k:H * k + H]
+
     PM, PG, PT, PA, C4, K4, C16 = [T.pc[:, j:j + 1] for j in range(7)]
 
     dma("S", T.xt[:, 0:640], T.x[:, 0:640], (), ["xt0"])
@@ -163,15 +167,15 @@ def rank_program(g, core, T, topo):
     iota(T.jrow[:], [[1, 17]], -1, 0, ["jrow"])
     iota(T.rowg[:], [[1, 8], [0, 16]], 0, 0, ["rowg"])
     iota(T.sg[:, H:512], [[0, 512 - H]], 0, 0, ["sgz"])
-    j = iota(T.rs[:], [[0, 480]], 1, 0, ["rs"])
+    j = iota(T.rs[:], [[0, H]], 1, 0, ["rs"])
     iota(T.ph[:], [[0, 12]], 0, 0, ["ph"], join=j)
     iota(T.fl[:, 3:640:4], [[0, H]], 0, 0, ["flz"], join=j)
-    j = iota(T.rs[:, 0:480:40], [[0, 12]], 0, 0, ["rs"])
+    j = iota(T.rs[:, 0:H:40], [[0, 4]], 0, 0, ["rs"])
     iota(T.ph[:, 0:12:4], [[0, 3]], 2 + 2 ** 7 + 2 ** 13 + 2 ** 19, 0, ["ph"], join=j)
-    j = iota(T.cl[:], [[0, 3], [16, 10]], 0, 0, ["cl"])
-    iota(T.k64[:], [[64, 3], [0, 10]], 0, 0, ["k64"], join=j)
     iota(T.ez[:], [[0, 520]], 64, 0, ["ez"])
     op("G", lambda: g.affine_select(T.ez[:], T.ez[:], [[-1, 520]], A.is_equal, 0.0, 3, 4), ["ez"], ["ez"])
+    j = iota(T.cl[:], [[16, 10]], 192, 0, ["cl"])
+    iota(T.k64[:], [[64, 3], [0, 10]], 0, 0, ["k64"], join=j)
     j = iota(T.idrow[:], [[1, H]], 0, 0, ["idrow"])
     for b in ("tw", "v1", "et"):
         iota(T[b][:, 640:644], [[0, 4]], 0, 0, [b + "z"], join=j)
@@ -186,49 +190,50 @@ def rank_program(g, core, T, topo):
     ts(T.pci[:, 3:4], T.pi[:], 2, 3, A.logical_shift_right, A.bitwise_and, ["pi"], ["pci3"], j)
     cp(T.pc[:, 0:4], T.pci[:], ["pci0"], ["pc"])
     j = ts(T.pw0[:], T.jrow[:, 1:17], PM, 1.0, A.is_le, A.add, ["jrow", "pc"], ["pw0"])
-    ts(T.pa1[:], T.jrow[:, 1:17], PA, BIG, A.is_equal, A.mult, ["jrow", "pc"], ["pa1"], j)
-    ts(T.pa2[:], T.jrow[:, 0:16], PA, -M, A.is_equal, A.mult, ["jrow", "pc"], ["pa2"], j)
-    ts(T.opt[:], T.rowg[:, 0:30], 0.0, PT, A.mult, A.add, ["rowg", "pc"], ["opt"], j)
-    ts(C4, PA, 3.0, M, A.is_lt, A.mult, ["pc"], ["c4"], j)
-    j = scan(T.pw1[:], T.pw0[:], T.zr[:], 0.5, A.mult, A.add, ["pw0", "zr"], ["pw1"])
-    tt(T.pat4[:], T.pa1[:], T.pa2[:], A.add, ["pa1", "pa2"], ["pat4"], j)
-    act(T.d4[:], T.pat4[:].indirect(T.opt[:]), ["pat4", "opt"], ["d4"])
+    j2 = ts(T.pa1[:], T.jrow[:, 1:17], PA, BIG, A.is_equal, A.mult, ["jrow", "pc"], ["pa1"])
+    ts(T.pa2[:], T.jrow[:, 0:16], PA, -M, A.is_equal, A.mult, ["jrow", "pc"], ["pa2"], j2)
+    ts(T.opt[:], T.rowg[:, 0:30], 0.0, PT, A.mult, A.add, ["rowg", "pc"], ["opt"], j2)
+    scan(T.pw1[:], T.pw0[:], T.zr[:], 0.5, A.mult, A.add, ["pw0", "zr"], ["pw1"])
+    j = ts(C4, PA, 3.0, M, A.is_lt, A.mult, ["pc"], ["c4"])
+    for d in range(4):
+        ts(T.wtab[:, 16 * d:16 * d + 16], T.jrow[:, 1:17], PM, float(2 ** (6 * d + 1)), A.is_equal, A.mult,
+           ["jrow", "pc"], ["wtab%d" % d], j)
     j = None
     for t in range(4):
         j = ts(T.ck[:, 5 * t:512:16], T.rowg[:, t:128:4], PG, T.pw1[:, 15:16], A.is_equal, A.mult,
                ["rowg", "pc", "pw1", "ck"], ["ck%d" % t], j)
-    for d in range(4):
-        ts(T.wtab[:, 16 * d:16 * d + 16], T.jrow[:, 1:17], PM, float(2 ** (6 * d + 1)), A.is_equal, A.mult,
-           ["jrow", "pc"], ["wtab%d" % d], j)
-    qz(T.qck[:], T.sck[:], T.ck[:], ["ck0"], ["qck"])
+    tt(T.pat4[:], T.pa1[:], T.pa2[:], A.add, ["pa1", "pa2"], ["pat4"])
+    act(T.d4[:], T.pat4[:].indirect(T.opt[:]), ["pat4", "opt"], ["d4"])
     j = qz(half(0)[0], half(0)[1], T.xt[:, 0:640], ["xt0"], ["qx0"])
     qz(T.qu[:], T.su[:], T.ut[:], ["ut"], ["qu"], j)
 
     def more_constants_1():
-        j = cp(T.hcf[:, 0:3], T.hci[:, 0:3], ["hci"], ["hcf"])
-        for t in range(4):
-            ts(T.cv[:, t:512:4], T.rowg[:], PG, float(4 >> t), A.is_equal, A.mult, ["rowg", "pc"], ["cv%d" % t], j)
+        j = qz(T.qck[:], T.sck[:], T.ck[:], ["ck0"], ["qck"])
+        cp(T.hcf[:, 0:3], T.hci[:, 0:3], ["hci"], ["hcf"], j)
 
     def more_constants_2():
-        j = qz(T.qcv[:], T.scv[:], T.cv[:], ["cv0"], ["qcv"])
-        ts(T.pb1[:], T.jrow[:, 1:17], PM, BIG, A.is_equal, A.mult, ["jrow", "pc"], ["pb1"], j)
-        ts(T.pb2[:], T.jrow[:, 0:16], PM, -M, A.is_equal, A.mult, ["jrow", "pc"], ["pb2"], j)
-        ts(T.opm[:], T.rowg[:, 0:10], 0.0, PM, A.mult, A.add, ["rowg", "pc"], ["opm"], j)
+        j = None
+        for t in range(4):
+            j = ts(T.cv[:, t:512:4], T.rowg[:], PG, (4 >> t) * U, A.is_equal, A.mult, ["rowg", "pc"], ["cv%d" % t], j)
 
     def more_constants_3():
-        j = ts(T.trip[:], T.cl[:], PM, None, A.add, None, ["cl", "pc"], ["trip"])
+        j = None
         for b in range(4):
-            qz(eb(b)[0], eb(b)[1], T.ez[:, 3 - b:515 - b], ["ez"], ["qe%d" % b], j)
+            j = qz(eb(b)[0], eb(b)[1], T.ez[:, 3 - b:515 - b], ["ez"], ["qe%d" % b], j)
 
     def more_constants_4():
-        j = ts(T.dump[:], T.cl[:, 0:10], PM, 192.0, A.add, A.add, ["cl", "pc"], ["dump"])
+        j = ts(T.pb1[:], T.jrow[:, 1:17], PM, BIG2, A.is_equal, A.mult, ["jrow", "pc"], ["pb1"])
+        ts(T.pb2[:], T.jrow[:, 0:16], PM, -M2, A.is_equal, A.mult, ["jrow", "pc"], ["pb2"], j)
+        j = ts(T.opm[:], T.rowg[:, 0:10], 0.0, PM, A.mult, A.add, ["rowg", "pc"], ["opm"])
+        ts(T.hb[:, 0:10], T.cl[:], PM, None, A.add, None, ["cl", "pc"], ["hb0"], j)
         ts(K4, C4, 4.0, PT, A.mult, A.add, ["c4", "pc"], ["k4"], j)
-        ts(C16, PM, 15.0, M, A.is_lt, A.mult, ["pc"], ["c16"], j)
-        tt(T.pat16[:], T.pb1[:], T.pb2[:], A.add, ["pb1", "pb2"], ["pat16"], j)
+        ts(C16, PM, 15.0, M2, A.is_lt, A.mult, ["pc"], ["c16"], j)
+        tt(T.pat16[:], T.pb1[:], T.pb2[:], A.add, ["pb1", "pb2"], ["pat16"])
         act(T.d16[:], T.pat16[:].indirect(T.opm[:]), ["pat16", "opm"], ["d16"])
 
     TW = ["tw0", "tw1", "tw2", "tw3"]
     ET = ["et0", "et1", "et2", "et3", "etz"]
+    YK = ["yk0", "yk1", "yk2"]
 
     def scores(h, b):
         mx(b, T.qu[:], T.su[:], half(h)[0], half(h)[1], ["qu", "qx%d" % h])
@@ -238,15 +243,18 @@ def rank_program(g, core, T, topo):
         qz(T.qs[:], T.ss[:], T.sg[:], ["sg", "sgz"], ["qs"])
         mx(kb, T.qck[:], T.sck[:], T.qs[:], T.ss[:], ["qck", "qs"], w=128)
 
-    def addresses(kb, hu):
+    def addresses(kb, hu, digits):
         scan(T.ks[:], T.d4[:, 0:40], bank(kb, 40), 0.0, A.add, A.min, ["d4", "B%d" % kb], ["ks"])
         j = None
         for k in range(3):
             j = ts(T.yk[:, 10 * k:10 * k + 10], T.ks[:, 3:40:4], C4, T.hcf[:, k:k + 1], A.add, A.mult,
                    ["ks", "c4", "hcf"], ["yk%d" % k], j)
-        j = ts(T.hd[:, 0:30], T.yk[:], 8, 63, A.logical_shift_right, A.bitwise_and, ["yk0", "yk1", "yk2"], ["hd0"])
-        ts(T.hd[:, 30:60], T.yk[:], 12, 3, A.logical_shift_right, A.bitwise_and, ["yk0", "yk1", "yk2"], ["hd1"], j)
-        cp(T[hu][:], T.hd[:], ["hd0", "hd1"], [hu])
+        ts(T.hd[:, 0:30], T.yk[:], 8, 63, A.logical_shift_right, A.bitwise_and, YK, ["hd0"])
+        if digits:
+            ts(T.hd[:, 30:60], T.yk[:], 12, 3, A.logical_shift_right, A.bitwise_and, YK, ["hd1"])
+        cp(T[hu][:, 0:30], T.hd[:, 0:30], ["hd0"], [hu])
+        if digits:
+            cp(T[hu][:, 30:60], T.hd[:, 30:60], ["hd1"], [hu + "d"])
 
     def decode(h, stop):
         for b in range(4):
@@ -257,16 +265,18 @@ def rank_program(g, core, T, topo):
             act(T.tw[:, b:640:4], bank(4 + b), ["B%d" % (4 + b)], ["tw%d" % b], scale=0.015625)
         act(T.tx[:], T.tw[:, 0:640], TW, ["tx"])
 
+    def cells():
+        tt(T.hb[:, 10:40], T.hd[:, 0:30], T.k64[:], A.add, ["hd0", "k64"], ["hb"])
+
     def choices():
-        j = tt(T.hb[:, 10:40], T.hd[:, 0:30], T.k64[:], A.add, ["hd0", "k64"], ["hb"])
-        cp(T.hb[:, 0:10], T.dump[:], ["dump"], ["hb0"], j)
-        j = tt(T.dd[:, 0:10], T.hb[:, 30:40], T.dump[:], A.subtract, ["hb", "dump"], ["dd0"])
+        j = tt(T.dd[:, 0:10], T.hb[:, 30:40], T.hb[:, 0:10], A.subtract, ["hb", "hb0"], ["dd0"])
         tt(T.dd[:, 10:30], T.hb[:, 20:40], T.hb[:, 10:30], A.subtract, ["hb"], ["dd1"], j)
 
-    def peel(p, hu):
-        wk = ["wm0", "wm1"]
-        scan(T.sc[:], T.rs[:], T.wm[:], 0.0, A.mult, A.add, ["rs"] + wk, ["sc"])
-        tt(T.xi[:], T.sc[:, 39:480:40], T.ph[:], A.add, ["sc", "ph"], ["xi"])
+    def peel(p, hu, order):
+        j = None
+        for k in order:
+            j = scan(third(T.sc, k), T.rs[:], third(T.wm, k), 0.0, A.mult, A.add, ["rs", "wm%d" % k], ["sc%d" % k], j)
+        tt(T.xi[:], T.sc[:, 39:480:40], T.ph[:], A.add, ["sc0", "sc1", "sc2", "ph"], ["xi"])
         j = None
         for d in range(4):
             j = ts(T.ex[:, d:48:4], T.xi[:], 1, 63 << (6 * d), A.logical_shift_right, A.bitwise_and, ["xi"], ["ex%d" % d], j)
@@ -275,15 +285,20 @@ def rank_program(g, core, T, topo):
         j = None
         for k in range(3):
             j = tt(T.fl[:, k:640:4], T.tab[:, 16 * k:16 * k + 4].indirect(T[hu][:, 30 + 10 * k:40 + 10 * k]),
-                   T.wm[:, H * k:H * k + H], A.is_equal, ["tab", hu] + wk, ["fl%d" % k], j)
+                   third(T.wm, k), A.is_equal, ["tab", hu + "d", "wm%d" % k], ["fl%d" % k], j)
+        if p == 0 and hu == "hu0":
+            qz(T.qcv[:], T.scv[:], T.cv[:], ["cv0"], ["qcv"])
         qz(T.qf[:], T.sf[:], T.fl[:], ["fl0", "fl1", "fl2", "flz"], ["qf"])
         if p < 2:
             mx(1, T.qcv[:], T.scv[:], T.qf[:], T.sf[:], ["qcv", "qf"])
         mx(2, T.qcv[:], T.scv[:], T.qf[:], T.sf[:], ["qcv", "qf"], start=p == 0, stop=p == 2)
 
     def remove():
-        ts(T.rem[:], bank(1), 0.0, None, A.is_equal, None, ["B1"], ["rem"])
-        tt(T.wm[:], T.rem[:].indirect(T.trip[:]), T.wm[:], A.mult, ["rem", "trip", "wm0", "wm1"], ["wm0", "wm1"])
+        for k in range(3):
+            tt(third(T.wx, k), third(T.wm, k), bank(1), A.subtract, ["wm%d" % k, "B1"], ["wx%d" % k])
+        act(third(T.wm, 0), third(T.wx, 0), ["wx0"], ["wm0"], f=AF.Relu)
+        for k in (1, 2):
+            ts(third(T.wm, k), third(T.wx, k), 0.0, None, A.max, None, ["wx%d" % k], ["wm%d" % k])
 
     def store(h, qs):
         lo = H * h
@@ -309,46 +324,50 @@ def rank_program(g, core, T, topo):
         if t == 2:
             store(0, "SSSSS")
             mx(3, T.qv[:], T.sv[:], half(0)[0], half(0)[1], ["qv", "qx0"])
-        addresses(1, hu)
-        cp(T.wm[:, 0:256], T.wtab[:].indirect(T[hu][:, 0:16]), ["wtab0", hu], ["wm0"])
-        act(T.wm[:, 256:480], T.wtab[:].indirect(T[hu][:, 16:30]), ["wtab0", hu], ["wm1"])
+        addresses(1, hu, True)
+        for k in (1, 2):
+            act(third(T.wm, k), T.wtab[:].indirect(T[hu][:, 10 * k:10 * k + 10]), ["wtab0", hu], ["wm%d" % k])
+        cp(third(T.wm, 0), T.wtab[:].indirect(T[hu][:, 0:10]), ["wtab0", hu], ["wm0"])
+        cells()
         if t > 0:
             writers_numbers()
         if t == 2:
             act(T.yb[:, 0:H], bank(3), ["B3"], ["yb0"])
             dma("S", T.y[:, 0:H], T.yb[:, 0:H], ["yb0"], ())
-        peel(0, hu)
+        peel(0, hu, (0, 1, 2))
         if t == 0:
             more_constants_3()
             decode(0, True)
-            writers_numbers()
         else:
             choices()
         remove()
-        peel(1, hu)
+        if t == 0:
+            writers_numbers()
+        peel(1, hu, (1, 2, 0))
         if t == 0:
             more_constants_4()
-            qz(half(1)[0], half(1)[1], T.xt[:, 640:1280], ["xt1"], ["qx1"])
-            scores(1, 3)
         if t == 1:
             qz(T.qv[:], T.sv[:], T.vt[:], ["vt"], ["qv"])
         remove()
-        peel(2, hu)
+        peel(2, hu, (1, 2, 0))
         if t == 0:
             choices()
+            qz(half(1)[0], half(1)[1], T.xt[:, 640:1280], ["xt1"], ["qx1"])
+            scores(1, 3)
         scan(T.vs[:], T.d16[:], bank(2), 0.0, A.add, A.min, ["d16", "B2"], ["vs"])
         j = None
         for i, th in enumerate((1.0, 4.0, 2.0)):
-            j = ts(T.mm[:, 10 * i:10 * i + 10], T.vs[:, 15:H:16], C16, th, A.add, A.is_ge, ["vs", "c16"], ["mm%d" % i], j)
+            j = ts(T.mm[:, 10 * i:10 * i + 10], T.vs[:, 15:H:16], C16, th * U, A.add, A.is_ge, ["vs", "c16"], ["mm%d" % i], j)
         tt(T.tt[:], T.mm[:], T.dd[:], A.mult, ["mm0", "mm1", "mm2", "dd0", "dd1"], ["tt"])
-        j = tt(T.sel[:], T.tt[:], T.hb[:, 0:30], A.add, ["tt", "hb", "hb0"], ["sel"])
+        j = tt(T.sel[:], T.tt[:], T.hb[:, 0:30], A.add, ["tt", "hb", "hb0"], ["sel", "sel0"])
         tt(T.w2[:], T.tt[:, 10:20], T.tt[:, 20:30], A.add, ["tt"], ["w2"], j)
-        tt(T.sel[:, 0:10], T.sel[:, 0:10], T.w2[:], A.subtract, ["sel", "w2"], ["sel"])
-        cp(T.selu[:], T.sel[:], ["sel"], ["selu"])
+        tt(T.sel[:, 0:10], T.sel[:, 0:10], T.w2[:], A.subtract, ["sel0", "w2"], ["sel0"])
+        cp(T.selu[:, 10:30], T.sel[:, 10:30], ["sel"], ["selu"])
+        cp(T.selu[:, 0:10], T.sel[:, 0:10], ["sel0"], ["selu0"])
         okey = "ot%d" % t
-        cp(ot[:].indirect(T.selu[:, 0:10]), T.idrow[:], ["selu", "idrow"], [okey])
-        cp(T.pab[:, 0:H], ot[:, 0:192].indirect(T.selu[:, 10:20]), [okey, "selu"], ["pab0"])
-        act(T.pab[:, H:2 * H], ot[:, 0:192].indirect(T.selu[:, 20:30]), [okey, "selu"], ["pab1"])
+        cp(ot[:].indirect(T.selu[:, 0:10]), T.idrow[:], ["selu0", "idrow"], [okey])
+        act(third(T.pab, 1), ot[:, 0:192].indirect(T.selu[:, 20:30]), [okey, "selu"], ["pab1"])
+        cp(third(T.pab, 0), ot[:, 0:192].indirect(T.selu[:, 10:20]), [okey, "selu"], ["pab0"])
         j = act(oz[:, 0:64], ot[:, 64:128], [okey], ["oza%d" % t], scale=256.0)
         act(oz[:, 64:128], ot[:, 128:192], [okey], ["ozb%d" % t], scale=65536.0, join=j)
         need("G", [okey, "oza%d" % t, "ozb%d" % t], ())
@@ -356,15 +375,20 @@ def rank_program(g, core, T, topo):
                                               remote_sem=T.sem["ro%d" % t], srcs=[ot[:, 0:64], oz[:, 0:64], oz[:, 64:128]],
                                               dsts=[T["lo%d" % t][:]], alu_op=1)], local_sem=T.sem.sent)
         sent[0] += nout
-        scan(T.pabs[:], T.d4[:, 0:320], T.pab[:], 0.0, A.add, A.min, ["d4", "pab0", "pab1"], ["pabs"])
-        ts(T.pabu[:], T.pabs[:, 3:320:4], 4.0, K4, A.mult, A.add, ["pabs", "k4"], ["pabu"])
+        for i in range(2):
+            scan(third(T.pabs, i), T.d4[:, 0:H], third(T.pab, i), 0.0, A.add, A.min, ["d4", "pab%d" % i], ["pabs%d" % i])
+        for i in range(2):
+            ts(T.pabu[:, 40 * i:40 * i + 40], T.pabs[:, H * i + 3:H * i + H:4], 4.0, K4, A.mult, A.add, ["pabs%d" % i, "k4"], ["pabu%d" % i])
         decode(o, False)
-        oa, ob = T.pabu[:, 0:40], T.pabu[:, 40:80]
-        tt(T.tmp[:], T.tw[:].indirect(oa), T.tx[:], A.subtract, TW + ["twz", "tx", "pabu"], ["tmp0", "tmp1"])
-        tt(T.v1[:, 0:640], T.tw[:].indirect(ob), T.tmp[:], A.add, TW + ["pabu", "tmp0", "tmp1"], ["v1"])
-        tt(T.tmp[:], T.v1[:].indirect(oa), T.tx[:], A.add, ["tx", "pabu", "v1", "v1z"], ["tmp0", "tmp1"])
-        tt(T.v2[:], T.v1[:].indirect(ob), T.tmp[:], A.add, ["pabu", "v1", "v1z", "tmp0", "tmp1"], ["v2"])
-        qz(T["qz%d" % t][:], T["sz%d" % t][:], T.v2[:], ["v2"], ["qz%d" % t])
+        for src, keys, first, dst in ((T.tw, TW + ["twz"], A.subtract, "v1"), (T.v1, ["v10", "v11", "v1z"], A.add, "v2")):
+            for i in range(2):
+                tt(T.tmp[:, 320 * i:320 * i + 320], src[:].indirect(T.pabu[:, 20 * i:20 * i + 20]), T.tx[:, 320 * i:320 * i + 320],
+                   first, keys + ["tx", "pabu0"], ["tmp%d" % i] + ["tmp2"] * i)
+            j = None
+            for i in range(2):
+                j = tt(T[dst][:, 320 * i:320 * i + 320], src[:].indirect(T.pabu[:, 40 + 20 * i:60 + 20 * i]),
+                       T.tmp[:, 320 * i:320 * i + 320], A.add, keys + ["pabu1", "tmp%d" % i], [dst + "%d" % i], j)
+        qz(T["qz%d" % t][:], T["sz%d" % t][:], T.v2[:], ["v20", "v21"], ["qz%d" % t])
         need("G", ["qz%d" % t], ())
         g.remote_dma(T["lq%d" % t][:].bitcast(dt.uint8), T["qz%d" % t][:].bitcast(dt.uint8), T.sem["rq%d" % t], T.sem.sent, pid, rid, mask)
         g.remote_dma(T["ls%d" % t][:], T["sz%d" % t][:], T.sem["rq%d" % t], T.sem.sent, pid, rid, mask)
@@ -377,28 +401,36 @@ def rank_program(g, core, T, topo):
         ts(T.otr[:, 64:128], T.oi[:], 8, 255, A.logical_shift_right, A.bitwise_and, ["oi"], ["otr1"], j)
         ts(T.otr[:, 128:192], T.oi[:], 16, None, A.logical_shift_right, None, ["oi"], ["otr2"], j)
         if t == 0:
-            addresses(3, hr)
+            addresses(3, hr, False)
+        for k in range(3):
+            cp(third(T.cg, k), T.otr[:, 64 * k:64 * k + 64].indirect(T[hr][:, 10 * k:10 * k + 10]),
+               ["otr0", "otr1", "otr2", hr], ["cg%d" % k])
         j = None
         for k in range(3):
-            j = cp(T.cg[:, H * k:H * k + H], T.otr[:, 64 * k:64 * k + 64].indirect(T[hr][:, 10 * k:10 * k + 10]),
-                   ["otr0", "otr1", "otr2", hr], ["cg%d" % k], j)
-        scan(T.cs[:], T.d4[:], T.cg[:], 0.0, A.add, A.min, ["d4", "cg0", "cg1", "cg2"], ["cs"])
-        ts(T.cu[:], T.cs[:, 3:480:4], 4.0, K4, A.mult, A.add, ["cs", "k4"], ["cu"])
+            j = scan(third(T.cs, k), T.d4[:, 0:H], third(T.cg, k), 0.0, A.add, A.min, ["d4", "cg%d" % k], ["cs%d" % k], j)
+        ts(T.cu[:], T.cs[:, 3:480:4], 4.0, K4, A.mult, A.add, ["cs0", "cs1", "cs2", "k4"], ["cu"])
         arrival("rq%d" % t, 2 * nin, ["lq%d" % t])
-        for b in (0, 2, 1, 3):
+        for b in (2, 0, 3, 1):
             mx(b, eb(b)[0], eb(b)[1], T["lq%d" % t][:], T["ls%d" % t][:], ["qe%d" % b, "lq%d" % t])
         for b in (0, 1):
             ts(T.et[:, b:640:4], bank(b), 0.015625, None, A.mult, None, ["B%d" % b], ["et%d" % b])
             act(T.et[:, b + 2:640:4], bank(b + 2), ["B%d" % (b + 2)], ["et%d" % (b + 2)], scale=0.015625)
-        act(T.e0[:, H:640], T.et[:].indirect(T.cu[:, 10:40]), ET + ["cu"], ["e01"])
+        cut = ((0, 10), (10, 24), (24, 40))
+        for i in (1, 2):
+            a, b = cut[i]
+            act(T.e0[:, 16 * a:16 * b], T.et[:].indirect(T.cu[:, a:b]), ET + ["cu"], ["e0%d" % i])
         cp(T.e0[:, 0:H], T.et[:].indirect(T.cu[:, 0:10]), ET + ["cu"], ["e00"])
-        for i, (a, b) in enumerate(((0, 10), (10, 40))):
-            tt(T.tmp[:, 16 * a:16 * b], T.et[:].indirect(T.cu[:, 40 + a:40 + b]), T.e0[:, 16 * a:16 * b], A.add,
-               ET + ["cu", "e0%d" % i], ["tmp%d" % i])
-            tt(T.ft[:, 16 * a:16 * b], T.et[:].indirect(T.cu[:, 80 + a:80 + b]), T.tmp[:, 16 * a:16 * b], A.add,
-               ET + ["cu", "tmp%d" % i], ["ft%d" % i])
-        qz(T.qg[:], T.sq[:], T.ft[:], ["ft0", "ft1"], ["qg"])
-        for b in (0, 2, 1, 3):
+        j = None
+        for step, i in ((1, 0), (1, 1), (2, 0), (1, 2), (2, 1), (2, 2)):
+            a, b = cut[i]
+            if step == 1:
+                tt(T.tmp[:, 16 * a:16 * b], T.et[:].indirect(T.cu[:, 40 + a:40 + b]), T.e0[:, 16 * a:16 * b], A.add,
+                   ET + ["cu", "e0%d" % i], ["tmp%d" % i])
+            else:
+                j = tt(T.ft[:, 16 * a:16 * b], T.et[:].indirect(T.cu[:, 80 + a:80 + b]), T.tmp[:, 16 * a:16 * b], A.add,
+                       ET + ["cu", "tmp%d" % i], ["ft%d" % i], j)
+        qz(T.qg[:], T.sq[:], T.ft[:], ["ft0", "ft1", "ft2"], ["qg"])
+        for b in (2, 0, 3, 1):
             mx(4 + b, T.qw[:, 128 * b:128 * b + 128], T.sw[:, 128 * b:128 * b + 128], T.qg[:], T.sq[:], ["qw", "sw", "qg"], start=False)
         for b in (0, 1):
             ts(T.xn[:, b:640:4], bank(4 + b), 0.015625, None, A.mult, None, ["B%d" % (4 + b)], ["xn%d" % b])

@@ -1,4 +1,3 @@
-from concourse.bass import DstId, RemoteDMATransfer
 from concourse.mybir import dt, AluOpType as A, ActivationFunctionType as AF
 
 H, R = 160, 3
@@ -8,15 +7,15 @@ F32, BF, I32, U16, QC, U8 = "float32", "bfloat16", "int32", "uint16", "float8_e4
 
 SCRATCH = {"ps": ("psum", [128, 4096], F32)}
 for _d, _l in (
-    (BF, "xt 1280 ut 512 vt 512 rowg 128 ck 512 cv 512 ez 520 wtab 64 rs 160 sg 512 wm 480 wx 480 fl 640 "
+    (BF, "xt 1280 ut 512 vt 512 rowg 128 ck 512 cv 512 ez 520 wtab 64 lone 64 rs 160 sg 512 wm 480 wx 480 fl 640 "
          "tw 644 tx 640 v1 644 v2 640 et 644 e0 640 ft 640 xn 640"),
-    (F32, "hcf 4 pc 8 jrow 17 pw0 16 pw1 16 zr 16 pa1 16 pa2 16 pat4 16 pb1 16 pb2 16 pat16 16 d4 480 d16 160 ph 12 cl 10 "
+    (F32, "hcf 4 pc 8 jrow 17 pw0 16 pw1 16 zr 16 pa1 16 pa2 16 pat4 16 pb1 16 pb2 16 pat16 16 d4 160 d16 160 ph 12 cl 10 "
           "k64 30 idrow 160 ks 40 hb 40 dd 30 sc 480 s1 40 tab 40 vs 160 mm 30 tt 30 sel 30 w2 10 pab 320 pabs 320 "
-          "tmp 640 yb 320 cg 480 cs 480 ot0 352 ot1 352 ot2 352 oz0 128 oz1 128 oz2 128 lo0 64 lo1 64 lo2 64"),
-    (I32, "hci 4 pi 1 pci 4 yk 30 hd 60 xi 12 ex 48 oi 64 otr 192"),
-    (U16, "opt 30 opm 10 hu0 60 hu1 60 hu2 60 hu3 60 selu 30 pabu 80 cu 120"),
-    (QC, "qx 320 qu 128 qv 128 qw 512 qck 128 qcv 128 qe 512 qs 128 qf 160 qg 160 qz0 160 qz1 160 qz2 160 lq0 160 lq1 160 lq2 160"),
-    (U8, "sx 320 su 128 sv 128 sw 512 sck 128 scv 128 se 512 ss 128 sf 160 sq 160 sz0 160 sz1 160 sz2 160 ls0 160 ls1 160 ls2 160"),
+          "tmp 640 yb 320 cg 480 cs 480 ot0 352 ot1 352 ot2 352"),
+    (I32, "hci 4 pi 1 pci 4 yk 30 hd 50 xi 12 ex 48"),
+    (U16, "opt 10 opm 10 oq 4 hu0 50 hu1 50 hu2 50 hu3 50 so0 30 so1 30 so2 30 lo0 30 lo1 30 lo2 30 pabu 80 cu 120"),
+    (QC, "qx 320 qu 128 qv 128 qw 512 qck 128 qcv 128 qe 512 qs 128 qf 160 qg 160 qz 160 lq0 160 lq1 160 lq2 160"),
+    (U8, "sx 320 su 128 sv 128 sw 512 sck 128 scv 128 se 512 ss 128 sf 160 sq 160 sz 160 ls0 160 ls1 160 ls2 160"),
 ):
     _w = _l.split()
     for _i in range(0, len(_w), 2):
@@ -25,7 +24,7 @@ for _d, _l in (
 POOL = {"V": 24, "A": 12, "P": 16, "G": 24}
 NDMA = 16
 SEMAPHORES = ([q + "%d" % i for q in POOL for i in range(POOL[q])] + ["D%d" % i for i in range(NDMA)]
-              + ["ro%d" % t for t in range(R)] + ["rq%d" % t for t in range(R)] + ["sent"])
+              + [s + "%d" % t for t in range(R) for s in ("ro", "rq", "so", "sq")])
 
 
 def rank_program(g, core, T, topo):
@@ -40,7 +39,7 @@ def rank_program(g, core, T, topo):
     Q = {"V": g.vector, "A": g.scalar, "P": g.tensor, "G": g, "S": g.sync}
     known = {q: set() for q in Q}
     lastw, readers, last, count = {}, {}, {}, {}
-    nid, ndma, sent = [0], [0], [0]
+    nid, ndma = [0], [0]
 
     def wait(q, grp):
         if grp["id"] in known[q]:
@@ -98,12 +97,20 @@ def rank_program(g, core, T, topo):
             readers[k] = []
         return grp
 
-    def arrival(sem, val, keys):
+    def event(sem, val, r, w):
         nid[0] += 1
         grp = {"id": nid[0], "sem": sem, "val": val, "known": set(), "closed": True, "q": "X"}
         last[sem] = grp
-        for k in keys:
+        for k in r:
+            readers.setdefault(k, []).append(grp)
+        for k in w:
             lastw[k] = grp
+
+    def send(pairs, there, here, r):
+        need("G", r, ())
+        for dst, src in pairs:
+            g.remote_dma(dst, src, T.sem[there], T.sem[here], pid, rid, mask)
+        event(here, nout * len(pairs), r, ())
 
     V, S = g.vector, g.scalar
 
@@ -130,8 +137,8 @@ def rank_program(g, core, T, topo):
     def qz(c, s, t, r, w, join=None):
         return op("V", lambda: V.quantize_mx(c, s, t), r, w, join)
 
-    def act(out, a, r, w, scale=1.0, join=None, f=AF.Copy):
-        return op("A", lambda: S.activation(out, a, f, scale=scale), r, w, join)
+    def act(out, a, r, w, scale=1.0, join=None, f=AF.Copy, acc=None):
+        return op("A", lambda: S.activation(out, a, f, scale=scale, accum_out=acc), r, w, join)
 
     def mx(b, lc, ls, rc, rs, r, start=True, stop=True, w=H):
         return op("P", lambda: g.tensor.matmul_mx(bank(b, w), lc, ls, rc, rs, start, stop), r, ["B%d" % b], acc=not start)
@@ -172,15 +179,17 @@ def rank_program(g, core, T, topo):
     iota(T.fl[:, 3:640:4], [[0, H]], 0, 0, ["flz"], join=j)
     j = iota(T.rs[:, 0:H:40], [[0, 4]], 0, 0, ["rs"])
     iota(T.ph[:, 0:12:4], [[0, 3]], 2 + 2 ** 7 + 2 ** 13 + 2 ** 19, 0, ["ph"], join=j)
-    iota(T.ez[:], [[0, 520]], 64, 0, ["ez"])
-    op("G", lambda: g.affine_select(T.ez[:], T.ez[:], [[-1, 520]], A.is_equal, 0.0, 3, 4), ["ez"], ["ez"])
     j = iota(T.cl[:], [[16, 10]], 192, 0, ["cl"])
     iota(T.k64[:], [[64, 3], [0, 10]], 0, 0, ["k64"], join=j)
-    j = iota(T.idrow[:], [[1, H]], 0, 0, ["idrow"])
-    for b in ("tw", "v1", "et"):
-        iota(T[b][:, 640:644], [[0, 4]], 0, 0, [b + "z"], join=j)
-    for t in range(R):
-        iota(T["ot%d" % t][:, 0:192], [[0, 192]], H, 0, ["ot%d" % t], join=j)
+
+    def late_fills():
+        iota(T.ez[:], [[0, 520]], 64, 0, ["ez"])
+        op("G", lambda: g.affine_select(T.ez[:], T.ez[:], [[-1, 520]], A.is_equal, 0.0, 3, 4), ["ez"], ["ez"])
+        j = iota(T.idrow[:], [[1, H]], 0, 0, ["idrow"])
+        for b in ("tw", "v1", "et"):
+            iota(T[b][:, 640:644], [[0, 4]], 0, 0, [b + "z"], join=j)
+        for t in range(R):
+            iota(T["ot%d" % t][:, 0:192], [[0, 192]], H, 0, ["ot%d" % t], join=j)
 
     j = ms(T.ck[:], 0.0, ["ck"])
     ms(T.zr[:], 0.0, ["zr"], j)
@@ -192,7 +201,7 @@ def rank_program(g, core, T, topo):
     j = ts(T.pw0[:], T.jrow[:, 1:17], PM, 1.0, A.is_le, A.add, ["jrow", "pc"], ["pw0"])
     j2 = ts(T.pa1[:], T.jrow[:, 1:17], PA, BIG, A.is_equal, A.mult, ["jrow", "pc"], ["pa1"])
     ts(T.pa2[:], T.jrow[:, 0:16], PA, -M, A.is_equal, A.mult, ["jrow", "pc"], ["pa2"], j2)
-    ts(T.opt[:], T.rowg[:, 0:30], 0.0, PT, A.mult, A.add, ["rowg", "pc"], ["opt"], j2)
+    ts(T.opt[:], T.rowg[:, 0:10], 0.0, PT, A.mult, A.add, ["rowg", "pc"], ["opt"], j2)
     scan(T.pw1[:], T.pw0[:], T.zr[:], 0.5, A.mult, A.add, ["pw0", "zr"], ["pw1"])
     j = ts(C4, PA, 3.0, M, A.is_lt, A.mult, ["pc"], ["c4"])
     for d in range(4):
@@ -210,6 +219,7 @@ def rank_program(g, core, T, topo):
     def more_constants_1():
         j = qz(T.qck[:], T.sck[:], T.ck[:], ["ck0"], ["qck"])
         cp(T.hcf[:, 0:3], T.hci[:, 0:3], ["hci"], ["hcf"], j)
+        cp(T.oq[:], T.jrow[:, 1:5], ["jrow"], ["oq"], j)
 
     def more_constants_2():
         j = None
@@ -217,19 +227,17 @@ def rank_program(g, core, T, topo):
             j = ts(T.cv[:, t:512:4], T.rowg[:], PG, (4 >> t) * U, A.is_equal, A.mult, ["rowg", "pc"], ["cv%d" % t], j)
 
     def more_constants_3():
-        j = None
-        for b in range(4):
-            j = qz(eb(b)[0], eb(b)[1], T.ez[:, 3 - b:515 - b], ["ez"], ["qe%d" % b], j)
-
-    def more_constants_4():
         j = ts(T.pb1[:], T.jrow[:, 1:17], PM, BIG2, A.is_equal, A.mult, ["jrow", "pc"], ["pb1"])
         ts(T.pb2[:], T.jrow[:, 0:16], PM, -M2, A.is_equal, A.mult, ["jrow", "pc"], ["pb2"], j)
         j = ts(T.opm[:], T.rowg[:, 0:10], 0.0, PM, A.mult, A.add, ["rowg", "pc"], ["opm"])
         ts(T.hb[:, 0:10], T.cl[:], PM, None, A.add, None, ["cl", "pc"], ["hb0"], j)
-        ts(K4, C4, 4.0, PT, A.mult, A.add, ["c4", "pc"], ["k4"], j)
         ts(C16, PM, 15.0, M2, A.is_lt, A.mult, ["pc"], ["c16"], j)
         tt(T.pat16[:], T.pb1[:], T.pb2[:], A.add, ["pb1", "pb2"], ["pat16"])
-        act(T.d16[:], T.pat16[:].indirect(T.opm[:]), ["pat16", "opm"], ["d16"])
+
+    def units(bs):
+        j = None
+        for b in bs:
+            j = qz(eb(b)[0], eb(b)[1], T.ez[:, 3 - b:515 - b], ["ez"], ["qe%d" % b], j)
 
     TW = ["tw0", "tw1", "tw2", "tw3"]
     ET = ["et0", "et1", "et2", "et3", "etz"]
@@ -251,16 +259,18 @@ def rank_program(g, core, T, topo):
                    ["ks", "c4", "hcf"], ["yk%d" % k], j)
         ts(T.hd[:, 0:30], T.yk[:], 8, 63, A.logical_shift_right, A.bitwise_and, YK, ["hd0"])
         if digits:
-            ts(T.hd[:, 30:60], T.yk[:], 12, 3, A.logical_shift_right, A.bitwise_and, YK, ["hd1"])
+            ts(T.hd[:, 30:50], T.yk[:, 0:20], 12, 3, A.logical_shift_right, A.bitwise_and, YK, ["hd1"])
         cp(T[hu][:, 0:30], T.hd[:, 0:30], ["hd0"], [hu])
         if digits:
-            cp(T[hu][:, 30:60], T.hd[:, 30:60], ["hd1"], [hu + "d"])
+            cp(T[hu][:, 30:50], T.hd[:, 30:50], ["hd1"], [hu + "d"])
 
-    def decode(h, stop):
-        for b in range(4):
-            mx(4 + b, eb(b)[0], eb(b)[1], half(h)[0], half(h)[1], ["qe%d" % b, "qx%d" % h], stop=stop)
+    def decode(b0, order, c, s, key, stop=True):
+        for b in order:
+            mx(b0 + b, eb(b)[0], eb(b)[1], c, s, ["qe%d" % b, key], stop=stop)
 
-    def writers_numbers():
+    def writers_numbers(t):
+        event("rq%d" % t, 2 * nin, (), ["lq%d" % t])
+        decode(4, range(4), T["lq%d" % t][:], T["ls%d" % t][:], "lq%d" % t)
         for b in range(4):
             act(T.tw[:, b:640:4], bank(4 + b), ["B%d" % (4 + b)], ["tw%d" % b], scale=0.015625)
         act(T.tx[:], T.tw[:, 0:640], TW, ["tx"])
@@ -282,8 +292,10 @@ def rank_program(g, core, T, topo):
             j = ts(T.ex[:, d:48:4], T.xi[:], 1, 63 << (6 * d), A.logical_shift_right, A.bitwise_and, ["xi"], ["ex%d" % d], j)
         tt(T.s1[:], T.ex[:, 0:40], T.ex[:, 8:48], A.add, ["ex0", "ex1", "ex2", "ex3"], ["s1"])
         tt(T.tab[:, 0:36], T.s1[:, 0:36], T.s1[:, 4:40], A.add, ["s1"], ["tab"])
+        tt(T.lone[:], T.tab[:, 32:36].indirect(T.oq[:]), T.wtab[:], A.is_equal, ["tab", "oq", "wtab0"], ["lone"])
+        act(T.fl[:, 2:640:4], T.lone[:].indirect(T[hu][:, 20:30]), ["lone", hu], ["fl2"])
         j = None
-        for k in range(3):
+        for k in range(2):
             j = tt(T.fl[:, k:640:4], T.tab[:, 16 * k:16 * k + 4].indirect(T[hu][:, 30 + 10 * k:40 + 10 * k]),
                    third(T.wm, k), A.is_equal, ["tab", hu + "d", "wm%d" % k], ["fl%d" % k], j)
         if p == 0 and hu == "hu0":
@@ -296,7 +308,9 @@ def rank_program(g, core, T, topo):
     def remove():
         for k in range(3):
             tt(third(T.wx, k), third(T.wm, k), bank(1), A.subtract, ["wm%d" % k, "B1"], ["wx%d" % k])
-        act(third(T.wm, 0), third(T.wx, 0), ["wx0"], ["wm0"], f=AF.Relu)
+        j = None
+        for c in range(0, H, 40):
+            j = act(T.wm[:, c:c + 40], T.wx[:, c:c + 40], ["wx0"], ["wm0", "sc0"], f=AF.Relu, acc=T.sc[:, c + 39:c + 40], join=j)
         for k in (1, 2):
             ts(third(T.wm, k), third(T.wx, k), 0.0, None, A.max, None, ["wx%d" % k], ["wm%d" % k])
 
@@ -312,15 +326,16 @@ def rank_program(g, core, T, topo):
     for t in range(R):
         w, o = t % 2, 1 - t % 2
         hu, hr = "hu%d" % t, "hu%d" % ((t - 1) % 4)
-        ot, oz = T["ot%d" % t], T["oz%d" % t]
+        ot, so, lo = T["ot%d" % t], T["so%d" % t], T["lo%d" % t]
         scores(w, 0)
+        send([(T["lq%d" % t][:].bitcast(dt.uint8), half(w)[0].bitcast(dt.uint8)), (T["ls%d" % t][:], half(w)[1])],
+             "rq%d" % t, "sq%d" % t, ["qx%d" % w])
         if t == 0:
+            late_fills()
             more_constants_1()
         signs(0, 1)
         if t == 0:
             more_constants_2()
-        else:
-            decode(w, True)
         if t == 2:
             store(0, "SSSSS")
             mx(3, T.qv[:], T.sv[:], half(0)[0], half(0)[1], ["qv", "qx0"])
@@ -329,31 +344,28 @@ def rank_program(g, core, T, topo):
             act(third(T.wm, k), T.wtab[:].indirect(T[hu][:, 10 * k:10 * k + 10]), ["wtab0", hu], ["wm%d" % k])
         cp(third(T.wm, 0), T.wtab[:].indirect(T[hu][:, 0:10]), ["wtab0", hu], ["wm0"])
         cells()
-        if t > 0:
-            writers_numbers()
-        if t == 2:
-            act(T.yb[:, 0:H], bank(3), ["B3"], ["yb0"])
-            dma("S", T.y[:, 0:H], T.yb[:, 0:H], ["yb0"], ())
         peel(0, hu, (0, 1, 2))
         if t == 0:
             more_constants_3()
-            decode(0, True)
         else:
             choices()
         remove()
         if t == 0:
-            writers_numbers()
-        peel(1, hu, (1, 2, 0))
-        if t == 0:
-            more_constants_4()
-        if t == 1:
-            qz(T.qv[:], T.sv[:], T.vt[:], ["vt"], ["qv"])
-        remove()
-        peel(2, hu, (1, 2, 0))
+            act(T.d16[:], T.pat16[:].indirect(T.opm[:]), ["pat16", "opm"], ["d16"])
+        peel(1, hu, (1, 2))
         if t == 0:
             choices()
             qz(half(1)[0], half(1)[1], T.xt[:, 640:1280], ["xt1"], ["qx1"])
             scores(1, 3)
+        remove()
+        peel(2, hu, (1, 2))
+        if t > 0:
+            writers_numbers(t)
+        else:
+            units((0, 1))
+        if t == 2:
+            act(T.yb[:, 0:H], bank(3), ["B3"], ["yb0"])
+            dma("S", T.y[:, 0:H], T.yb[:, 0:H], ["yb0"], ())
         scan(T.vs[:], T.d16[:], bank(2), 0.0, A.add, A.min, ["d16", "B2"], ["vs"])
         j = None
         for i, th in enumerate((1.0, 4.0, 2.0)):
@@ -362,24 +374,32 @@ def rank_program(g, core, T, topo):
         j = tt(T.sel[:], T.tt[:], T.hb[:, 0:30], A.add, ["tt", "hb", "hb0"], ["sel", "sel0"])
         tt(T.w2[:], T.tt[:, 10:20], T.tt[:, 20:30], A.add, ["tt"], ["w2"], j)
         tt(T.sel[:, 0:10], T.sel[:, 0:10], T.w2[:], A.subtract, ["sel0", "w2"], ["sel0"])
-        cp(T.selu[:, 10:30], T.sel[:, 10:30], ["sel"], ["selu"])
-        cp(T.selu[:, 0:10], T.sel[:, 0:10], ["sel0"], ["selu0"])
-        okey = "ot%d" % t
-        cp(ot[:].indirect(T.selu[:, 0:10]), T.idrow[:], ["selu0", "idrow"], [okey])
-        act(third(T.pab, 1), ot[:, 0:192].indirect(T.selu[:, 20:30]), [okey, "selu"], ["pab1"])
-        cp(third(T.pab, 0), ot[:, 0:192].indirect(T.selu[:, 10:20]), [okey, "selu"], ["pab0"])
-        j = act(oz[:, 0:64], ot[:, 64:128], [okey], ["oza%d" % t], scale=256.0)
-        act(oz[:, 64:128], ot[:, 128:192], [okey], ["ozb%d" % t], scale=65536.0, join=j)
-        need("G", [okey, "oza%d" % t, "ozb%d" % t], ())
-        g.remote_dma_fused([RemoteDMATransfer(dst_ids=[DstId(rid=rid, pnc=pid)], dma_engine_mask=mask,
-                                              remote_sem=T.sem["ro%d" % t], srcs=[ot[:, 0:64], oz[:, 0:64], oz[:, 64:128]],
-                                              dsts=[T["lo%d" % t][:]], alu_op=1)], local_sem=T.sem.sent)
-        sent[0] += nout
+        cp(so[:], T.sel[:], ["sel", "sel0"], ["so%d" % t])
+        send([(lo[:], so[:])], "ro%d" % t, "so%d" % t, ["so%d" % t])
+        if t == 0:
+            signs(3, 3)
+            units((2, 3))
+            ts(K4, C4, 4.0, PT, A.mult, A.add, ["c4", "pc"], ["k4"])
+            writers_numbers(0)
+            addresses(3, hr, False)
+        if t == 1:
+            qz(T.qv[:], T.sv[:], T.vt[:], ["vt"], ["qv"])
+        decode(4, range(4), half(o)[0], half(o)[1], "qx%d" % o, False)
+        okey, lkey = "ot%d" % t, "lo%d" % t
+        event("ro%d" % t, nin, (), [lkey])
+        cp(ot[:].indirect(lo[:, 0:10]), T.idrow[:], [lkey, "idrow"], [okey])
+        act(third(T.pab, 1), ot[:, 0:192].indirect(lo[:, 20:30]), [okey, lkey], ["pab1"])
+        cp(third(T.pab, 0), ot[:, 0:192].indirect(lo[:, 10:20]), [okey, lkey], ["pab0"])
+        for k in range(3):
+            act(third(T.cg, k), ot[:, 64 * k:64 * k + 64].indirect(T[hr][:, 10 * k:10 * k + 10]), [okey, hr], ["cg%d" % k])
         for i in range(2):
-            scan(third(T.pabs, i), T.d4[:, 0:H], third(T.pab, i), 0.0, A.add, A.min, ["d4", "pab%d" % i], ["pabs%d" % i])
+            scan(third(T.pabs, i), T.d4[:], third(T.pab, i), 0.0, A.add, A.min, ["d4", "pab%d" % i], ["pabs%d" % i])
         for i in range(2):
             ts(T.pabu[:, 40 * i:40 * i + 40], T.pabs[:, H * i + 3:H * i + H:4], 4.0, K4, A.mult, A.add, ["pabs%d" % i, "k4"], ["pabu%d" % i])
-        decode(o, False)
+
+        def compose(k):
+            scan(third(T.cs, k), T.d4[:], third(T.cg, k), 0.0, A.add, A.min, ["d4", "cg%d" % k], ["cs%d" % k])
+
         for src, keys, first, dst in ((T.tw, TW + ["twz"], A.subtract, "v1"), (T.v1, ["v10", "v11", "v1z"], A.add, "v2")):
             for i in range(2):
                 tt(T.tmp[:, 320 * i:320 * i + 320], src[:].indirect(T.pabu[:, 20 * i:20 * i + 20]), T.tx[:, 320 * i:320 * i + 320],
@@ -388,30 +408,11 @@ def rank_program(g, core, T, topo):
             for i in range(2):
                 j = tt(T[dst][:, 320 * i:320 * i + 320], src[:].indirect(T.pabu[:, 40 + 20 * i:60 + 20 * i]),
                        T.tmp[:, 320 * i:320 * i + 320], A.add, keys + ["pabu1", "tmp%d" % i], [dst + "%d" % i], j)
-        qz(T["qz%d" % t][:], T["sz%d" % t][:], T.v2[:], ["v20", "v21"], ["qz%d" % t])
-        need("G", ["qz%d" % t], ())
-        g.remote_dma(T["lq%d" % t][:].bitcast(dt.uint8), T["qz%d" % t][:].bitcast(dt.uint8), T.sem["rq%d" % t], T.sem.sent, pid, rid, mask)
-        g.remote_dma(T["ls%d" % t][:], T["sz%d" % t][:], T.sem["rq%d" % t], T.sem.sent, pid, rid, mask)
-        sent[0] += 2 * nout
-        if t == 0:
-            signs(3, 3)
-        arrival("ro%d" % t, nin, ["lo%d" % t])
-        cp(T.oi[:], T["lo%d" % t][:], ["lo%d" % t], ["oi"])
-        j = ts(T.otr[:, 0:64], T.oi[:], 255, None, A.bitwise_and, None, ["oi"], ["otr0"])
-        ts(T.otr[:, 64:128], T.oi[:], 8, 255, A.logical_shift_right, A.bitwise_and, ["oi"], ["otr1"], j)
-        ts(T.otr[:, 128:192], T.oi[:], 16, None, A.logical_shift_right, None, ["oi"], ["otr2"], j)
-        if t == 0:
-            addresses(3, hr, False)
-        for k in range(3):
-            cp(third(T.cg, k), T.otr[:, 64 * k:64 * k + 64].indirect(T[hr][:, 10 * k:10 * k + 10]),
-               ["otr0", "otr1", "otr2", hr], ["cg%d" % k])
-        j = None
-        for k in range(3):
-            j = scan(third(T.cs, k), T.d4[:, 0:H], third(T.cg, k), 0.0, A.add, A.min, ["d4", "cg%d" % k], ["cs%d" % k], j)
+            compose(0 if dst == "v1" else 1)
+        qz(T.qz[:], T.sz[:], T.v2[:], ["v20", "v21"], ["qz"])
+        decode(0, (2, 0, 3, 1), T.qz[:], T.sz[:], "qz")
+        compose(2)
         ts(T.cu[:], T.cs[:, 3:480:4], 4.0, K4, A.mult, A.add, ["cs0", "cs1", "cs2", "k4"], ["cu"])
-        arrival("rq%d" % t, 2 * nin, ["lq%d" % t])
-        for b in (2, 0, 3, 1):
-            mx(b, eb(b)[0], eb(b)[1], T["lq%d" % t][:], T["ls%d" % t][:], ["qe%d" % b, "lq%d" % t])
         for b in (0, 1):
             ts(T.et[:, b:640:4], bank(b), 0.015625, None, A.mult, None, ["B%d" % b], ["et%d" % b])
             act(T.et[:, b + 2:640:4], bank(b + 2), ["B%d" % (b + 2)], ["et%d" % (b + 2)], scale=0.015625)
@@ -436,7 +437,6 @@ def rank_program(g, core, T, topo):
             ts(T.xn[:, b:640:4], bank(4 + b), 0.015625, None, A.mult, None, ["B%d" % (4 + b)], ["xn%d" % b])
             act(T.xn[:, b + 2:640:4], bank(6 + b), ["B%d" % (6 + b)], ["xn%d" % (b + 2)], scale=0.015625)
         if t == R - 1:
-            g.wait_ge(T.sem.sent, sent[0])
             for grp in sorted(last.values(), key=lambda x: -x["id"]):
                 wait("G", grp)
         qz(half(o)[0], half(o)[1], T.xn[:], ["xn0", "xn1", "xn2", "xn3"], ["qx%d" % o])

@@ -1,27 +1,30 @@
 from concourse.mybir import dt, AluOpType as A, ActivationFunctionType as AF
 
 H, R = 160, 3
-BIG, M = float(2 ** 20), float(2 ** 17)
+CH, TH, PL = 54, 162, 176
+BIG, M = float(2 ** 20), float(2 ** 16)
 U, BIG2, M2 = float(2 ** 20), float(2 ** 26), float(2 ** 24)
+TOP, HUGE, TINY = 2 ** 24 - 1, float(2 ** 60), float(2 ** -60)
+MID = [27 * sum(64 ** e for e in range(d, 3)) for d in range(4)]
 F32, BF, I32, U16, QC, U8 = "float32", "bfloat16", "int32", "uint16", "float8_e4m3fn_x4", "uint8"
 
 SCRATCH = {"ps": ("psum", [128, 4096], F32)}
 for _d, _l in (
-    (BF, "xt 1280 ut 512 vt 512 rowg 128 ck 512 cv 512 ez 520 wtab 64 lone 64 rs 160 sg 512 wm 480 wx 480 fl 640 "
-         "tw 644 tx 640 v1 644 v2 640 et 644 e0 640 ft 640 xn 640"),
-    (F32, "hcf 4 pc 8 jrow 17 pw0 16 pw1 16 zr 16 pa1 16 pa2 16 pat4 16 pb1 16 pb2 16 pat16 16 d4 160 d16 160 ph 12 cl 10 "
-          "k64 30 idrow 160 ks 40 hb 40 dd 30 sc 480 s1 40 tab 40 vs 160 mm 30 tt 30 sel 30 w2 10 pab 320 pabs 320 "
-          "tmp 640 yb 320 cg 480 cs 480 ot0 352 ot1 352 ot2 352"),
-    (I32, "hci 4 pi 1 pci 4 yk 30 hd 50 xi 12 ex 48"),
-    (U16, "opt 10 opm 10 oq 4 hu0 50 hu1 50 hu2 50 hu3 50 so0 30 so1 30 so2 30 lo0 30 lo1 30 lo2 30 pabu 80 cu 120"),
-    (QC, "qx 320 qu 128 qv 128 qw 512 qck 128 qcv 128 qe 512 qs 128 qf 160 qg 160 qz 160 lq0 160 lq1 160 lq2 160"),
-    (U8, "sx 320 su 128 sv 128 sw 512 sck 128 scv 128 se 512 ss 128 sf 160 sq 160 sz 160 ls0 160 ls1 160 ls2 160"),
+    (BF, "xt 1280 ut 512 vt 512 rowg 128 ck 512 cv 512 ez 520 e1 520 wtab 64 lone 64 sg 512 wm 486 dec 486 wx 320 fl 640 "
+         "tw 704 tx 320 ga 960 v1 704 v2 640 et 704 e0 640 ft 640 xn 640"),
+    (F32, "hcf 4 pc 10 jrow 17 pw0 16 pw1 16 zr 16 pa1 16 pa2 16 pat4 16 pb1 16 pb2 16 pat16 16 d4 64 d16 160 cl 10 sp 10 "
+          "k64 48 crow 48 idrow 160 ks 48 hb 48 rs0 162 rs1 162 sc 486 rb 135 tab 108 vs 160 r4 4 r6 6 th0 96 thr 96 dh 96 mm 96 sel 96 "
+          "pab 320 pabs 320 tq 640 yb 320 cg 480 cs 480 ot0 352 ot1 352 ot2 352"),
+    (I32, "hci 4 pi 1 pci 4 yk 48 hd 48 dg 32"),
+    (U16, "opt 10 opm 10 oq 4 lk 4 lv 6 hu0 48 hu1 48 hu2 48 hu3 48 du 32 so0 34 so1 34 so2 34 lo0 34 lo1 34 lo2 34 pabu 20 cu 30"),
+    (QC, "qx 320 qu 128 qv 128 qw 512 qck 128 qcv 128 qe 512 q1 512 qs 128 qf 160 qg 160 qz 160 lq0 160 lq1 160 lq2 160"),
+    (U8, "sx 320 su 128 sv 128 sw 512 sck 128 scv 128 se 512 s1 512 ss 128 sf 160 sq 160 sz 160 ls0 160 ls1 160 ls2 160"),
 ):
     _w = _l.split()
     for _i in range(0, len(_w), 2):
         SCRATCH[_w[_i]] = ("sbuf", [128, int(_w[_i + 1])], _d)
 
-POOL = {"V": 24, "A": 12, "P": 16, "G": 24}
+POOL = {"V": 40, "A": 20, "P": 16, "G": 24}
 NDMA = 16
 SEMAPHORES = ([q + "%d" % i for q in POOL for i in range(POOL[q])] + ["D%d" % i for i in range(NDMA)]
               + [s + "%d" % t for t in range(R) for s in ("ro", "rq", "so", "sq")])
@@ -137,8 +140,8 @@ def rank_program(g, core, T, topo):
     def qz(c, s, t, r, w, join=None):
         return op("V", lambda: V.quantize_mx(c, s, t), r, w, join)
 
-    def act(out, a, r, w, scale=1.0, join=None, f=AF.Copy, acc=None):
-        return op("A", lambda: S.activation(out, a, f, scale=scale, accum_out=acc), r, w, join)
+    def act(out, a, r, w, scale=1.0, join=None):
+        return op("A", lambda: S.activation(out, a, AF.Copy, scale=scale), r, w, join)
 
     def mx(b, lc, ls, rc, rs, r, start=True, stop=True, w=H):
         return op("P", lambda: g.tensor.matmul_mx(bank(b, w), lc, ls, rc, rs, start, stop), r, ["B%d" % b], acc=not start)
@@ -151,16 +154,23 @@ def rank_program(g, core, T, topo):
             return op("G", lambda: g.iota(out, pat, base, cm, allow_small_or_imprecise_dtypes=True), (), w, join)
         return op("G", lambda: g.iota(out, pat, base, cm), (), w, join)
 
+    def fill(out, n, c, w, join=None):
+        return iota(out, [[0, n]], c, 0, w, join=join)
+
     def half(h):
         return T.qx[:, H * h:H * h + H], T.sx[:, H * h:H * h + H]
 
-    def eb(b):
-        return T.qe[:, 128 * b:128 * b + 128], T.se[:, 128 * b:128 * b + 128]
+    def eb(b, unit):
+        c, s = (T.q1, T.s1) if unit else (T.qe, T.se)
+        return c[:, 128 * b:128 * b + 128], s[:, 128 * b:128 * b + 128]
 
-    def third(buf, k):
-        return buf[:, H * k:H * k + H]
+    def third(buf, k, w=H, step=H):
+        return buf[:, step * k:step * k + w]
 
-    PM, PG, PT, PA, C4, K4, C16 = [T.pc[:, j:j + 1] for j in range(7)]
+    def lst(buf, k):
+        return buf[:, 16 * k:16 * k + 10]
+
+    PM, PG, PT, PA, C16, A16 = [T.pc[:, j:j + 1] for j in range(6)]
 
     dma("S", T.xt[:, 0:640], T.x[:, 0:640], (), ["xt0"])
     dma("A", T.ut[:], T.u[:], (), ["ut"])
@@ -173,23 +183,40 @@ def rank_program(g, core, T, topo):
     iota(T.pi[:], [[0, 1]], 0, 1, ["pi"], flt=False)
     iota(T.jrow[:], [[1, 17]], -1, 0, ["jrow"])
     iota(T.rowg[:], [[1, 8], [0, 16]], 0, 0, ["rowg"])
-    iota(T.sg[:, H:512], [[0, 512 - H]], 0, 0, ["sgz"])
-    j = iota(T.rs[:], [[0, H]], 1, 0, ["rs"])
-    iota(T.ph[:], [[0, 12]], 0, 0, ["ph"], join=j)
-    iota(T.fl[:, 3:640:4], [[0, H]], 0, 0, ["flz"], join=j)
-    j = iota(T.rs[:, 0:H:40], [[0, 4]], 0, 0, ["rs"])
-    iota(T.ph[:, 0:12:4], [[0, 3]], 2 + 2 ** 7 + 2 ** 13 + 2 ** 19, 0, ["ph"], join=j)
-    j = iota(T.cl[:], [[16, 10]], 192, 0, ["cl"])
-    iota(T.k64[:], [[64, 3], [0, 10]], 0, 0, ["k64"], join=j)
+    fill(T.sg[:, H:512], 512 - H, 0, ["sgz"])
+    fill(T.rs0[:], TH, TOP, ["rs0"])
+    iota(T.r4[:], [[27, 4]], 26, 0, ["r4"])
+    fill(T.rb[:], 135, 0, ["rbz"])
+    fill(T.rs0[:, 0:TH:CH], 3, -MID[0], ["rs0"])
+
+    def centre():
+        j = None
+        need("G", ["rbz"], ())
+        for d in range(4):
+            j = fill(T.rb[:, 27 * d + 2:27 * d + 27:3], 9, MID[d], ["rbB%d" % d], j)
+
+    def peel_fills():
+        j = fill(T.fl[:, 3:640:4], H, 0, ["flz"])
+        fill(T.rs1[:], TH, -TOP, ["rs1"])
+        j = iota(T.cl[:], [[16, 10]], 192, 0, ["cl"])
+        iota(T.k64[:], [[64, 3], [0, 16]], 0, 0, ["k64"], join=j)
+        fill(T.rs1[:, 0:TH:CH], 3, MID[0], ["rs1"])
+        fill(T.ez[:], 520, 64, ["ez"])
+        fill(T.dh[:], 96, 0, ["dhz"])
+        op("G", lambda: g.affine_select(T.ez[:], T.ez[:], [[-1, 520]], A.is_equal, 0.0, 3, 4), ["ez"], ["ez"])
 
     def late_fills():
-        iota(T.ez[:], [[0, 520]], 64, 0, ["ez"])
-        op("G", lambda: g.affine_select(T.ez[:], T.ez[:], [[-1, 520]], A.is_equal, 0.0, 3, 4), ["ez"], ["ez"])
+        fill(T.th0[:], 96, TOP, ["th0"])
+        iota(T.r6[:], [[0, 2], [64, 3]], 15, 0, ["r6"])
+        j = None
+        for at, cnt, c in ((slice(1, 96, 4), 24, 4), (slice(2, 48, 4), 12, 2), (slice(51, 96, 4), 12, 2), (slice(3, 48, 4), 12, 1)):
+            need("G", (), ["th0"])
+            j = fill(T.th0[:, at], cnt, c * int(U), ["th1"], j)
         j = iota(T.idrow[:], [[1, H]], 0, 0, ["idrow"])
         for b in ("tw", "v1", "et"):
-            iota(T[b][:, 640:644], [[0, 4]], 0, 0, [b + "z"], join=j)
+            fill(T[b][:, H:4 * PL:PL], 4, 0, [b + "z"], j)
         for t in range(R):
-            iota(T["ot%d" % t][:, 0:192], [[0, 192]], H, 0, ["ot%d" % t], join=j)
+            fill(T["ot%d" % t][:, 0:192], 192, H, ["ot%d" % t], j)
 
     j = ms(T.ck[:], 0.0, ["ck"])
     ms(T.zr[:], 0.0, ["zr"], j)
@@ -197,122 +224,173 @@ def rank_program(g, core, T, topo):
     ts(T.pci[:, 1:2], T.pi[:], 4, None, A.logical_shift_right, None, ["pi"], ["pci1"], j)
     ts(T.pci[:, 2:3], T.pi[:], 3, None, A.bitwise_and, None, ["pi"], ["pci2"], j)
     ts(T.pci[:, 3:4], T.pi[:], 2, 3, A.logical_shift_right, A.bitwise_and, ["pi"], ["pci3"], j)
+    j = ms(T.wm[:, H:3 * TH:TH], 0.0, ["wmz"])
+    ms(T.wm[:, H + 1:3 * TH:TH], 0.0, ["wmz"], j)
+    ms(T.dec[:], 0.0, ["decz"], j)
     cp(T.pc[:, 0:4], T.pci[:], ["pci0"], ["pc"])
     j = ts(T.pw0[:], T.jrow[:, 1:17], PM, 1.0, A.is_le, A.add, ["jrow", "pc"], ["pw0"])
     j2 = ts(T.pa1[:], T.jrow[:, 1:17], PA, BIG, A.is_equal, A.mult, ["jrow", "pc"], ["pa1"])
     ts(T.pa2[:], T.jrow[:, 0:16], PA, -M, A.is_equal, A.mult, ["jrow", "pc"], ["pa2"], j2)
     ts(T.opt[:], T.rowg[:, 0:10], 0.0, PT, A.mult, A.add, ["rowg", "pc"], ["opt"], j2)
     scan(T.pw1[:], T.pw0[:], T.zr[:], 0.5, A.mult, A.add, ["pw0", "zr"], ["pw1"])
-    j = ts(C4, PA, 3.0, M, A.is_lt, A.mult, ["pc"], ["c4"])
+    j = ts(T.opm[:], T.rowg[:, 0:10], 0.0, PM, A.mult, A.add, ["rowg", "pc"], ["opm"])
     for d in range(4):
-        ts(T.wtab[:, 16 * d:16 * d + 16], T.jrow[:, 1:17], PM, float(2 ** (6 * d + 1)), A.is_equal, A.mult,
+        ts(T.wtab[:, 16 * d:16 * d + 16], T.jrow[:, 1:17], PM, float(64 ** d), A.is_equal, A.mult,
            ["jrow", "pc"], ["wtab%d" % d], j)
     j = None
     for t in range(4):
         j = ts(T.ck[:, 5 * t:512:16], T.rowg[:, t:128:4], PG, T.pw1[:, 15:16], A.is_equal, A.mult,
                ["rowg", "pc", "pw1", "ck"], ["ck%d" % t], j)
     tt(T.pat4[:], T.pa1[:], T.pa2[:], A.add, ["pa1", "pa2"], ["pat4"])
-    act(T.d4[:], T.pat4[:].indirect(T.opt[:]), ["pat4", "opt"], ["d4"])
+    act(T.d4[:], T.pat4[:].indirect(T.opt[:, 0:4]), ["pat4", "opt"], ["d4"])
     j = qz(half(0)[0], half(0)[1], T.xt[:, 0:640], ["xt0"], ["qx0"])
     qz(T.qu[:], T.su[:], T.ut[:], ["ut"], ["qu"], j)
 
     def more_constants_1():
         j = qz(T.qck[:], T.sck[:], T.ck[:], ["ck0"], ["qck"])
         cp(T.hcf[:, 0:3], T.hci[:, 0:3], ["hci"], ["hcf"], j)
-        cp(T.oq[:], T.jrow[:, 1:5], ["jrow"], ["oq"], j)
+        ts(T.lk[:], T.opm[:, 0:4], 9.0, 4.0, A.min, A.mult, ["opm"], ["lk"], j)
+        ts(T.wtab[:], T.wtab[:], TINY, None, A.max, None, ["wtab0"], ["wtab"], j)
 
     def more_constants_2():
+        j = None
+        for k in range(3):
+            j = ts(T.crow[:, 16 * k:16 * k + 16], T.zr[:], T.hcf[:, k:k + 1], None, A.add, None, ["zr", "hcf"], ["crow%d" % k], j)
+        j = cp(T.oq[:], T.r4[:], ["r4"], ["oq"])
+        need("V", (), ["rbz"])
+        ms(T.rb[:, 0:135:9], HUGE, ["rbh"], j)
+
+    def more_constants_3():
         j = None
         for t in range(4):
             j = ts(T.cv[:, t:512:4], T.rowg[:], PG, (4 >> t) * U, A.is_equal, A.mult, ["rowg", "pc"], ["cv%d" % t], j)
 
-    def more_constants_3():
+    def more_constants_4():
         j = ts(T.pb1[:], T.jrow[:, 1:17], PM, BIG2, A.is_equal, A.mult, ["jrow", "pc"], ["pb1"])
         ts(T.pb2[:], T.jrow[:, 0:16], PM, -M2, A.is_equal, A.mult, ["jrow", "pc"], ["pb2"], j)
-        j = ts(T.opm[:], T.rowg[:, 0:10], 0.0, PM, A.mult, A.add, ["rowg", "pc"], ["opm"])
-        ts(T.hb[:, 0:10], T.cl[:], PM, None, A.add, None, ["cl", "pc"], ["hb0"], j)
+
+    def more_constants_5():
+        qz(T.qcv[:], T.scv[:], T.cv[:], ["cv0"], ["qcv"])
+
+    def more_constants_6():
+        j = ts(T.sp[:], T.cl[:], PM, None, A.add, None, ["cl", "pc"], ["sp"])
         ts(C16, PM, 15.0, M2, A.is_lt, A.mult, ["pc"], ["c16"], j)
+        ts(A16, PA, 16.0, None, A.mult, None, ["pc"], ["a16"], j)
         tt(T.pat16[:], T.pb1[:], T.pb2[:], A.add, ["pb1", "pb2"], ["pat16"])
+        act(T.d16[:], T.pat16[:].indirect(T.opm[:]), ["pat16", "opm"], ["d16"])
 
-    def units(bs):
+    def more_constants_7():
+        j = ts(T.lv[:], T.r6[:], A16, 159.0, A.add, A.min, ["r6", "a16"], ["lv"])
+        ts(T.thr[:], T.th0[:], C16, None, A.subtract, None, ["th0", "th1", "c16"], ["thr"], j)
+        cp(T.dh[:, 3:40:4], T.sp[:], ["sp", "dhz"], ["dh3"], j)
+
+    def units(bs, unit):
         j = None
+        src, key = (T.e1, "e1") if unit else (T.ez, "ez")
         for b in bs:
-            j = qz(eb(b)[0], eb(b)[1], T.ez[:, 3 - b:515 - b], ["ez"], ["qe%d" % b], j)
+            j = qz(eb(b, unit)[0], eb(b, unit)[1], src[:, 3 - b:515 - b], [key], ["q%s%d" % (key, b)], j)
 
-    TW = ["tw0", "tw1", "tw2", "tw3"]
-    ET = ["et0", "et1", "et2", "et3", "etz"]
-    YK = ["yk0", "yk1", "yk2"]
+    SC = ["sc0", "sc1", "sc2"]
+    DH = ["dh%d" % i for i in range(8)]
 
     def scores(h, b):
         mx(b, T.qu[:], T.su[:], half(h)[0], half(h)[1], ["qu", "qx%d" % h])
 
-    def signs(b, kb):
+    def signs(b):
         ts(T.sg[:, 0:H], bank(b), 0.0, None, A.is_gt, None, ["B%d" % b], ["sg"])
+
+    def keys(kb):
         qz(T.qs[:], T.ss[:], T.sg[:], ["sg", "sgz"], ["qs"])
         mx(kb, T.qck[:], T.sck[:], T.qs[:], T.ss[:], ["qck", "qs"], w=128)
 
-    def addresses(kb, hu, digits):
-        scan(T.ks[:], T.d4[:, 0:40], bank(kb, 40), 0.0, A.add, A.min, ["d4", "B%d" % kb], ["ks"])
-        j = None
-        for k in range(3):
-            j = ts(T.yk[:, 10 * k:10 * k + 10], T.ks[:, 3:40:4], C4, T.hcf[:, k:k + 1], A.add, A.mult,
-                   ["ks", "c4", "hcf"], ["yk%d" % k], j)
-        ts(T.hd[:, 0:30], T.yk[:], 8, 63, A.logical_shift_right, A.bitwise_and, YK, ["hd0"])
-        if digits:
-            ts(T.hd[:, 30:50], T.yk[:, 0:20], 12, 3, A.logical_shift_right, A.bitwise_and, YK, ["hd1"])
-        cp(T[hu][:, 0:30], T.hd[:, 0:30], ["hd0"], [hu])
-        if digits:
-            cp(T[hu][:, 30:50], T.hd[:, 30:50], ["hd1"], [hu + "d"])
+    def addresses(kb, hu):
+        return [lambda: scan(T.ks[:, 5:45], T.d4[:, 0:40], bank(kb, 40), 0.0, A.add, A.min, ["d4", "B%d" % kb], ["ks"]),
+                lambda: tt(T.yk[:], T.ks[:, 8:45].indirect(T.lk[:, 0:3]), T.crow[:], A.mult, ["ks", "lk", "crow0"], ["yk"]),
+                lambda: ts(T.hd[:], T.yk[:], 8, 63, A.logical_shift_right, A.bitwise_and, ["yk"], ["hd"]),
+                lambda: cp(T[hu][:], T.hd[:], ["hd"], [hu])]
 
-    def decode(b0, order, c, s, key, stop=True):
+    def writers_addresses(kb, hu):
+        steps = addresses(kb, hu)
+        for step in steps[:3]:
+            step()
+        ts(T.dg[:], T.yk[:, 0:32], 12, 3, A.logical_shift_right, A.bitwise_and, ["yk"], ["dg"])
+        steps[3]()
+        j = None
+        for k in range(2):
+            j = ts(T.du[:, 16 * k:16 * k + 16], T.dg[:, 16 * k:16 * k + 16], 27.0, 9.0 * k + 8, A.mult, A.add, ["dg"], ["du%d" % k], j)
+
+    def first_readers():
+        qz(half(1)[0], half(1)[1], T.xt[:, 640:1280], ["xt1"], ["qx1"])
+        scores(1, 3)
+
+    ra = addresses(3, "hu3")
+    un = [lambda b=b, u=u: units((b,), u) for u in (False, True) for b in range(4)]
+    spare = [first_readers, more_constants_4, lambda: signs(3), more_constants_5, lambda: keys(3), ra[0], ra[1], ra[2], un[0], ra[3]] + un[1:]
+
+    def gap(n=1):
+        for i in range(min(n, len(spare))):
+            spare.pop(0)()
+
+    def decode(b0, order, c, s, key, unit, stop=True):
         for b in order:
-            mx(b0 + b, eb(b)[0], eb(b)[1], c, s, ["qe%d" % b, key], stop=stop)
+            mx(b0 + b, eb(b, unit)[0], eb(b, unit)[1], c, s, ["q%s%d" % ("e1" if unit else "ez", b), key], stop=stop)
 
     def writers_numbers(t):
         event("rq%d" % t, 2 * nin, (), ["lq%d" % t])
-        decode(4, range(4), T["lq%d" % t][:], T["ls%d" % t][:], "lq%d" % t)
+        decode(4, range(4), T["lq%d" % t][:], T["ls%d" % t][:], "lq%d" % t, True)
         for b in range(4):
-            act(T.tw[:, b:640:4], bank(4 + b), ["B%d" % (4 + b)], ["tw%d" % b], scale=0.015625)
-        act(T.tx[:], T.tw[:, 0:640], TW, ["tx"])
+            act(third(T.tw, b, H, PL), bank(4 + b), ["B%d" % (4 + b)], ["tw%d" % b])
+        for b in range(2):
+            act(third(T.tx, b), bank(4 + b), ["B%d" % (4 + b)], ["tx%d" % b])
 
     def cells():
-        tt(T.hb[:, 10:40], T.hd[:, 0:30], T.k64[:], A.add, ["hd0", "k64"], ["hb"])
+        tt(T.hb[:], T.hd[:], T.k64[:], A.add, ["hd", "k64"], ["hb"])
 
     def choices():
-        j = tt(T.dd[:, 0:10], T.hb[:, 30:40], T.hb[:, 0:10], A.subtract, ["hb", "hb0"], ["dd0"])
-        tt(T.dd[:, 10:30], T.hb[:, 20:40], T.hb[:, 10:30], A.subtract, ["hb"], ["dd1"], j)
+        h = [lst(T.hb, k) for k in range(3)]
+        j = None
+        for i, at, x, y in ((0, 0, h[0], h[1]), (1, 1, h[1], h[2]), (2, 2, h[2], T.sp[:]), (4, 48, h[1], h[0]), (6, 50, h[2], h[1])):
+            j = tt(T.dh[:, at:at + 40:4], x, y, A.subtract, ["hb", "sp", "dhz"], [DH[i]], j)
+        for i, at, x in ((5, 49, h[0]), (7, 51, h[1])):
+            j = cp(T.dh[:, at:at + 40:4], x, ["hb", "dhz"], [DH[i]], j)
 
-    def peel(p, hu, order):
+    def counts(p, b):
+        src = "dec" if p else "wm"
+        if p:
+            for k in range(3):
+                tt(third(T.dec, k, H, TH), third(T.wm, k, H, TH), bank(b), A.min, ["wm%d" % k, "B%d" % b, "decz"], ["dec%d" % k])
+        for k in range(3):
+            a = (T.rs1[:], A.max, A.subtract) if p else (T.rs0[:], A.min, A.add)
+            scan(third(T.sc, k, TH, TH), a[0], third(T[src], k, TH, TH), 0.0, a[1], a[2],
+                 ["rs%d" % min(p, 1), src + "%d" % k, src + "z"], ["sc%d" % k])
+
+    def left(k, b):
+        tt(third(T.wx, k), third(T.wm, k, H, TH), bank(b), A.subtract, ["wm%d" % k, "B%d" % b], ["wx%d" % k])
+
+    def peel(p, hu, b):
+        key, at = ("rbB", 2) if p else ("rbA", 1)
+        ends = T.sc[:, CH - 1:3 * TH:CH]
+        left(0, b) if p else gap()
+        act(T.rb[:, at:27:3], ends, SC + ["rbz"], [key + "0"])
         j = None
-        for k in order:
-            j = scan(third(T.sc, k), T.rs[:], third(T.wm, k), 0.0, A.mult, A.add, ["rs", "wm%d" % k], ["sc%d" % k], j)
-        tt(T.xi[:], T.sc[:, 39:480:40], T.ph[:], A.add, ["sc0", "sc1", "sc2", "ph"], ["xi"])
-        j = None
-        for d in range(4):
-            j = ts(T.ex[:, d:48:4], T.xi[:], 1, 63 << (6 * d), A.logical_shift_right, A.bitwise_and, ["xi"], ["ex%d" % d], j)
-        tt(T.s1[:], T.ex[:, 0:40], T.ex[:, 8:48], A.add, ["ex0", "ex1", "ex2", "ex3"], ["s1"])
-        tt(T.tab[:, 0:36], T.s1[:, 0:36], T.s1[:, 4:40], A.add, ["s1"], ["tab"])
-        tt(T.lone[:], T.tab[:, 32:36].indirect(T.oq[:]), T.wtab[:], A.is_equal, ["tab", "oq", "wtab0"], ["lone"])
-        act(T.fl[:, 2:640:4], T.lone[:].indirect(T[hu][:, 20:30]), ["lone", hu], ["fl2"])
+        for d in (1, 2, 3):
+            big = 1.5 * 2 ** (23 + 6 * d)
+            j = ts(T.rb[:, 27 * d + at:27 * d + 27:3], ends, big, big, A.add, A.subtract, SC + ["rbz"], [key + "%d" % d], j)
+        left(1, b) if p else gap()
+        scan(T.tab[:], T.rb[:, 0:108], T.rb[:, 27:135], 0.0, A.add, A.subtract,
+             ["rbh"] + ["rb%s%d" % (s, d) for s in "AB" for d in range(4)], ["tab"])
+        gap()
+        tt(T.lone[:], T.tab[:].indirect(T.oq[:]), T.wtab[:], A.is_equal, ["tab", "oq", "wtab"], ["lone"])
+        act(T.fl[:, 2:640:4], T.lone[:].indirect(lst(T[hu], 2)), ["lone", hu], ["fl2"])
         j = None
         for k in range(2):
-            j = tt(T.fl[:, k:640:4], T.tab[:, 16 * k:16 * k + 4].indirect(T[hu][:, 30 + 10 * k:40 + 10 * k]),
-                   third(T.wm, k), A.is_equal, ["tab", hu + "d", "wm%d" % k], ["fl%d" % k], j)
-        if p == 0 and hu == "hu0":
-            qz(T.qcv[:], T.scv[:], T.cv[:], ["cv0"], ["qcv"])
+            x, xk = (third(T.wx, k), "wx%d" % k) if p else (third(T.wm, k, H, TH), "wm%d" % k)
+            j = tt(T.fl[:, k:640:4], T.tab[:].indirect(lst(T.du, k)), x, A.is_equal, ["tab", "du0", xk], ["fl%d" % k], j)
+        gap()
         qz(T.qf[:], T.sf[:], T.fl[:], ["fl0", "fl1", "fl2", "flz"], ["qf"])
-        if p < 2:
-            mx(1, T.qcv[:], T.scv[:], T.qf[:], T.sf[:], ["qcv", "qf"])
-        mx(2, T.qcv[:], T.scv[:], T.qf[:], T.sf[:], ["qcv", "qf"], start=p == 0, stop=p == 2)
-
-    def remove():
-        for k in range(3):
-            tt(third(T.wx, k), third(T.wm, k), bank(1), A.subtract, ["wm%d" % k, "B1"], ["wx%d" % k])
-        j = None
-        for c in range(0, H, 40):
-            j = act(T.wm[:, c:c + 40], T.wx[:, c:c + 40], ["wx0"], ["wm0", "sc0"], f=AF.Relu, acc=T.sc[:, c + 39:c + 40], join=j)
-        for k in (1, 2):
-            ts(third(T.wm, k), third(T.wx, k), 0.0, None, A.max, None, ["wx%d" % k], ["wm%d" % k])
+        for i, bk in enumerate((1, 0, 2)):
+            if i >= p:
+                mx(bk, T.qcv[:], T.scv[:], T.qf[:], T.sf[:], ["qcv", "qf"], start=p == 0, stop=p == i)
 
     def store(h, qs):
         lo = H * h
@@ -328,109 +406,134 @@ def rank_program(g, core, T, topo):
         hu, hr = "hu%d" % t, "hu%d" % ((t - 1) % 4)
         ot, so, lo = T["ot%d" % t], T["so%d" % t], T["lo%d" % t]
         scores(w, 0)
+        if t == 0:
+            centre()
+            peel_fills()
         send([(T["lq%d" % t][:].bitcast(dt.uint8), half(w)[0].bitcast(dt.uint8)), (T["ls%d" % t][:], half(w)[1])],
              "rq%d" % t, "sq%d" % t, ["qx%d" % w])
         if t == 0:
             late_fills()
             more_constants_1()
-        signs(0, 1)
+        else:
+            centre()
+        signs(0)
+        keys(1)
         if t == 0:
             more_constants_2()
         if t == 2:
             store(0, "SSSSS")
             mx(3, T.qv[:], T.sv[:], half(0)[0], half(0)[1], ["qv", "qx0"])
-        addresses(1, hu, True)
+        writers_addresses(1, hu)
         for k in (1, 2):
-            act(third(T.wm, k), T.wtab[:].indirect(T[hu][:, 10 * k:10 * k + 10]), ["wtab0", hu], ["wm%d" % k])
-        cp(third(T.wm, 0), T.wtab[:].indirect(T[hu][:, 0:10]), ["wtab0", hu], ["wm0"])
-        cells()
-        peel(0, hu, (0, 1, 2))
+            act(third(T.wm, k, H, TH), T.wtab[:].indirect(lst(T[hu], k)), ["wtab", hu], ["wm%d" % k])
+        cp(third(T.wm, 0, H, TH), T.wtab[:].indirect(lst(T[hu], 0)), ["wtab", hu], ["wm0"])
         if t == 0:
             more_constants_3()
+        counts(0, None)
+        peel(0, hu, None)
+        cells()
+        gap()
+        if t == 0:
+            more_constants_6()
+        counts(1, 1)
+        peel(1, hu, 1)
+        choices()
+        gap()
+        if t == 0:
+            act(T.e1[:], T.ez[:], ["ez"], ["e1"], scale=0.015625)
         else:
-            choices()
-        remove()
-        if t == 0:
-            act(T.d16[:], T.pat16[:].indirect(T.opm[:]), ["pat16", "opm"], ["d16"])
-        peel(1, hu, (1, 2))
-        if t == 0:
-            choices()
-            qz(half(1)[0], half(1)[1], T.xt[:, 640:1280], ["xt1"], ["qx1"])
-            scores(1, 3)
-        remove()
-        peel(2, hu, (1, 2))
-        if t > 0:
             writers_numbers(t)
-        else:
-            units((0, 1))
+        counts(2, 0)
+        peel(2, hu, 0)
+        gap(2)
+        if t == 0:
+            more_constants_7()
         if t == 2:
             act(T.yb[:, 0:H], bank(3), ["B3"], ["yb0"])
             dma("S", T.y[:, 0:H], T.yb[:, 0:H], ["yb0"], ())
         scan(T.vs[:], T.d16[:], bank(2), 0.0, A.add, A.min, ["d16", "B2"], ["vs"])
-        j = None
-        for i, th in enumerate((1.0, 4.0, 2.0)):
-            j = ts(T.mm[:, 10 * i:10 * i + 10], T.vs[:, 15:H:16], C16, th * U, A.add, A.is_ge, ["vs", "c16"], ["mm%d" % i], j)
-        tt(T.tt[:], T.mm[:], T.dd[:], A.mult, ["mm0", "mm1", "mm2", "dd0", "dd1"], ["tt"])
-        j = tt(T.sel[:], T.tt[:], T.hb[:, 0:30], A.add, ["tt", "hb", "hb0"], ["sel", "sel0"])
-        tt(T.w2[:], T.tt[:, 10:20], T.tt[:, 20:30], A.add, ["tt"], ["w2"], j)
-        tt(T.sel[:, 0:10], T.sel[:, 0:10], T.w2[:], A.subtract, ["sel0", "w2"], ["sel0"])
-        cp(so[:], T.sel[:], ["sel", "sel0"], ["so%d" % t])
-        send([(lo[:], so[:])], "ro%d" % t, "so%d" % t, ["so%d" % t])
+        gap()
+        tt(T.mm[:], T.vs[:].indirect(T.lv[:]), T.thr[:], A.is_ge, ["vs", "lv", "thr"], ["mm"])
+        gap()
+        scan(T.sel[:], T.mm[:], T.dh[:], 0.0, A.mult, A.add, ["mm", "dhz"] + DH, ["sel"])
+        gap()
+        j = cp(so[:, 0:24], T.sel[:, 3:96:4], ["sel"], ["so%d" % t])
+        cp(so[:, 24:34], T.sel[:, 49:89:4], ["sel"], ["sa%d" % t], j)
+        send([(lo[:], so[:])], "ro%d" % t, "so%d" % t, ["so%d" % t, "sa%d" % t])
         if t == 0:
-            signs(3, 3)
-            units((2, 3))
-            ts(K4, C4, 4.0, PT, A.mult, A.add, ["c4", "pc"], ["k4"])
+            gap(len(spare))
             writers_numbers(0)
-            addresses(3, hr, False)
         if t == 1:
             qz(T.qv[:], T.sv[:], T.vt[:], ["vt"], ["qv"])
-        decode(4, range(4), half(o)[0], half(o)[1], "qx%d" % o, False)
         okey, lkey = "ot%d" % t, "lo%d" % t
         event("ro%d" % t, nin, (), [lkey])
         cp(ot[:].indirect(lo[:, 0:10]), T.idrow[:], [lkey, "idrow"], [okey])
-        act(third(T.pab, 1), ot[:, 0:192].indirect(lo[:, 20:30]), [okey, lkey], ["pab1"])
-        cp(third(T.pab, 0), ot[:, 0:192].indirect(lo[:, 10:20]), [okey, lkey], ["pab0"])
+        act(third(T.pab, 1), ot[:, 0:192].indirect(lo[:, 12:22]), [okey, lkey], ["pab1"])
+        cp(third(T.pab, 0), ot[:, 0:192].indirect(lo[:, 24:34]), [okey, lkey], ["pab0"])
         for k in range(3):
-            act(third(T.cg, k), ot[:, 64 * k:64 * k + 64].indirect(T[hr][:, 10 * k:10 * k + 10]), [okey, hr], ["cg%d" % k])
+            act(third(T.cg, k), ot[:, 64 * k:64 * k + 64].indirect(lst(T[hr], k)), [okey, hr], ["cg%d" % k])
         for i in range(2):
-            scan(third(T.pabs, i), T.d4[:], third(T.pab, i), 0.0, A.add, A.min, ["d4", "pab%d" % i], ["pabs%d" % i])
-        for i in range(2):
-            ts(T.pabu[:, 40 * i:40 * i + 40], T.pabs[:, H * i + 3:H * i + H:4], 4.0, K4, A.mult, A.add, ["pabs%d" % i, "k4"], ["pabu%d" % i])
+            scan(third(T.pabs, i), T.d16[:], third(T.pab, i), 0.0, A.add, A.min, ["d16", "pab%d" % i], ["pabs%d" % i])
+
+        def places(i):
+            ts(T.pabu[:, 10 * i:10 * i + 10], T.pabs[:, H * i + 15:H * i + H:16], C16, None, A.add, None, ["pabs%d" % i, "c16"], ["pabu%d" % i])
 
         def compose(k):
-            scan(third(T.cs, k), T.d4[:], third(T.cg, k), 0.0, A.add, A.min, ["d4", "cg%d" % k], ["cs%d" % k])
+            scan(third(T.cs, k), T.d16[:], third(T.cg, k), 0.0, A.add, A.min, ["d16", "cg%d" % k], ["cs%d" % k])
 
-        for src, keys, first, dst in ((T.tw, TW + ["twz"], A.subtract, "v1"), (T.v1, ["v10", "v11", "v1z"], A.add, "v2")):
-            for i in range(2):
-                tt(T.tmp[:, 320 * i:320 * i + 320], src[:].indirect(T.pabu[:, 20 * i:20 * i + 20]), T.tx[:, 320 * i:320 * i + 320],
-                   first, keys + ["tx", "pabu0"], ["tmp%d" % i] + ["tmp2"] * i)
-            j = None
-            for i in range(2):
-                j = tt(T[dst][:, 320 * i:320 * i + 320], src[:].indirect(T.pabu[:, 40 + 20 * i:60 + 20 * i]),
-                       T.tmp[:, 320 * i:320 * i + 320], A.add, keys + ["pabu1", "tmp%d" % i], [dst + "%d" % i], j)
-            compose(0 if dst == "v1" else 1)
-        qz(T.qz[:], T.sz[:], T.v2[:], ["v20", "v21"], ["qz"])
-        decode(0, (2, 0, 3, 1), T.qz[:], T.sz[:], "qz")
-        compose(2)
-        ts(T.cu[:], T.cs[:, 3:480:4], 4.0, K4, A.mult, A.add, ["cs0", "cs1", "cs2", "k4"], ["cu"])
-        for b in (0, 1):
-            ts(T.et[:, b:640:4], bank(b), 0.015625, None, A.mult, None, ["B%d" % b], ["et%d" % b])
-            act(T.et[:, b + 2:640:4], bank(b + 2), ["B%d" % (b + 2)], ["et%d" % (b + 2)], scale=0.015625)
-        cut = ((0, 10), (10, 24), (24, 40))
-        for i in (1, 2):
-            a, b = cut[i]
-            act(T.e0[:, 16 * a:16 * b], T.et[:].indirect(T.cu[:, a:b]), ET + ["cu"], ["e0%d" % i])
-        cp(T.e0[:, 0:H], T.et[:].indirect(T.cu[:, 0:10]), ET + ["cu"], ["e00"])
-        j = None
-        for step, i in ((1, 0), (1, 1), (2, 0), (1, 2), (2, 1), (2, 2)):
-            a, b = cut[i]
-            if step == 1:
-                tt(T.tmp[:, 16 * a:16 * b], T.et[:].indirect(T.cu[:, 40 + a:40 + b]), T.e0[:, 16 * a:16 * b], A.add,
-                   ET + ["cu", "e0%d" % i], ["tmp%d" % i])
+        pa, pb = T.pabu[:, 0:10], T.pabu[:, 10:20]
+
+        def window(s, b):
+            return third(T["v1" if s else "tw"], b, H + 1, PL), [("v1" if s else "tw") + c for c in ("z", "%d" % b)]
+
+        def fetch(s, b):
+            act(third(T.ga, 4 * s + b - 2), window(s, b)[0].indirect(pa), window(s, b)[1] + ["pabu0"], ["ga%d%d" % (s, b)])
+
+        def one(s, b):
+            if s == 0 and b < 2:
+                tt(third(T.tq, b), window(s, b)[0].indirect(pa), third(T.tx, b), A.subtract, window(s, b)[1] + ["pabu0", "tx%d" % b], ["tq%d" % b])
             else:
-                j = tt(T.ft[:, 16 * a:16 * b], T.et[:].indirect(T.cu[:, 80 + a:80 + b]), T.tmp[:, 16 * a:16 * b], A.add,
-                       ET + ["cu", "tmp%d" % i], ["ft%d" % i], j)
-        qz(T.qg[:], T.sq[:], T.ft[:], ["ft0", "ft1", "ft2"], ["qg"])
+                tt(third(T.tq, b), third(T.ga, 4 * s + b - 2), bank(4 + b), A.add if s else A.subtract,
+                   ["ga%d%d" % (s, b), "B%d" % (4 + b)], ["tq%d" % b])
+
+        def two(s, b):
+            out = T.v2[:, b:640:4] if s else third(T.v1, b, H, PL)
+            tt(out, window(s, b)[0].indirect(pb), third(T.tq, b), A.add, window(s, b)[1] + ["pabu1", "tq%d" % b], ["v%d%d" % (s + 1, b)])
+            if s == 0:
+                fetch(1, b)
+
+        places(0)
+        compose(0)
+        places(1)
+        fetch(0, 2)
+        fetch(0, 3)
+        todo = [(s, b) for s in range(2) for b in range(4)]
+        one(0, 0)
+        for i in range(8):
+            if i < 7:
+                one(*todo[i + 1])
+            two(*todo[i])
+        decode(4, range(4), half(o)[0], half(o)[1], "qx%d" % o, False, False)
+        compose(1)
+        qz(T.qz[:], T.sz[:], T.v2[:], ["v20", "v21", "v22", "v23"], ["qz"])
+        decode(0, range(4), T.qz[:], T.sz[:], "qz", True)
+        compose(2)
+        ts(T.cu[:], T.cs[:, 15:480:16], C16, None, A.add, None, ["cs0", "cs1", "cs2", "c16"], ["cu"])
+
+        def read(k, b):
+            return third(T.et, b, H + 1, PL).indirect(T.cu[:, 10 * k:10 * k + 10]), ["etz", "et%d" % b, "cu"]
+
+        for b in range(4):
+            (act if b == 1 else cp)(third(T.et, b, H, PL), bank(b), ["B%d" % b], ["et%d" % b])
+        for b in range(4):
+            act(third(T.e0, b), read(0, b)[0], read(0, b)[1], ["e0%d" % b])
+        j = None
+        for k, b in ((1, 0), (1, 1), (2, 0), (1, 2), (2, 1), (1, 3), (2, 2), (2, 3)):
+            if k == 1:
+                tt(third(T.tq, b), read(1, b)[0], third(T.e0, b), A.add, read(1, b)[1] + ["e0%d" % b], ["tq%d" % b])
+            else:
+                j = tt(T.ft[:, b:640:4], read(2, b)[0], third(T.tq, b), A.add, read(2, b)[1] + ["tq%d" % b], ["ft%d" % b], j)
+        qz(T.qg[:], T.sq[:], T.ft[:], ["ft0", "ft1", "ft2", "ft3"], ["qg"])
         for b in (2, 0, 3, 1):
             mx(4 + b, T.qw[:, 128 * b:128 * b + 128], T.sw[:, 128 * b:128 * b + 128], T.qg[:], T.sq[:], ["qw", "sw", "qg"], start=False)
         for b in (0, 1):

@@ -1,7 +1,8 @@
 from concourse.mybir import dt, AluOpType as A, ActivationFunctionType as AF
 
 H, R = 160, 3
-CH, TH, PL = 54, 162, 176
+TH, PL = 180, 176
+SA, SB = 19 * 53, 9 * 53
 BIG, M = float(2 ** 20), float(2 ** 16)
 U, BIG2, M2 = float(2 ** 20), float(2 ** 26), float(2 ** 24)
 TOP, HUGE, TINY = 2 ** 24 - 1, float(2 ** 60), float(2 ** -60)
@@ -10,10 +11,10 @@ F32, BF, I32, U16, QC, U8 = "float32", "bfloat16", "int32", "uint16", "float8_e4
 
 SCRATCH = {"ps": ("psum", [128, 4096], F32)}
 for _d, _l in (
-    (BF, "xt 1280 ut 512 vt 512 rowg 128 ck 512 cv 512 ez 520 e1 520 wtab 64 lone 64 sg 512 wm 486 dec 486 wx 320 fl 640 "
+    (BF, "xt 1280 ut 512 vt 512 rowg 128 ck 512 cv 512 ez 520 e1 520 wtab 64 lone 64 sg 512 wm 540 dec 540 cut 20 z60 60 wx 320 fl 640 "
          "tw 704 tx 320 ga 960 v1 704 v2 640 et 704 e0 640 ft 640 xn 640"),
     (F32, "hcf 4 pc 10 jrow 17 pw0 16 pw1 16 zr 16 pa1 16 pa2 16 pat4 16 pb1 16 pb2 16 pat16 16 d4 64 d16 160 cl 10 sp 10 "
-          "k64 48 crow 48 idrow 160 ks 48 hb 48 rs0 162 rs1 162 sc 486 rb 135 tab 108 vs 160 r4 4 r6 6 th0 96 thr 96 dh 96 mm 96 sel 96 "
+          "k64 48 crow 48 idrow 160 ks 48 hb 48 sa 1200 sb 570 tab 76 tab2 36 vs 160 r4 4 r6 6 th0 96 thr 96 dh 96 mm 96 sel 96 "
           "pab 320 pabs 320 tq 640 yb 320 cg 480 cs 480 ot0 352 ot1 352 ot2 352"),
     (I32, "hci 4 pi 1 pci 4 yk 48 hd 48 dg 32"),
     (U16, "opt 10 opm 10 oq 4 lk 4 lv 6 hu0 48 hu1 48 hu2 48 hu3 48 du 32 so0 34 so1 34 so2 34 lo0 34 lo1 34 lo2 34 pabu 20 cu 30"),
@@ -184,23 +185,22 @@ def rank_program(g, core, T, topo):
     iota(T.jrow[:], [[1, 17]], -1, 0, ["jrow"])
     iota(T.rowg[:], [[1, 8], [0, 16]], 0, 0, ["rowg"])
     fill(T.sg[:, H:512], 512 - H, 0, ["sgz"])
-    fill(T.rs0[:], TH, TOP, ["rs0"])
-    iota(T.r4[:], [[27, 4]], 26, 0, ["r4"])
-    fill(T.rb[:], 135, 0, ["rbz"])
-    fill(T.rs0[:, 0:TH:CH], 3, -MID[0], ["rs0"])
+    iota(T.r4[:], [[9, 4]], 8, 0, ["r4"])
+    fill(T.z60[:], 60, 0, ["z60"])
+    j = fill(T.sa[:, SA:SA + 190:2], 95, 0, ["scz"])
+    fill(T.sb[:, SB:SB + 90:2], 45, 0, (), j)
 
     def centre():
         j = None
-        need("G", ["rbz"], ())
+        need("G", ["scz"], ())
         for d in range(4):
-            j = fill(T.rb[:, 27 * d + 2:27 * d + 27:3], 9, MID[d], ["rbB%d" % d], j)
+            j = fill(T.sa[:, SA + 38 * d + 4:SA + 38 * d + 36:6], 6, MID[d], ["saB", "sbB"] * (d == 0), j)
+            fill(T.sb[:, SB + 18 * d + 4:SB + 18 * d + 18:6], 3, MID[d], (), j)
 
     def peel_fills():
         j = fill(T.fl[:, 3:640:4], H, 0, ["flz"])
-        fill(T.rs1[:], TH, -TOP, ["rs1"])
         j = iota(T.cl[:], [[16, 10]], 192, 0, ["cl"])
         iota(T.k64[:], [[64, 3], [0, 16]], 0, 0, ["k64"], join=j)
-        fill(T.rs1[:, 0:TH:CH], 3, MID[0], ["rs1"])
         fill(T.ez[:], 520, 64, ["ez"])
         fill(T.dh[:], 96, 0, ["dhz"])
         op("G", lambda: g.affine_select(T.ez[:], T.ez[:], [[-1, 520]], A.is_equal, 0.0, 3, 4), ["ez"], ["ez"])
@@ -224,41 +224,52 @@ def rank_program(g, core, T, topo):
     ts(T.pci[:, 1:2], T.pi[:], 4, None, A.logical_shift_right, None, ["pi"], ["pci1"], j)
     ts(T.pci[:, 2:3], T.pi[:], 3, None, A.bitwise_and, None, ["pi"], ["pci2"], j)
     ts(T.pci[:, 3:4], T.pi[:], 2, 3, A.logical_shift_right, A.bitwise_and, ["pi"], ["pci3"], j)
-    j = ms(T.wm[:, H:3 * TH:TH], 0.0, ["wmz"])
-    ms(T.wm[:, H + 1:3 * TH:TH], 0.0, ["wmz"], j)
-    ms(T.dec[:], 0.0, ["decz"], j)
+    cut = [0.0] + [s * 1.5 * 2 ** (23 + 6 * d) for d in (1, 2, 3) for s in (1, -1)]
+    j = ms(T.cut[:, 0:2], cut[0], ["cut"])
+    for e in (1, 2):
+        ms(T.cut[:, 3 * e - 1:3 * e + 2], cut[e], (), j)
     cp(T.pc[:, 0:4], T.pci[:], ["pci0"], ["pc"])
+    for e in (3, 4, 5, 6):
+        ms(T.cut[:, 3 * e - 1:3 * e + 2], cut[e], (), j)
+    j = None
+    for b in ("wm", "dec"):
+        for k in range(3):
+            j = act(T[b][:, TH * k + H:TH * k + TH], T.cut[:], ["cut"], [b + "z"] * (k == 0), join=j)
     j = ts(T.pw0[:], T.jrow[:, 1:17], PM, 1.0, A.is_le, A.add, ["jrow", "pc"], ["pw0"])
     j2 = ts(T.pa1[:], T.jrow[:, 1:17], PA, BIG, A.is_equal, A.mult, ["jrow", "pc"], ["pa1"])
     ts(T.pa2[:], T.jrow[:, 0:16], PA, -M, A.is_equal, A.mult, ["jrow", "pc"], ["pa2"], j2)
     ts(T.opt[:], T.rowg[:, 0:10], 0.0, PT, A.mult, A.add, ["rowg", "pc"], ["opt"], j2)
     scan(T.pw1[:], T.pw0[:], T.zr[:], 0.5, A.mult, A.add, ["pw0", "zr"], ["pw1"])
-    j = ts(T.opm[:], T.rowg[:, 0:10], 0.0, PM, A.mult, A.add, ["rowg", "pc"], ["opm"])
-    for d in range(4):
-        ts(T.wtab[:, 16 * d:16 * d + 16], T.jrow[:, 1:17], PM, float(64 ** d), A.is_equal, A.mult,
-           ["jrow", "pc"], ["wtab%d" % d], j)
-    j = None
-    for t in range(4):
-        j = ts(T.ck[:, 5 * t:512:16], T.rowg[:, t:128:4], PG, T.pw1[:, 15:16], A.is_equal, A.mult,
-               ["rowg", "pc", "pw1", "ck"], ["ck%d" % t], j)
+    ts(T.opm[:], T.rowg[:, 0:10], 0.0, PM, A.mult, A.add, ["rowg", "pc"], ["opm"])
     tt(T.pat4[:], T.pa1[:], T.pa2[:], A.add, ["pa1", "pa2"], ["pat4"])
     act(T.d4[:], T.pat4[:].indirect(T.opt[:, 0:4]), ["pat4", "opt"], ["d4"])
-    j = qz(half(0)[0], half(0)[1], T.xt[:, 0:640], ["xt0"], ["qx0"])
-    qz(T.qu[:], T.su[:], T.ut[:], ["ut"], ["qu"], j)
+    qz(T.qu[:], T.su[:], T.ut[:], ["ut"], ["qu"])
+    qz(half(0)[0], half(0)[1], T.xt[:, 0:640], ["xt0"], ["qx0"])
+
+    def more_constants_0():
+        j = None
+        for t in range(4):
+            j = ts(T.ck[:, 5 * t:512:16], T.rowg[:, t:128:4], PG, T.pw1[:, 15:16], A.is_equal, A.mult,
+                   ["rowg", "pc", "pw1", "ck"], ["ck%d" % t], j)
+        j = cp(T.hcf[:, 0:3], T.hci[:, 0:3], ["hci"], ["hcf"])
+        ts(T.lk[:], T.opm[:, 0:4], 9.0, 4.0, A.min, A.mult, ["opm"], ["lk"], j)
+        qz(T.qck[:], T.sck[:], T.ck[:], ["ck0"], ["qck"])
 
     def more_constants_1():
-        j = qz(T.qck[:], T.sck[:], T.ck[:], ["ck0"], ["qck"])
-        cp(T.hcf[:, 0:3], T.hci[:, 0:3], ["hci"], ["hcf"], j)
-        ts(T.lk[:], T.opm[:, 0:4], 9.0, 4.0, A.min, A.mult, ["opm"], ["lk"], j)
-        ts(T.wtab[:], T.wtab[:], TINY, None, A.max, None, ["wtab0"], ["wtab"], j)
+        j = None
+        for d in range(4):
+            j = ts(T.wtab[:, 16 * d:16 * d + 16], T.jrow[:, 1:17], PM, float(64 ** d), A.is_equal, A.mult,
+                   ["jrow", "pc"], ["wtab%d" % d], j)
 
     def more_constants_2():
+        ts(T.wtab[:], T.wtab[:], TINY, None, A.max, None, ["wtab0"], ["wtab"])
         j = None
         for k in range(3):
             j = ts(T.crow[:, 16 * k:16 * k + 16], T.zr[:], T.hcf[:, k:k + 1], None, A.add, None, ["zr", "hcf"], ["crow%d" % k], j)
         j = cp(T.oq[:], T.r4[:], ["r4"], ["oq"])
-        need("V", (), ["rbz"])
-        ms(T.rb[:, 0:135:9], HUGE, ["rbh"], j)
+        need("V", ["scz"], ())
+        for at in (T.sa[:, SA:SA + 190:38], T.sa[:, SA + 18:SA + 190:38], T.sb[:, SB:SB + 90:18]):
+            j = ms(at, HUGE, ["sch"], j)
 
     def more_constants_3():
         j = None
@@ -290,7 +301,6 @@ def rank_program(g, core, T, topo):
         for b in bs:
             j = qz(eb(b, unit)[0], eb(b, unit)[1], src[:, 3 - b:515 - b], [key], ["q%s%d" % (key, b)], j)
 
-    SC = ["sc0", "sc1", "sc2"]
     DH = ["dh%d" % i for i in range(8)]
 
     def scores(h, b):
@@ -311,21 +321,22 @@ def rank_program(g, core, T, topo):
 
     def writers_addresses(kb, hu):
         steps = addresses(kb, hu)
-        for step in steps[:3]:
+        for step in (steps[0], gap, steps[1], gap, steps[2]):
             step()
         ts(T.dg[:], T.yk[:, 0:32], 12, 3, A.logical_shift_right, A.bitwise_and, ["yk"], ["dg"])
         steps[3]()
         j = None
         for k in range(2):
-            j = ts(T.du[:, 16 * k:16 * k + 16], T.dg[:, 16 * k:16 * k + 16], 27.0, 9.0 * k + 8, A.mult, A.add, ["dg"], ["du%d" % k], j)
+            j = ts(T.du[:, 16 * k:16 * k + 16], T.dg[:, 16 * k:16 * k + 16], 19.0, 9.0 * k + 8, A.mult, A.add, ["dg"], ["du%d" % k], j)
 
     def first_readers():
         qz(half(1)[0], half(1)[1], T.xt[:, 640:1280], ["xt1"], ["qx1"])
         scores(1, 3)
 
     ra = addresses(3, "hu3")
-    un = [lambda b=b, u=u: units((b,), u) for u in (False, True) for b in range(4)]
-    spare = [first_readers, more_constants_4, lambda: signs(3), more_constants_5, lambda: keys(3), ra[0], ra[1], ra[2], un[0], ra[3]] + un[1:]
+    un = [lambda b=b, u=u: units((b,), u) for u in (True, False) for b in range(4)]
+    spare = [more_constants_3, first_readers, more_constants_5, lambda: signs(3), lambda: keys(3),
+             ra[0], ra[1], ra[2], un[0], ra[3]] + un[1:]
 
     def gap(n=1):
         for i in range(min(n, len(spare))):
@@ -357,30 +368,26 @@ def rank_program(g, core, T, topo):
     def counts(p, b):
         src = "dec" if p else "wm"
         if p:
-            for k in range(3):
-                tt(third(T.dec, k, H, TH), third(T.wm, k, H, TH), bank(b), A.min, ["wm%d" % k, "B%d" % b, "decz"], ["dec%d" % k])
-        for k in range(3):
-            a = (T.rs1[:], A.max, A.subtract) if p else (T.rs0[:], A.min, A.add)
-            scan(third(T.sc, k, TH, TH), a[0], third(T[src], k, TH, TH), 0.0, a[1], a[2],
-                 ["rs%d" % min(p, 1), src + "%d" % k, src + "z"], ["sc%d" % k])
+            for k in (2, 0, 1):
+                tt(third(T.dec, k, H, TH), third(T.wm, k, H, TH), bank(b), A.min, ["wm%d" % k, "B%d" % b], ["dec%d" % k])
+        j = {}
+        for k in (2, 0, 1):
+            buf, s = ("sb", 9) if k == 2 else ("sa", 19)
+            for c in range(3):
+                at = 2 * (9 * (k % 2) + 3 * c + (2 if p else 1))
+                j[buf] = scan(T[buf][:, at:at + s * 59 + 1:s], T.z60[:], T[src][:, TH * k + c:TH * k + TH:3], float(MID[0] if p else -MID[0]),
+                              A.add, A.subtract if p else A.add, ["z60", src + "%d" % k, src + "z", "scz"], [buf + ("B" if p else "A")], j.get(buf))
 
     def left(k, b):
         tt(third(T.wx, k), third(T.wm, k, H, TH), bank(b), A.subtract, ["wm%d" % k, "B%d" % b], ["wx%d" % k])
 
     def peel(p, hu, b):
-        key, at = ("rbB", 2) if p else ("rbA", 1)
-        ends = T.sc[:, CH - 1:3 * TH:CH]
+        scan(T.tab2[:], T.sb[:, SB:SB + 72:2], T.sb[:, SB + 18:SB + 90:2], 0.0, A.add, A.subtract, ["sch", "sbA", "sbB"], ["tab2"])
         left(0, b) if p else gap()
-        act(T.rb[:, at:27:3], ends, SC + ["rbz"], [key + "0"])
-        j = None
-        for d in (1, 2, 3):
-            big = 1.5 * 2 ** (23 + 6 * d)
-            j = ts(T.rb[:, 27 * d + at:27 * d + 27:3], ends, big, big, A.add, A.subtract, SC + ["rbz"], [key + "%d" % d], j)
-        left(1, b) if p else gap()
-        scan(T.tab[:], T.rb[:, 0:108], T.rb[:, 27:135], 0.0, A.add, A.subtract,
-             ["rbh"] + ["rb%s%d" % (s, d) for s in "AB" for d in range(4)], ["tab"])
-        gap()
-        tt(T.lone[:], T.tab[:].indirect(T.oq[:]), T.wtab[:], A.is_equal, ["tab", "oq", "wtab"], ["lone"])
+        scan(T.tab[:], T.sa[:, SA:SA + 152:2], T.sa[:, SA + 38:SA + 190:2], 0.0, A.add, A.subtract, ["sch", "saA", "saB"], ["tab"])
+        tt(T.lone[:], T.tab2[:].indirect(T.oq[:]), T.wtab[:], A.is_equal, ["tab2", "oq", "wtab"], ["lone"])
+        if p:
+            left(1, b)
         act(T.fl[:, 2:640:4], T.lone[:].indirect(lst(T[hu], 2)), ["lone", hu], ["fl2"])
         j = None
         for k in range(2):
@@ -413,10 +420,12 @@ def rank_program(g, core, T, topo):
              "rq%d" % t, "sq%d" % t, ["qx%d" % w])
         if t == 0:
             late_fills()
-            more_constants_1()
+            more_constants_0()
         else:
             centre()
         signs(0)
+        if t == 0:
+            more_constants_1()
         keys(1)
         if t == 0:
             more_constants_2()
@@ -424,13 +433,13 @@ def rank_program(g, core, T, topo):
             store(0, "SSSSS")
             mx(3, T.qv[:], T.sv[:], half(0)[0], half(0)[1], ["qv", "qx0"])
         writers_addresses(1, hu)
-        for k in (1, 2):
+        for k in (2, 1):
             act(third(T.wm, k, H, TH), T.wtab[:].indirect(lst(T[hu], k)), ["wtab", hu], ["wm%d" % k])
         cp(third(T.wm, 0, H, TH), T.wtab[:].indirect(lst(T[hu], 0)), ["wtab", hu], ["wm0"])
-        if t == 0:
-            more_constants_3()
         counts(0, None)
         peel(0, hu, None)
+        if t == 0:
+            more_constants_4()
         cells()
         gap()
         if t == 0:

@@ -2,30 +2,34 @@ from concourse.mybir import dt, AluOpType as A, ActivationFunctionType as AF
 
 H, R = 160, 3
 TH, PL = 180, 176
-SA, SB = 19 * 53, 9 * 53
+SC, S0 = 576, 9 * 53
 BIG, M = float(2 ** 20), float(2 ** 16)
-U, BIG2, M2 = float(2 ** 20), float(2 ** 26), float(2 ** 24)
-TOP, HUGE, TINY = 2 ** 24 - 1, float(2 ** 60), float(2 ** -60)
+BIG2, M2 = 1024.0, 256.0
+U, HUGE, TINY = float(2 ** 20), float(2 ** 60), float(2 ** -60)
 MID = [27 * sum(64 ** e for e in range(d, 3)) for d in range(4)]
+WEIGH = [(U, U, U, 0.0)] + [(128.0, 3.0 * 4 ** (2 - p), -2.0 * 4 ** (2 - p), 0.0) for p in range(3)]
 F32, BF, I32, U16, QC, U8 = "float32", "bfloat16", "int32", "uint16", "float8_e4m3fn_x4", "uint8"
 
 SCRATCH = {"ps": ("psum", [128, 4096], F32)}
 for _d, _l in (
-    (BF, "xt 1280 ut 512 vt 512 rowg 128 ck 512 cv 512 ez 520 e1 520 wtab 64 lone 64 sg 512 wm 540 dec 540 cut 20 z60 60 wx 320 fl 640 "
-         "tw 704 tx 320 ga 960 v1 704 v2 640 et 704 e0 640 ft 640 xn 640"),
-    (F32, "hcf 4 pc 10 jrow 17 pw0 16 pw1 16 zr 16 pa1 16 pa2 16 pat4 16 pb1 16 pb2 16 pat16 16 d4 64 d16 160 cl 10 sp 10 "
-          "k64 48 crow 48 idrow 160 ks 48 hb 48 sa 1200 sb 570 tab 76 tab2 36 vs 160 r4 4 r6 6 th0 96 thr 96 dh 96 mm 96 sel 96 "
-          "pab 320 pabs 320 tq 640 yb 320 cg 480 cs 480 ot0 352 ot1 352 ot2 352"),
+    (BF, "xt 1280 ut 512 vt 512 rowg 128 same 128 ck 512 cv 2048 ez 520 e1 520 wtab 64 lone 64 sg 512 wm 540 dec 540 cut 20 "
+         "z60 60 wx 160 fl 640 d16 160 idrow 160 ot0 352 ot1 352 ot2 352 pab 320 pabs 320 cg 480 cs 480 "
+         "tw 704 tx 320 ga 640 v1 704 v2 640 et 704 e3 1920 o3 2048 m3 480 ft 640 xn 640"),
+    (F32, "hcf 4 pc 10 jrow 17 pw0 16 pw1 16 zr 16 pa1 16 pa2 16 pat4 16 d4 64 cl 10 sp 10 k64 48 crow 48 ks 48 hb 48 "
+          "sc 1728 mid 12 tab 120 vs 160 r4 4 r6 6 r7 6 th0 80 thr 80 dh 80 mm 80 sel 80 tq 640 yb 320"),
     (I32, "hci 4 pi 1 pci 4 yk 48 hd 48 dg 32"),
-    (U16, "opt 10 opm 10 oq 4 lk 4 lv 6 hu0 48 hu1 48 hu2 48 hu3 48 du 32 so0 34 so1 34 so2 34 lo0 34 lo1 34 lo2 34 pabu 20 cu 30"),
-    (QC, "qx 320 qu 128 qv 128 qw 512 qck 128 qcv 128 qe 512 q1 512 qs 128 qf 160 qg 160 qz 160 lq0 160 lq1 160 lq2 160"),
-    (U8, "sx 320 su 128 sv 128 sw 512 sck 128 scv 128 se 512 s1 512 ss 128 sf 160 sq 160 sz 160 ls0 160 ls1 160 ls2 160"),
+    (U16, "opt 10 opm 10 oq 4 lk 4 lv 6 hu0 48 hu1 48 hu2 48 hu3 48 du 32 so0 30 so1 30 so2 30 lo0 30 lo1 30 lo2 30 pabu 40 cu 30"),
+    (QC, "qx 320 qu 128 qv 128 qw 512 qck 128 qcv 512 qe 512 q1 512 qs 128 qf 160 qg 160 qz 160 lq0 160 lq1 160 lq2 160"),
+    (U8, "sx 320 su 128 sv 128 sw 512 sck 128 scv 512 se 512 s1 512 ss 128 sf 160 sq 160 sz 160 ls0 160 ls1 160 ls2 160"),
 ):
     _w = _l.split()
     for _i in range(0, len(_w), 2):
         SCRATCH[_w[_i]] = ("sbuf", [128, int(_w[_i + 1])], _d)
 
-POOL = {"V": 40, "A": 20, "P": 16, "G": 24}
+TABLE = "a00 t02 b00 t03 a01 v02 b01 v03 s00 a12 t13 a10 s01 v13 b10 p12 a11 s10 p11 c10 v12 v11"
+READ = "c0 C1 C2 g0 G1 c3 G2 t0 K0 t1 K1 f0 f1 K2 t2 s3 f2 o3"
+
+POOL = {"V": 40, "A": 24, "P": 16, "G": 24}
 NDMA = 16
 SEMAPHORES = ([q + "%d" % i for q in POOL for i in range(POOL[q])] + ["D%d" % i for i in range(NDMA)]
               + [s + "%d" % t for t in range(R) for s in ("ro", "rq", "so", "sq")])
@@ -161,9 +165,11 @@ def rank_program(g, core, T, topo):
     def half(h):
         return T.qx[:, H * h:H * h + H], T.sx[:, H * h:H * h + H]
 
-    def eb(b, unit):
-        c, s = (T.q1, T.s1) if unit else (T.qe, T.se)
+    def part(c, s, b):
         return c[:, 128 * b:128 * b + 128], s[:, 128 * b:128 * b + 128]
+
+    def eb(b, unit):
+        return part(T.q1, T.s1, b) if unit else part(T.qe, T.se, b)
 
     def third(buf, k, w=H, step=H):
         return buf[:, step * k:step * k + w]
@@ -173,9 +179,9 @@ def rank_program(g, core, T, topo):
 
     PM, PG, PT, PA, C16, A16 = [T.pc[:, j:j + 1] for j in range(6)]
 
+    dma("S", T.ut[:], T.u[:], (), ["ut"])
     dma("S", T.xt[:, 0:640], T.x[:, 0:640], (), ["xt0"])
-    dma("A", T.ut[:], T.u[:], (), ["ut"])
-    dma("S", T.hci[:, 0:3], T.hc[:], (), ["hci"])
+    dma("A", T.hci[:, 0:3], T.hc[:], (), ["hci"])
     dma("S", T.xt[:, 640:1280], T.x[:, 640:1280], (), ["xt1"])
     j = dma("S", T.qw[:].bitcast(dt.uint8), T.wc[:], (), ["qw"])
     dma("S", T.sw[:], T.ws[:], (), ["sw"], join=j)
@@ -187,36 +193,39 @@ def rank_program(g, core, T, topo):
     fill(T.sg[:, H:512], 512 - H, 0, ["sgz"])
     iota(T.r4[:], [[9, 4]], 8, 0, ["r4"])
     fill(T.z60[:], 60, 0, ["z60"])
-    j = fill(T.sa[:, SA:SA + 190:2], 95, 0, ["scz"])
-    fill(T.sb[:, SB:SB + 90:2], 45, 0, (), j)
+    j = None
+    for k in range(3):
+        j = fill(T.sc[:, SC * k + S0:SC * k + S0 + 90:2], 45, 0, ["scz"], j)
+    j = None
+    for d in range(4):
+        j = fill(T.mid[:, 3 * d:3 * d + 3], 3, MID[d], ["mid"], j)
 
     def centre():
-        j = None
-        need("G", ["scz"], ())
-        for d in range(4):
-            j = fill(T.sa[:, SA + 38 * d + 4:SA + 38 * d + 36:6], 6, MID[d], ["saB", "sbB"] * (d == 0), j)
-            fill(T.sb[:, SB + 18 * d + 4:SB + 18 * d + 18:6], 3, MID[d], (), j)
+        for k in range(3):
+            act(T.sc[:, SC * k + S0 + 4:SC * k + S0 + 72:6], T.mid[:], ["mid", "scz"], ["scB%d" % k])
 
     def peel_fills():
-        j = fill(T.fl[:, 3:640:4], H, 0, ["flz"])
+        fill(T.fl[:, 3:640:4], H, 0, ["flz"])
         j = iota(T.cl[:], [[16, 10]], 192, 0, ["cl"])
         iota(T.k64[:], [[64, 3], [0, 16]], 0, 0, ["k64"], join=j)
         fill(T.ez[:], 520, 64, ["ez"])
-        fill(T.dh[:], 96, 0, ["dhz"])
+        iota(T.r6[:], [[64, 6]], 15, 0, ["r6"])
         op("G", lambda: g.affine_select(T.ez[:], T.ez[:], [[-1, 520]], A.is_equal, 0.0, 3, 4), ["ez"], ["ez"])
 
     def late_fills():
-        fill(T.th0[:], 96, TOP, ["th0"])
-        iota(T.r6[:], [[0, 2], [64, 3]], 15, 0, ["r6"])
         j = None
-        for at, cnt, c in ((slice(1, 96, 4), 24, 4), (slice(2, 48, 4), 12, 2), (slice(51, 96, 4), 12, 2), (slice(3, 48, 4), 12, 1)):
-            need("G", (), ["th0"])
-            j = fill(T.th0[:, at], cnt, c * int(U), ["th1"], j)
+        for at, c in ((slice(0, 80, 4), 1000), (slice(1, 80, 4), 64), (slice(2, 40, 4), 1), (slice(42, 80, 4), 1000), (slice(3, 80, 4), 0)):
+            j = fill(T.th0[:, at], len(range(80)[at]), c, ["th0"], j)
         j = iota(T.idrow[:], [[1, H]], 0, 0, ["idrow"])
         for b in ("tw", "v1", "et"):
             fill(T[b][:, H:4 * PL:PL], 4, 0, [b + "z"], j)
-        for t in range(R):
-            fill(T["ot%d" % t][:, 0:192], 192, H, ["ot%d" % t], j)
+        fill(T.o3[:, 496:2048:512], 4, 0, ["o3z"], j)
+        fill(T.ot0[:, 0:192], 192, H, ["ot0"], j)
+        j = fill(T.m3[:, 0:480:3], H, 0, ["m3"])
+        for e in (1, 2):
+            fill(T.m3[:, e:480:3], H, 1, (), j)
+        for t in (1, 2):
+            fill(T["ot%d" % t][:, 0:192], 192, H, ["ot%d" % t])
 
     j = ms(T.ck[:], 0.0, ["ck"])
     ms(T.zr[:], 0.0, ["zr"], j)
@@ -241,12 +250,17 @@ def rank_program(g, core, T, topo):
     ts(T.opt[:], T.rowg[:, 0:10], 0.0, PT, A.mult, A.add, ["rowg", "pc"], ["opt"], j2)
     scan(T.pw1[:], T.pw0[:], T.zr[:], 0.5, A.mult, A.add, ["pw0", "zr"], ["pw1"])
     ts(T.opm[:], T.rowg[:, 0:10], 0.0, PM, A.mult, A.add, ["rowg", "pc"], ["opm"])
+    ts(T.same[:], T.rowg[:], PG, None, A.is_equal, None, ["rowg", "pc"], ["same"])
     tt(T.pat4[:], T.pa1[:], T.pa2[:], A.add, ["pa1", "pa2"], ["pat4"])
     act(T.d4[:], T.pat4[:].indirect(T.opt[:, 0:4]), ["pat4", "opt"], ["d4"])
+    for i in range(4):
+        j = None
+        for t in range(4):
+            j = act(T.cv[:, 512 * i + t:512 * i + 512:4], T.same[:], ["same"], ["cv%d" % i], scale=WEIGH[i][t], join=j)
     qz(T.qu[:], T.su[:], T.ut[:], ["ut"], ["qu"])
     qz(half(0)[0], half(0)[1], T.xt[:, 0:640], ["xt0"], ["qx0"])
 
-    def more_constants_0():
+    def key_tile():
         j = None
         for t in range(4):
             j = ts(T.ck[:, 5 * t:512:16], T.rowg[:, t:128:4], PG, T.pw1[:, 15:16], A.is_equal, A.mult,
@@ -255,53 +269,51 @@ def rank_program(g, core, T, topo):
         ts(T.lk[:], T.opm[:, 0:4], 9.0, 4.0, A.min, A.mult, ["opm"], ["lk"], j)
         qz(T.qck[:], T.sck[:], T.ck[:], ["ck0"], ["qck"])
 
-    def more_constants_1():
+    def digits():
         j = None
         for d in range(4):
             j = ts(T.wtab[:, 16 * d:16 * d + 16], T.jrow[:, 1:17], PM, float(64 ** d), A.is_equal, A.mult,
                    ["jrow", "pc"], ["wtab%d" % d], j)
 
-    def more_constants_2():
+    def address_rows():
         ts(T.wtab[:], T.wtab[:], TINY, None, A.max, None, ["wtab0"], ["wtab"])
         j = None
         for k in range(3):
             j = ts(T.crow[:, 16 * k:16 * k + 16], T.zr[:], T.hcf[:, k:k + 1], None, A.add, None, ["zr", "hcf"], ["crow%d" % k], j)
         j = cp(T.oq[:], T.r4[:], ["r4"], ["oq"])
         need("V", ["scz"], ())
-        for at in (T.sa[:, SA:SA + 190:38], T.sa[:, SA + 18:SA + 190:38], T.sb[:, SB:SB + 90:18]):
-            j = ms(at, HUGE, ["sch"], j)
+        for k in range(3):
+            j = ms(T.sc[:, SC * k + S0:SC * k + S0 + 90:18], HUGE, ["sch"], j)
 
-    def more_constants_3():
-        j = None
-        for t in range(4):
-            j = ts(T.cv[:, t:512:4], T.rowg[:], PG, (4 >> t) * U, A.is_equal, A.mult, ["rowg", "pc"], ["cv%d" % t], j)
+    def flag_tile(i):
+        qz(part(T.qcv, T.scv, i)[0], part(T.qcv, T.scv, i)[1], T.cv[:, 512 * i:512 * i + 512], ["cv%d" % i], ["qcv%d" % i])
 
-    def more_constants_4():
-        j = ts(T.pb1[:], T.jrow[:, 1:17], PM, BIG2, A.is_equal, A.mult, ["jrow", "pc"], ["pb1"])
-        ts(T.pb2[:], T.jrow[:, 0:16], PM, -M2, A.is_equal, A.mult, ["jrow", "pc"], ["pb2"], j)
+    def owner_rows(step):
+        if step == 0:
+            j = ts(T.pa1[:], T.jrow[:, 1:17], PM, BIG2, A.is_equal, A.mult, ["jrow", "pc"], ["pa1"])
+            ts(T.pa2[:], T.jrow[:, 0:16], PM, -M2, A.is_equal, A.mult, ["jrow", "pc"], ["pa2"], j)
+        elif step == 1:
+            j = ts(T.sp[:], T.cl[:], PM, None, A.add, None, ["cl", "pc"], ["sp"])
+            ts(C16, PM, 15.0, M2, A.is_lt, A.mult, ["pc"], ["c16"], j)
+            ts(A16, PA, 16.0, None, A.mult, None, ["pc"], ["a16"], j)
+            tt(T.pat4[:], T.pa1[:], T.pa2[:], A.add, ["pa1", "pa2"], ["pat4"])
+            act(T.d16[:], T.pat4[:].indirect(T.opm[:]), ["pat4", "opm"], ["d16"])
+        elif step == 2:
+            ts(T.r7[:], T.r6[:], A16, 160.0, A.add, A.is_ge, ["r6", "a16"], ["r7"])
+        elif step == 3:
+            ts(T.r7[:], T.r7[:], -160.0, A16, A.mult, A.add, ["r7", "a16"], ["r7"])
+        elif step == 4:
+            tt(T.r7[:], T.r7[:], T.r6[:], A.add, ["r7", "r6"], ["r7"])
+        else:
+            j = cp(T.lv[:], T.r7[:], ["r7"], ["lv"])
+            ts(T.thr[:], T.th0[:], C16, None, A.subtract, None, ["th0", "c16"], ["thr"], j)
 
-    def more_constants_5():
-        qz(T.qcv[:], T.scv[:], T.cv[:], ["cv0"], ["qcv"])
-
-    def more_constants_6():
-        j = ts(T.sp[:], T.cl[:], PM, None, A.add, None, ["cl", "pc"], ["sp"])
-        ts(C16, PM, 15.0, M2, A.is_lt, A.mult, ["pc"], ["c16"], j)
-        ts(A16, PA, 16.0, None, A.mult, None, ["pc"], ["a16"], j)
-        tt(T.pat16[:], T.pb1[:], T.pb2[:], A.add, ["pb1", "pb2"], ["pat16"])
-        act(T.d16[:], T.pat16[:].indirect(T.opm[:]), ["pat16", "opm"], ["d16"])
-
-    def more_constants_7():
-        j = ts(T.lv[:], T.r6[:], A16, 159.0, A.add, A.min, ["r6", "a16"], ["lv"])
-        ts(T.thr[:], T.th0[:], C16, None, A.subtract, None, ["th0", "th1", "c16"], ["thr"], j)
-        cp(T.dh[:, 3:40:4], T.sp[:], ["sp", "dhz"], ["dh3"], j)
-
-    def units(bs, unit):
-        j = None
+    def units(b, unit):
         src, key = (T.e1, "e1") if unit else (T.ez, "ez")
-        for b in bs:
-            j = qz(eb(b, unit)[0], eb(b, unit)[1], src[:, 3 - b:515 - b], [key], ["q%s%d" % (key, b)], j)
+        qz(eb(b, unit)[0], eb(b, unit)[1], src[:, 3 - b:515 - b], [key], ["q%s%d" % (key, b)])
 
-    DH = ["dh%d" % i for i in range(8)]
+    DH = ["dh0", "dh1"]
+    WM = [["wm0", "wm3"], ["wm1"], ["wm2", "wm4"]]
 
     def scores(h, b):
         mx(b, T.qu[:], T.su[:], half(h)[0], half(h)[1], ["qu", "qx%d" % h])
@@ -325,18 +337,21 @@ def rank_program(g, core, T, topo):
             step()
         ts(T.dg[:], T.yk[:, 0:32], 12, 3, A.logical_shift_right, A.bitwise_and, ["yk"], ["dg"])
         steps[3]()
-        j = None
-        for k in range(2):
-            j = ts(T.du[:, 16 * k:16 * k + 16], T.dg[:, 16 * k:16 * k + 16], 19.0, 9.0 * k + 8, A.mult, A.add, ["dg"], ["du%d" % k], j)
+        gap()
+        ts(T.du[:], T.dg[:], 9.0, 8.0, A.mult, A.add, ["dg"], ["du"])
+
+    def writers_digits(hu):
+        for f, k, a, b, key in ((cp, 2, 0, 6, "wm2"), (act, 2, 6, 10, "wm4"), (cp, 0, 0, 6, "wm0"), (act, 0, 6, 10, "wm3"), (act, 1, 0, 10, "wm1")):
+            f(T.wm[:, TH * k + 16 * a:TH * k + 16 * b], T.wtab[:].indirect(T[hu][:, 16 * k + a:16 * k + b]), ["wtab", hu], [key])
 
     def first_readers():
         qz(half(1)[0], half(1)[1], T.xt[:, 640:1280], ["xt1"], ["qx1"])
         scores(1, 3)
 
     ra = addresses(3, "hu3")
-    un = [lambda b=b, u=u: units((b,), u) for u in (True, False) for b in range(4)]
-    spare = [more_constants_3, first_readers, more_constants_5, lambda: signs(3), lambda: keys(3),
-             ra[0], ra[1], ra[2], un[0], ra[3]] + un[1:]
+    un = [lambda b=b, u=u: units(b, u) for u in (True, False) for b in range(4)]
+    ft = [lambda i=i: flag_tile(i) for i in range(4)]
+    spare = [ft[0], ft[1], first_readers, lambda: signs(3), lambda: keys(3), ft[2], ra[0], ft[3]] + un[0:4] + [ra[1], ra[2]] + un[4:6] + [ra[3]] + un[6:8]
 
     def gap(n=1):
         for i in range(min(n, len(spare))):
@@ -351,8 +366,22 @@ def rank_program(g, core, T, topo):
         decode(4, range(4), T["lq%d" % t][:], T["ls%d" % t][:], "lq%d" % t, True)
         for b in range(4):
             act(third(T.tw, b, H, PL), bank(4 + b), ["B%d" % (4 + b)], ["tw%d" % b])
-        for b in range(2):
-            act(third(T.tx, b), bank(4 + b), ["B%d" % (4 + b)], ["tx%d" % b])
+
+    def writers_copies():
+        for b in (2, 3):
+            act(third(T.tx, b - 2), bank(4 + b), ["B%d" % (4 + b)], ["tx%d" % b])
+        for i, b, c in ((0, 0, -1.0), (1, 1, -1.0), (2, 0, 1.0)):
+            act(term(i, 0), bank(4 + b), ["B%d" % (4 + b)], ["e3%d0" % i], scale=c)
+
+    def term(i, k):
+        return T.e3[:, 480 * i + k:480 * i + 480:3]
+
+    def add3(i):
+        scan(T.o3[:, 512 * i + 14:512 * i + 494], T.m3[:], T.e3[:, 480 * i:480 * i + 480], 0.0, A.mult, A.add,
+             ["m3"] + ["e3%d%d" % (i, k) for k in range(3)], ["o3%d" % i])
+
+    def sums(i):
+        return T.o3[:, 512 * i + 16:512 * i + 496:3]
 
     def cells():
         tt(T.hb[:], T.hd[:], T.k64[:], A.add, ["hd", "k64"], ["hb"])
@@ -360,44 +389,54 @@ def rank_program(g, core, T, topo):
     def choices():
         h = [lst(T.hb, k) for k in range(3)]
         j = None
-        for i, at, x, y in ((0, 0, h[0], h[1]), (1, 1, h[1], h[2]), (2, 2, h[2], T.sp[:]), (4, 48, h[1], h[0]), (6, 50, h[2], h[1])):
-            j = tt(T.dh[:, at:at + 40:4], x, y, A.subtract, ["hb", "sp", "dhz"], [DH[i]], j)
-        for i, at, x in ((5, 49, h[0]), (7, 51, h[1])):
-            j = cp(T.dh[:, at:at + 40:4], x, ["hb", "dhz"], [DH[i]], j)
+        for at, x, y in ((0, h[0], h[1]), (1, h[1], T.sp[:]), (2, T.sp[:], h[2]), (40, h[1], h[0]), (42, h[2], h[1])):
+            j = tt(T.dh[:, at:at + 37:4], x, y, A.subtract, ["hb", "sp"], ["dh0"], j)
+        j = None
+        for at, x in ((3, h[2]), (41, h[0]), (43, h[1])):
+            j = act(T.dh[:, at:at + 37:4], x, ["hb"], ["dh1"], join=j)
 
     def counts(p, b):
         src = "dec" if p else "wm"
         if p:
-            for k in (2, 0, 1):
-                tt(third(T.dec, k, H, TH), third(T.wm, k, H, TH), bank(b), A.min, ["wm%d" % k, "B%d" % b], ["dec%d" % k])
-        j = {}
-        for k in (2, 0, 1):
-            buf, s = ("sb", 9) if k == 2 else ("sa", 19)
+            for k in (2, 1, 0):
+                tt(third(T.dec, k, H, TH), third(T.wm, k, H, TH), bank(b), A.min, WM[k] + ["B%d" % b], ["dec%d" % k])
+        for k in ((2, 1, 0) if p else (2, 0, 1)):
+            j = None
+            if k == 1 and not p:
+                totals(2)
             for c in range(3):
-                at = 2 * (9 * (k % 2) + 3 * c + (2 if p else 1))
-                j[buf] = scan(T[buf][:, at:at + s * 59 + 1:s], T.z60[:], T[src][:, TH * k + c:TH * k + TH:3], float(MID[0] if p else -MID[0]),
-                              A.add, A.subtract if p else A.add, ["z60", src + "%d" % k, src + "z", "scz"], [buf + ("B" if p else "A")], j.get(buf))
+                at = SC * k + 2 * (3 * c + (2 if p else 1))
+                j = scan(T.sc[:, at:at + 9 * 59 + 1:9], T.z60[:], T[src][:, TH * k + c:TH * k + TH:3], float(MID[0] if p else -MID[0]),
+                         A.add, A.subtract if p else A.add, ["z60", src + "z", "scz"] + (["dec%d" % k] if p else WM[k]),
+                         ["sc%s%d" % ("B" if p else "A", k)], j)
 
-    def left(k, b):
-        tt(third(T.wx, k), third(T.wm, k, H, TH), bank(b), A.subtract, ["wm%d" % k, "B%d" % b], ["wx%d" % k])
+    def totals(k):
+        at = SC * k + S0
+        scan(third(T.tab, k, 36, 40), T.sc[:, at:at + 72:2], T.sc[:, at + 18:at + 90:2], 0.0, A.add, A.subtract,
+             ["sch", "scA%d" % k, "scB%d" % k], ["tab%d" % k])
 
     def peel(p, hu, b):
-        scan(T.tab2[:], T.sb[:, SB:SB + 72:2], T.sb[:, SB + 18:SB + 90:2], 0.0, A.add, A.subtract, ["sch", "sbA", "sbB"], ["tab2"])
-        left(0, b) if p else gap()
-        scan(T.tab[:], T.sa[:, SA:SA + 152:2], T.sa[:, SA + 38:SA + 190:2], 0.0, A.add, A.subtract, ["sch", "saA", "saB"], ["tab"])
-        tt(T.lone[:], T.tab2[:].indirect(T.oq[:]), T.wtab[:], A.is_equal, ["tab2", "oq", "wtab"], ["lone"])
+        order = (1, 0) if p else (0, 1)
         if p:
-            left(1, b)
+            totals(2)
+        totals(order[0])
+        if p:
+            tt(T.wx[:], third(T.wm, 0, H, TH), bank(b), A.subtract, WM[0] + ["B%d" % b], ["wx"])
+            totals(0)
+        tt(T.lone[:], third(T.tab, 2, 36, 40).indirect(T.oq[:]), T.wtab[:], A.is_equal, ["tab2", "oq", "wtab"], ["lone"])
+        if not p:
+            totals(1)
         act(T.fl[:, 2:640:4], T.lone[:].indirect(lst(T[hu], 2)), ["lone", hu], ["fl2"])
         j = None
-        for k in range(2):
-            x, xk = (third(T.wx, k), "wx%d" % k) if p else (third(T.wm, k, H, TH), "wm%d" % k)
-            j = tt(T.fl[:, k:640:4], T.tab[:].indirect(lst(T.du, k)), x, A.is_equal, ["tab", "du0", xk], ["fl%d" % k], j)
+        for k in order:
+            x, xk = (T.wx[:], ["wx"]) if p and k == 0 else (third(T.wm, k, H, TH), WM[k])
+            j = tt(T.fl[:, k:640:4], third(T.tab, k, 36, 40).indirect(lst(T.du, k)), x, A.is_equal, ["tab%d" % k, "du"] + xk, ["fl%d" % k], j)
         gap()
         qz(T.qf[:], T.sf[:], T.fl[:], ["fl0", "fl1", "fl2", "flz"], ["qf"])
         for i, bk in enumerate((1, 0, 2)):
             if i >= p:
-                mx(bk, T.qcv[:], T.scv[:], T.qf[:], T.sf[:], ["qcv", "qf"], start=p == 0, stop=p == i)
+                c = p + 1 if i == 2 else 0
+                mx(bk, part(T.qcv, T.scv, c)[0], part(T.qcv, T.scv, c)[1], T.qf[:], T.sf[:], ["qcv%d" % c, "qf"], start=p == 0, stop=p == i)
 
     def store(h, qs):
         lo = H * h
@@ -414,115 +453,117 @@ def rank_program(g, core, T, topo):
         ot, so, lo = T["ot%d" % t], T["so%d" % t], T["lo%d" % t]
         scores(w, 0)
         if t == 0:
-            centre()
             peel_fills()
         send([(T["lq%d" % t][:].bitcast(dt.uint8), half(w)[0].bitcast(dt.uint8)), (T["ls%d" % t][:], half(w)[1])],
              "rq%d" % t, "sq%d" % t, ["qx%d" % w])
         if t == 0:
             late_fills()
-            more_constants_0()
-        else:
-            centre()
+            key_tile()
+        centre()
         signs(0)
         if t == 0:
-            more_constants_1()
+            digits()
         keys(1)
         if t == 0:
-            more_constants_2()
+            address_rows()
         if t == 2:
             store(0, "SSSSS")
             mx(3, T.qv[:], T.sv[:], half(0)[0], half(0)[1], ["qv", "qx0"])
         writers_addresses(1, hu)
-        for k in (2, 1):
-            act(third(T.wm, k, H, TH), T.wtab[:].indirect(lst(T[hu], k)), ["wtab", hu], ["wm%d" % k])
-        cp(third(T.wm, 0, H, TH), T.wtab[:].indirect(lst(T[hu], 0)), ["wtab", hu], ["wm0"])
+        writers_digits(hu)
         counts(0, None)
         peel(0, hu, None)
         if t == 0:
-            more_constants_4()
+            owner_rows(0)
         cells()
         gap()
         if t == 0:
-            more_constants_6()
-        counts(1, 1)
-        peel(1, hu, 1)
-        choices()
-        gap()
-        if t == 0:
-            act(T.e1[:], T.ez[:], ["ez"], ["e1"], scale=0.015625)
+            owner_rows(1)
         else:
             writers_numbers(t)
+        counts(1, 1)
+        peel(1, hu, 1)
+        if t == 0:
+            owner_rows(2)
+        choices()
+        if t == 0:
+            owner_rows(3)
+            act(T.e1[:], T.ez[:], ["ez"], ["e1"], scale=0.015625)
+        else:
+            writers_copies()
+        gap()
         counts(2, 0)
         peel(2, hu, 0)
+        if t == 0:
+            owner_rows(4)
         gap(2)
         if t == 0:
-            more_constants_7()
+            owner_rows(5)
         if t == 2:
             act(T.yb[:, 0:H], bank(3), ["B3"], ["yb0"])
             dma("S", T.y[:, 0:H], T.yb[:, 0:H], ["yb0"], ())
         scan(T.vs[:], T.d16[:], bank(2), 0.0, A.add, A.min, ["d16", "B2"], ["vs"])
         gap()
-        tt(T.mm[:], T.vs[:].indirect(T.lv[:]), T.thr[:], A.is_ge, ["vs", "lv", "thr"], ["mm"])
+        tt(T.mm[:], T.vs[:].indirect(T.lv[:, 0:5]), T.thr[:], A.is_ge, ["vs", "lv", "thr"], ["mm"])
         gap()
-        scan(T.sel[:], T.mm[:], T.dh[:], 0.0, A.mult, A.add, ["mm", "dhz"] + DH, ["sel"])
+        scan(T.sel[:], T.mm[:], T.dh[:], 0.0, A.mult, A.add, ["mm"] + DH, ["sel"])
         gap()
-        j = cp(so[:, 0:24], T.sel[:, 3:96:4], ["sel"], ["so%d" % t])
-        cp(so[:, 24:34], T.sel[:, 49:89:4], ["sel"], ["sa%d" % t], j)
-        send([(lo[:], so[:])], "ro%d" % t, "so%d" % t, ["so%d" % t, "sa%d" % t])
+        j = cp(so[:, 0:20], T.sel[:, 3:80:4], ["sel"], ["so%d" % t])
+        cp(so[:, 20:30], T.sel[:, 41:80:4], ["sel"], (), j)
+        send([(lo[:], so[:])], "ro%d" % t, "so%d" % t, ["so%d" % t])
         if t == 0:
-            gap(len(spare))
             writers_numbers(0)
+            writers_copies()
+            gap(len(spare))
         if t == 1:
             qz(T.qv[:], T.sv[:], T.vt[:], ["vt"], ["qv"])
         okey, lkey = "ot%d" % t, "lo%d" % t
         event("ro%d" % t, nin, (), [lkey])
         cp(ot[:].indirect(lo[:, 0:10]), T.idrow[:], [lkey, "idrow"], [okey])
-        act(third(T.pab, 1), ot[:, 0:192].indirect(lo[:, 12:22]), [okey, lkey], ["pab1"])
-        cp(third(T.pab, 0), ot[:, 0:192].indirect(lo[:, 24:34]), [okey, lkey], ["pab0"])
-        for k in range(3):
-            act(third(T.cg, k), ot[:, 64 * k:64 * k + 64].indirect(lst(T[hr], k)), [okey, hr], ["cg%d" % k])
-        for i in range(2):
-            scan(third(T.pabs, i), T.d16[:], third(T.pab, i), 0.0, A.add, A.min, ["d16", "pab%d" % i], ["pabs%d" % i])
+        for f, i, a, b, key in ((cp, 0, 0, 6, "pab0"), (act, 0, 6, 10, "pab2"), (cp, 1, 0, 4, "pab1"), (act, 1, 4, 10, "pab3")):
+            at = 20 - 10 * i
+            f(T.pab[:, H * i + 16 * a:H * i + 16 * b], ot[:, 0:192].indirect(lo[:, at + a:at + b]), [okey, lkey], [key])
 
-        def places(i):
-            ts(T.pabu[:, 10 * i:10 * i + 10], T.pabs[:, H * i + 15:H * i + H:16], C16, None, A.add, None, ["pabs%d" % i, "c16"], ["pabu%d" % i])
+        def asked(k):
+            act(third(T.cg, k), ot[:, 64 * k:64 * k + 64].indirect(lst(T[hr], k)), [okey, hr], ["cg%d" % k])
 
         def compose(k):
             scan(third(T.cs, k), T.d16[:], third(T.cg, k), 0.0, A.add, A.min, ["d16", "cg%d" % k], ["cs%d" % k])
 
-        pa, pb = T.pabu[:, 0:10], T.pabu[:, 10:20]
+        asked(0)
+        asked(1)
+        for i in range(2):
+            scan(third(T.pabs, i), T.d16[:], third(T.pab, i), 0.0, A.add, A.min, ["d16", "pab%d" % i, "pab%d" % (i + 2)], ["pabs%d" % i])
+        for i in range(2):
+            ts(T.pabu[:, 10 * i:10 * i + 10], T.pabs[:, H * i + 15:H * i + H:16], C16, None, A.add, None, ["pabs%d" % i, "c16"], ["pabu%d" % i])
+        ts(T.pabu[:, 20:40], T.pabs[:, 15:320:16], C16, 3.0, A.add, A.mult, ["pabs0", "pabs1", "c16"], ["pabu2"])
 
-        def window(s, b):
-            return third(T["v1" if s else "tw"], b, H + 1, PL), [("v1" if s else "tw") + c for c in ("z", "%d" % b)]
+        def cell(s, b, i):
+            if s and b < 2:
+                return T.o3[:, 512 * b + 16:512 * b + 497].indirect(T.pabu[:, 20 + 10 * i:30 + 10 * i]), ["o3z", "o3%d" % b, "pabu2"]
+            buf = "v1" if s else "tw"
+            return third(T[buf], b, H + 1, PL).indirect(T.pabu[:, 10 * i:10 * i + 10]), [buf + "z", buf + "%d" % b, "pabu%d" % i]
 
-        def fetch(s, b):
-            act(third(T.ga, 4 * s + b - 2), window(s, b)[0].indirect(pa), window(s, b)[1] + ["pabu0"], ["ga%d%d" % (s, b)])
-
-        def one(s, b):
-            if s == 0 and b < 2:
-                tt(third(T.tq, b), window(s, b)[0].indirect(pa), third(T.tx, b), A.subtract, window(s, b)[1] + ["pabu0", "tx%d" % b], ["tq%d" % b])
+        for what, s, b in [(x[0], int(x[1]), int(x[2])) for x in TABLE.split()]:
+            x, xk = cell(s, b, 1 if what in "bv" else 0)
+            i = 2 * s + b
+            if what in "ab" and (b == 0 or s == 0):
+                act(term(i, 1 + "ab".index(what)), x, xk, ["e3%d%d" % (i, 1 + "ab".index(what))])
+            elif what == "a":
+                act(third(T.ga, b), x, xk, ["ga%d" % b])
+            elif what == "s":
+                add3(i)
+            elif what == "c":
+                act(T.v2[:, b:640:4], sums(i), ["o3%d" % i], ["v2%d" % b])
+            elif what == "p":
+                tt(third(T.tq, b), third(T.ga, b), bank(4 + b), A.add, ["ga%d" % b, "B%d" % (4 + b)], ["tq%d" % b])
+            elif what == "t":
+                tt(third(T.tq, b), x, third(T.tx, b - 2), A.add if s else A.subtract, xk + ["tx%d" % b], ["tq%d" % b])
             else:
-                tt(third(T.tq, b), third(T.ga, 4 * s + b - 2), bank(4 + b), A.add if s else A.subtract,
-                   ["ga%d%d" % (s, b), "B%d" % (4 + b)], ["tq%d" % b])
-
-        def two(s, b):
-            out = T.v2[:, b:640:4] if s else third(T.v1, b, H, PL)
-            tt(out, window(s, b)[0].indirect(pb), third(T.tq, b), A.add, window(s, b)[1] + ["pabu1", "tq%d" % b], ["v%d%d" % (s + 1, b)])
-            if s == 0:
-                fetch(1, b)
-
-        places(0)
+                tt(T.v2[:, b:640:4] if s else third(T.v1, b, H, PL), x, third(T.tq, b), A.add, xk + ["tq%d" % b], ["v%d%d" % (s + 1, b)])
+        asked(2)
+        decode(4, (0, 3, 2, 1), half(o)[0], half(o)[1], "qx%d" % o, False, False)
         compose(0)
-        places(1)
-        fetch(0, 2)
-        fetch(0, 3)
-        todo = [(s, b) for s in range(2) for b in range(4)]
-        one(0, 0)
-        for i in range(8):
-            if i < 7:
-                one(*todo[i + 1])
-            two(*todo[i])
-        decode(4, range(4), half(o)[0], half(o)[1], "qx%d" % o, False, False)
         compose(1)
         qz(T.qz[:], T.sz[:], T.v2[:], ["v20", "v21", "v22", "v23"], ["qz"])
         decode(0, range(4), T.qz[:], T.sz[:], "qz", True)
@@ -532,16 +573,21 @@ def rank_program(g, core, T, topo):
         def read(k, b):
             return third(T.et, b, H + 1, PL).indirect(T.cu[:, 10 * k:10 * k + 10]), ["etz", "et%d" % b, "cu"]
 
-        for b in range(4):
-            (act if b == 1 else cp)(third(T.et, b, H, PL), bank(b), ["B%d" % b], ["et%d" % b])
-        for b in range(4):
-            act(third(T.e0, b), read(0, b)[0], read(0, b)[1], ["e0%d" % b])
-        j = None
-        for k, b in ((1, 0), (1, 1), (2, 0), (1, 2), (2, 1), (1, 3), (2, 2), (2, 3)):
-            if k == 1:
-                tt(third(T.tq, b), read(1, b)[0], third(T.e0, b), A.add, read(1, b)[1] + ["e0%d" % b], ["tq%d" % b])
+        for what, b in [(x[0], int(x[1])) for x in READ.split()]:
+            if what in "cC":
+                (cp if what == "c" else act)(third(T.et, b, H, PL), bank(b), ["B%d" % b], ["et%d" % b])
+            elif what in "gG":
+                (cp if what == "g" else act)(third(T.ga, b), read(0, b)[0], read(0, b)[1], ["ga%d" % b])
+            elif what == "t":
+                tt(third(T.tq, b), read(1, b)[0], third(T.ga, b), A.add, read(1, b)[1] + ["ga%d" % b], ["tq%d" % b])
+            elif what == "f":
+                tt(T.ft[:, b:640:4], read(2, b)[0], third(T.tq, b), A.add, read(2, b)[1] + ["tq%d" % b], ["ft%d" % b])
+            elif what == "K":
+                act(term(3, b), read(b, 3)[0], read(b, 3)[1], ["e33%d" % b])
+            elif what == "s":
+                add3(3)
             else:
-                j = tt(T.ft[:, b:640:4], read(2, b)[0], third(T.tq, b), A.add, read(2, b)[1] + ["tq%d" % b], ["ft%d" % b], j)
+                cp(T.ft[:, 3:640:4], sums(3), ["o33"], ["ft3"])
         qz(T.qg[:], T.sq[:], T.ft[:], ["ft0", "ft1", "ft2", "ft3"], ["qg"])
         for b in (2, 0, 3, 1):
             mx(4 + b, T.qw[:, 128 * b:128 * b + 128], T.sw[:, 128 * b:128 * b + 128], T.qg[:], T.sq[:], ["qw", "sw", "qg"], start=False)

@@ -1,33 +1,37 @@
 from concourse.mybir import dt, AluOpType as A, ActivationFunctionType as AF
 
 H, R = 160, 3
-TH, PL = 180, 176
-SC, S0 = 576, 9 * 53
+TH = 180
+SC, S0 = 448, 7 * 53
 BIG, M = float(2 ** 20), float(2 ** 16)
 BIG2, M2 = 1024.0, 256.0
-U, HUGE, TINY = float(2 ** 20), float(2 ** 60), float(2 ** -60)
-MID = [27 * sum(64 ** e for e in range(d, 3)) for d in range(4)]
-WEIGH = [(U, U, U, 0.0)] + [(128.0, 3.0 * 4 ** (2 - p), -2.0 * 4 ** (2 - p), 0.0) for p in range(3)]
+U, HUGE, TINY = float(13 * 2 ** 16), float(2 ** 60), float(2 ** -60)
+SMALL = 0.015625
+MID = [27 * sum(64 ** e for e in range(d, 4)) for d in range(4)]
+WEIGH = [(U, U, U, 0.0), (4.0, 2.0, 1.0, 0.0)]
 F32, BF, I32, U16, QC, U8 = "float32", "bfloat16", "int32", "uint16", "float8_e4m3fn_x4", "uint8"
 
 SCRATCH = {"ps": ("psum", [128, 4096], F32)}
 for _d, _l in (
-    (BF, "xt 1280 ut 512 vt 512 rowg 128 same 128 ck 512 cv 2048 ez 520 e1 520 wtab 64 lone 64 sg 512 wm 540 dec 540 cut 20 "
-         "z60 60 wx 160 fl 640 d16 160 idrow 160 ot0 352 ot1 352 ot2 352 pab 320 pabs 320 cg 480 cs 480 "
-         "tw 704 tx 320 ga 640 v1 704 v2 640 et 704 e3 1920 o3 2048 m3 480 ft 640 xn 640"),
+    (BF, "xt 1280 ut 512 vt 512 rowg 128 same 128 ck 512 cv 1024 ez 520 wtab 64 lone 64 sg 512 wm 540 dec 540 cut 20 "
+         "z60 60 fl 720 d16 160 idrow 160 ot0 352 ot1 352 ot2 352 pab 320 pabs 320 cg 480 cs 480 "
+         "w0 2048 w1 2048 w2 2048 tx 640 e3 3840 m3 480 gt 1920 ft 640 xn 640"),
     (F32, "hcf 4 pc 10 jrow 17 pw0 16 pw1 16 zr 16 pa1 16 pa2 16 pat4 16 d4 64 cl 10 sp 10 k64 48 crow 48 ks 48 hb 48 "
-          "sc 1728 mid 12 tab 120 vs 160 r4 4 r6 6 r7 6 th0 80 thr 80 dh 80 mm 80 sel 80 tq 640 yb 320"),
+          "sc 1344 tab 120 vs 160 r4 4 r6 6 r7 6 th0 80 thr 80 dh 80 mm 80 sel 80 tq 640 yb 320"),
     (I32, "hci 4 pi 1 pci 4 yk 48 hd 48 dg 32"),
-    (U16, "opt 10 opm 10 oq 4 lk 4 lv 6 hu0 48 hu1 48 hu2 48 hu3 48 du 32 so0 30 so1 30 so2 30 lo0 30 lo1 30 lo2 30 pabu 40 cu 30"),
-    (QC, "qx 320 qu 128 qv 128 qw 512 qck 128 qcv 512 qe 512 q1 512 qs 128 qf 160 qg 160 qz 160 lq0 160 lq1 160 lq2 160"),
-    (U8, "sx 320 su 128 sv 128 sw 512 sck 128 scv 512 se 512 s1 512 ss 128 sf 160 sq 160 sz 160 ls0 160 ls1 160 ls2 160"),
+    (U16, "opt 10 opm 10 oq 4 lk 4 lv 6 hu0 48 hu1 48 hu2 48 hu3 48 du 32 so0 30 so1 30 so2 30 lo0 30 lo1 30 lo2 30 pabu 20 cu 30"),
+    (QC, "qx 320 qu 128 qv 128 qw 512 qck 128 qcv 256 qe 512 qs 128 qf 180 qg 160 qz 480 lq0 160 lq1 160 lq2 160"),
+    (U8, "sx 320 su 128 sv 128 sw 512 sck 128 scv 256 se 512 ss 128 sf 180 sq 160 sz 480 ls0 160 ls1 160 ls2 160"),
 ):
     _w = _l.split()
     for _i in range(0, len(_w), 2):
         SCRATCH[_w[_i]] = ("sbuf", [128, int(_w[_i + 1])], _d)
 
-TABLE = "a00 t02 b00 t03 a01 v02 b01 v03 s00 a12 t13 a10 s01 v13 b10 p12 a11 s10 p11 c10 v12 v11"
-READ = "c0 C1 C2 g0 G1 c3 G2 t0 K0 t1 K1 f0 f1 K2 t2 s3 f2 o3"
+PEEL = ("s2 s0 t2 s1 t0 l2 t1 f0 f1", "d2 d1 d0 s2 s1 t2 s0 t1 l2 t0 f1 f0")
+MODE = "VVSSSSVV"
+LISTS = "PA0610 PV0006 kA2 kA0 PV1020 S0 S1 U0 m2 kA1 m0 U1"
+TABLE = "a02 t00 m1 b02 t01 v00 s02 b03 a03 a10 v01 s03 b10 t12 u s10 a11 t13 b11 v12 s11"
+READ = "rA003 v13 rA201 rV101 rV213 rA301 q0 rA312 rV123 rA112 q1 rA323 q2 eA2 eV3 eA0 eV1"
 
 POOL = {"V": 40, "A": 24, "P": 16, "G": 24}
 NDMA = 16
@@ -148,6 +152,11 @@ def rank_program(g, core, T, topo):
     def act(out, a, r, w, scale=1.0, join=None):
         return op("A", lambda: S.activation(out, a, AF.Copy, scale=scale), r, w, join)
 
+    def shrink(e, out, b, w):
+        if e == "V":
+            return ts(out, bank(b), SMALL, None, A.mult, None, ["B%d" % b], w)
+        return act(out, bank(b), ["B%d" % b], w, scale=SMALL)
+
     def mx(b, lc, ls, rc, rs, r, start=True, stop=True, w=H):
         return op("P", lambda: g.tensor.matmul_mx(bank(b, w), lc, ls, rc, rs, start, stop), r, ["B%d" % b], acc=not start)
 
@@ -167,9 +176,6 @@ def rank_program(g, core, T, topo):
 
     def part(c, s, b):
         return c[:, 128 * b:128 * b + 128], s[:, 128 * b:128 * b + 128]
-
-    def eb(b, unit):
-        return part(T.q1, T.s1, b) if unit else part(T.qe, T.se, b)
 
     def third(buf, k, w=H, step=H):
         return buf[:, step * k:step * k + w]
@@ -191,21 +197,18 @@ def rank_program(g, core, T, topo):
     iota(T.jrow[:], [[1, 17]], -1, 0, ["jrow"])
     iota(T.rowg[:], [[1, 8], [0, 16]], 0, 0, ["rowg"])
     fill(T.sg[:, H:512], 512 - H, 0, ["sgz"])
-    iota(T.r4[:], [[9, 4]], 8, 0, ["r4"])
+    iota(T.r4[:], [[7, 4]], 6, 0, ["r4"])
     fill(T.z60[:], 60, 0, ["z60"])
     j = None
     for k in range(3):
-        j = fill(T.sc[:, SC * k + S0:SC * k + S0 + 90:2], 45, 0, ["scz"], j)
-    j = None
-    for d in range(4):
-        j = fill(T.mid[:, 3 * d:3 * d + 3], 3, MID[d], ["mid"], j)
-
-    def centre():
-        for k in range(3):
-            act(T.sc[:, SC * k + S0 + 4:SC * k + S0 + 72:6], T.mid[:], ["mid", "scz"], ["scB%d" % k])
+        at = SC * k + S0
+        j = fill(T.sc[:, at + 58:at + 70:2], 6, 0, ["scz"], j)
+        for d in range(4):
+            j = fill(T.sc[:, at + 14 * d + 4:at + 14 * d + 14:4], 3, MID[d], (), j)
 
     def peel_fills():
-        fill(T.fl[:, 3:640:4], H, 0, ["flz"])
+        j = fill(T.fl[:, 3:640:4], H, 0, ["flz"])
+        fill(T.fl[:, 640:720], 80, 0, (), j)
         j = iota(T.cl[:], [[16, 10]], 192, 0, ["cl"])
         iota(T.k64[:], [[64, 3], [0, 16]], 0, 0, ["k64"], join=j)
         fill(T.ez[:], 520, 64, ["ez"])
@@ -214,12 +217,12 @@ def rank_program(g, core, T, topo):
 
     def late_fills():
         j = None
-        for at, c in ((slice(0, 80, 4), 1000), (slice(1, 80, 4), 64), (slice(2, 40, 4), 1), (slice(42, 80, 4), 1000), (slice(3, 80, 4), 0)):
+        for at, c in ((slice(0, 80, 4), 1000), (slice(1, 80, 4), 4), (slice(2, 40, 4), 2), (slice(42, 80, 4), 1000),
+                      (slice(3, 40, 4), 1), (slice(43, 80, 4), 2)):
             j = fill(T.th0[:, at], len(range(80)[at]), c, ["th0"], j)
         j = iota(T.idrow[:], [[1, H]], 0, 0, ["idrow"])
-        for b in ("tw", "v1", "et"):
-            fill(T[b][:, H:4 * PL:PL], 4, 0, [b + "z"], j)
-        fill(T.o3[:, 496:2048:512], 4, 0, ["o3z"], j)
+        for b in ("w0", "w1", "w2"):
+            fill(T[b][:, 496:2048:512], 4, 0, [b + "z"], j)
         fill(T.ot0[:, 0:192], 192, H, ["ot0"], j)
         j = fill(T.m3[:, 0:480:3], H, 0, ["m3"])
         for e in (1, 2):
@@ -253,7 +256,7 @@ def rank_program(g, core, T, topo):
     ts(T.same[:], T.rowg[:], PG, None, A.is_equal, None, ["rowg", "pc"], ["same"])
     tt(T.pat4[:], T.pa1[:], T.pa2[:], A.add, ["pa1", "pa2"], ["pat4"])
     act(T.d4[:], T.pat4[:].indirect(T.opt[:, 0:4]), ["pat4", "opt"], ["d4"])
-    for i in range(4):
+    for i in range(2):
         j = None
         for t in range(4):
             j = act(T.cv[:, 512 * i + t:512 * i + 512:4], T.same[:], ["same"], ["cv%d" % i], scale=WEIGH[i][t], join=j)
@@ -281,9 +284,8 @@ def rank_program(g, core, T, topo):
         for k in range(3):
             j = ts(T.crow[:, 16 * k:16 * k + 16], T.zr[:], T.hcf[:, k:k + 1], None, A.add, None, ["zr", "hcf"], ["crow%d" % k], j)
         j = cp(T.oq[:], T.r4[:], ["r4"], ["oq"])
-        need("V", ["scz"], ())
         for k in range(3):
-            j = ms(T.sc[:, SC * k + S0:SC * k + S0 + 90:18], HUGE, ["sch"], j)
+            j = ms(T.sc[:, SC * k + S0:SC * k + S0 + 70:14], HUGE, ["sch"], j)
 
     def flag_tile(i):
         qz(part(T.qcv, T.scv, i)[0], part(T.qcv, T.scv, i)[1], T.cv[:, 512 * i:512 * i + 512], ["cv%d" % i], ["qcv%d" % i])
@@ -308,9 +310,8 @@ def rank_program(g, core, T, topo):
             j = cp(T.lv[:], T.r7[:], ["r7"], ["lv"])
             ts(T.thr[:], T.th0[:], C16, None, A.subtract, None, ["th0", "c16"], ["thr"], j)
 
-    def units(b, unit):
-        src, key = (T.e1, "e1") if unit else (T.ez, "ez")
-        qz(eb(b, unit)[0], eb(b, unit)[1], src[:, 3 - b:515 - b], [key], ["q%s%d" % (key, b)])
+    def units(b):
+        qz(part(T.qe, T.se, b)[0], part(T.qe, T.se, b)[1], T.ez[:, 3 - b:515 - b], ["ez"], ["qe%d" % b])
 
     DH = ["dh0", "dh1"]
     WM = [["wm0", "wm3"], ["wm1"], ["wm2", "wm4"]]
@@ -338,7 +339,7 @@ def rank_program(g, core, T, topo):
         ts(T.dg[:], T.yk[:, 0:32], 12, 3, A.logical_shift_right, A.bitwise_and, ["yk"], ["dg"])
         steps[3]()
         gap()
-        ts(T.du[:], T.dg[:], 9.0, 8.0, A.mult, A.add, ["dg"], ["du"])
+        ts(T.du[:], T.dg[:], 7.0, 6.0, A.mult, A.add, ["dg"], ["du"])
 
     def writers_digits(hu):
         for f, k, a, b, key in ((cp, 2, 0, 6, "wm2"), (act, 2, 6, 10, "wm4"), (cp, 0, 0, 6, "wm0"), (act, 0, 6, 10, "wm3"), (act, 1, 0, 10, "wm1")):
@@ -349,39 +350,41 @@ def rank_program(g, core, T, topo):
         scores(1, 3)
 
     ra = addresses(3, "hu3")
-    un = [lambda b=b, u=u: units(b, u) for u in (True, False) for b in range(4)]
-    ft = [lambda i=i: flag_tile(i) for i in range(4)]
-    spare = [ft[0], ft[1], first_readers, lambda: signs(3), lambda: keys(3), ft[2], ra[0], ft[3]] + un[0:4] + [ra[1], ra[2]] + un[4:6] + [ra[3]] + un[6:8]
+    un = [lambda b=b: units(b) for b in range(4)]
+    ft = [lambda i=i: flag_tile(i) for i in range(2)]
+    spare = [ft[0], ft[1], first_readers, lambda: signs(3), lambda: keys(3), ra[0]] + un + [ra[1], ra[2], ra[3]]
 
     def gap(n=1):
         for i in range(min(n, len(spare))):
             spare.pop(0)()
 
-    def decode(b0, order, c, s, key, unit, stop=True):
+    def decode(b0, order, c, s, key, start=True, stop=True):
         for b in order:
-            mx(b0 + b, eb(b, unit)[0], eb(b, unit)[1], c, s, ["q%s%d" % ("e1" if unit else "ez", b), key], stop=stop)
+            mx(b0 + b, part(T.qe, T.se, b)[0], part(T.qe, T.se, b)[1], c, s, ["qe%d" % b, key], start, stop)
+
+    def plane(s, b):
+        return T["w%d" % s][:, 512 * b + 16:512 * b + 496:3]
+
+    def window(s, b):
+        return T["w%d" % s][:, 512 * b + 16:512 * b + 497]
+
+    def term(u, k):
+        return T.e3[:, 480 * u + k:480 * u + 480:3]
 
     def writers_numbers(t):
         event("rq%d" % t, 2 * nin, (), ["lq%d" % t])
-        decode(4, range(4), T["lq%d" % t][:], T["ls%d" % t][:], "lq%d" % t, True)
+        decode(4, range(4), T["lq%d" % t][:], T["ls%d" % t][:], "lq%d" % t)
         for b in range(4):
-            act(third(T.tw, b, H, PL), bank(4 + b), ["B%d" % (4 + b)], ["tw%d" % b])
+            shrink("A", plane(0, b), 4 + b, ["w0%d" % b])
 
-    def writers_copies():
-        for b in (2, 3):
-            act(third(T.tx, b - 2), bank(4 + b), ["B%d" % (4 + b)], ["tx%d" % b])
-        for i, b, c in ((0, 0, -1.0), (1, 1, -1.0), (2, 0, 1.0)):
-            act(term(i, 0), bank(4 + b), ["B%d" % (4 + b)], ["e3%d0" % i], scale=c)
-
-    def term(i, k):
-        return T.e3[:, 480 * i + k:480 * i + 480:3]
-
-    def add3(i):
-        scan(T.o3[:, 512 * i + 14:512 * i + 494], T.m3[:], T.e3[:, 480 * i:480 * i + 480], 0.0, A.mult, A.add,
-             ["m3"] + ["e3%d%d" % (i, k) for k in range(3)], ["o3%d" % i])
-
-    def sums(i):
-        return T.o3[:, 512 * i + 16:512 * i + 496:3]
+    def writers_copies(o):
+        for u in range(8):
+            b = u % 4
+            if MODE[u] == "S":
+                act(term(u, 0), bank(4 + b), ["B%d" % (4 + b)], ["e3%d0" % u], scale=SMALL if u > 3 else -SMALL)
+            elif u < 4:
+                shrink("A", third(T.tx, b), 4 + b, ["tx%d" % b])
+        decode(4, range(4), half(o)[0], half(o)[1], "qx%d" % o, True, False)
 
     def cells():
         tt(T.hb[:], T.hd[:], T.k64[:], A.add, ["hd", "k64"], ["hb"])
@@ -389,54 +392,90 @@ def rank_program(g, core, T, topo):
     def choices():
         h = [lst(T.hb, k) for k in range(3)]
         j = None
-        for at, x, y in ((0, h[0], h[1]), (1, h[1], T.sp[:]), (2, T.sp[:], h[2]), (40, h[1], h[0]), (42, h[2], h[1])):
+        for at, x, y in ((0, h[0], h[1]), (1, h[1], h[2]), (2, h[2], T.sp[:]), (40, h[1], h[0]), (42, h[2], h[1])):
             j = tt(T.dh[:, at:at + 37:4], x, y, A.subtract, ["hb", "sp"], ["dh0"], j)
         j = None
-        for at, x in ((3, h[2]), (41, h[0]), (43, h[1])):
-            j = act(T.dh[:, at:at + 37:4], x, ["hb"], ["dh1"], join=j)
+        for at, x in ((3, T.sp[:]), (41, h[0]), (43, h[1])):
+            j = act(T.dh[:, at:at + 37:4], x, ["hb", "sp"], ["dh1"], join=j)
 
-    def counts(p, b):
+    def peel(p, hu, b, wide=H):
         src = "dec" if p else "wm"
-        if p:
-            for k in (2, 1, 0):
-                tt(third(T.dec, k, H, TH), third(T.wm, k, H, TH), bank(b), A.min, WM[k] + ["B%d" % b], ["dec%d" % k])
-        for k in ((2, 1, 0) if p else (2, 0, 1)):
-            j = None
-            if k == 1 and not p:
-                totals(2)
-            for c in range(3):
-                at = SC * k + 2 * (3 * c + (2 if p else 1))
-                j = scan(T.sc[:, at:at + 9 * 59 + 1:9], T.z60[:], T[src][:, TH * k + c:TH * k + TH:3], float(MID[0] if p else -MID[0]),
-                         A.add, A.subtract if p else A.add, ["z60", src + "z", "scz"] + (["dec%d" % k] if p else WM[k]),
-                         ["sc%s%d" % ("B" if p else "A", k)], j)
-
-    def totals(k):
-        at = SC * k + S0
-        scan(third(T.tab, k, 36, 40), T.sc[:, at:at + 72:2], T.sc[:, at + 18:at + 90:2], 0.0, A.add, A.subtract,
-             ["sch", "scA%d" % k, "scB%d" % k], ["tab%d" % k])
-
-    def peel(p, hu, b):
-        order = (1, 0) if p else (0, 1)
-        if p:
-            totals(2)
-        totals(order[0])
-        if p:
-            tt(T.wx[:], third(T.wm, 0, H, TH), bank(b), A.subtract, WM[0] + ["B%d" % b], ["wx"])
-            totals(0)
-        tt(T.lone[:], third(T.tab, 2, 36, 40).indirect(T.oq[:]), T.wtab[:], A.is_equal, ["tab2", "oq", "wtab"], ["lone"])
-        if not p:
-            totals(1)
-        act(T.fl[:, 2:640:4], T.lone[:].indirect(lst(T[hu], 2)), ["lone", hu], ["fl2"])
-        j = None
-        for k in order:
-            x, xk = (T.wx[:], ["wx"]) if p and k == 0 else (third(T.wm, k, H, TH), WM[k])
-            j = tt(T.fl[:, k:640:4], third(T.tab, k, 36, 40).indirect(lst(T.du, k)), x, A.is_equal, ["tab%d" % k, "du"] + xk, ["fl%d" % k], j)
+        for what, k in [(x[0], int(x[1])) for x in PEEL[p > 0].split()]:
+            x, xk = (third(T.dec, k, H, TH), ["dec%d" % k]) if p else (third(T.wm, k, H, TH), WM[k])
+            if what == "d":
+                tt(x, third(T.wm, k, H, TH), bank(b), A.max, WM[k] + ["B%d" % b], xk)
+            elif what == "s":
+                j = None
+                for c in range(3):
+                    at = SC * k + 2 * (2 * c + 1)
+                    off, key = (T.ps[:, 512 * b + c:512 * b + TH:3], "B%d" % b) if p else (T.z60[:], "z60")
+                    j = scan(T.sc[:, at:at + 7 * 59 + 1:7], T[src][:, TH * k + c:TH * k + TH:3], off, float(-MID[0]),
+                             A.add, A.subtract, [key, src + "z"] + xk, ["sc%d" % k], j)
+            elif what == "t":
+                at = SC * k + S0
+                scan(third(T.tab, k, 28, 40), T.sc[:, at:at + 56:2], T.sc[:, at + 14:at + 70:2], 0.0, A.add, A.subtract,
+                     ["sch", "scz", "sc%d" % k], ["tab%d" % k])
+            elif what == "l":
+                tt(T.lone[:], third(T.tab, k, 28, 40).indirect(T.oq[:]), T.wtab[:], A.is_equal, ["tab%d" % k, "oq", "wtab"], ["lone"])
+                act(T.fl[:, k:640:4], T.lone[:].indirect(lst(T[hu], k)), ["lone", hu], ["fl%d" % k])
+            else:
+                tt(T.fl[:, k:640:4], third(T.tab, k, 28, 40).indirect(lst(T.du, k)), x, A.is_equal, ["tab%d" % k, "du"] + xk, ["fl%d" % k])
         gap()
-        qz(T.qf[:], T.sf[:], T.fl[:], ["fl0", "fl1", "fl2", "flz"], ["qf"])
+        qz(T.qf[:, 0:wide], T.sf[:, 0:wide], T.fl[:, 0:4 * wide], ["fl0", "fl1", "fl2", "flz"], ["qf"])
         for i, bk in enumerate((1, 0, 2)):
             if i >= p:
-                c = p + 1 if i == 2 else 0
-                mx(bk, part(T.qcv, T.scv, c)[0], part(T.qcv, T.scv, c)[1], T.qf[:], T.sf[:], ["qcv%d" % c, "qf"], start=p == 0, stop=p == i)
+                c, n = (1, H) if i == 2 else (0, TH)
+                mx(bk, part(T.qcv, T.scv, c)[0], part(T.qcv, T.scv, c)[1], T.qf[:, 0:n], T.sf[:, 0:n], ["qcv%d" % c, "qf"],
+                   start=p == 0, stop=p == i, w=n)
+
+    def lists(x, ot, lo, hr, keys):
+        e = {"V": cp, "A": act}.get(x[1:2])
+        if x[0] == "P":
+            a, b = int(x[2:4]), int(x[4:6])
+            at = 20 - 20 * (a // 10)
+            e(T.pab[:, 16 * a:16 * b], ot[:, 0:192].indirect(lo[:, at + a:at + b]), keys, ["pab%d" % a])
+        elif x[0] == "k":
+            k = int(x[2])
+            e(third(T.cg, k), ot[:, 64 * k:64 * k + 64].indirect(lst(T[hr], k)), [keys[0], hr], ["cg%d" % k])
+        elif x[0] == "S":
+            i = int(x[1])
+            scan(third(T.pabs, i), T.d16[:], third(T.pab, i), 0.0, A.add, A.min,
+                 ["d16"] + ["pab%d" % a for a in range(10 * i, 10 * i + 10)], ["pabs%d" % i])
+        elif x[0] == "m":
+            k = int(x[1])
+            scan(third(T.cs, k), T.d16[:], third(T.cg, k), 0.0, A.add, A.min, ["d16", "cg%d" % k], ["cs%d" % k])
+        elif x[0] == "U":
+            i = int(x[1])
+            ts(T.pabu[:, 10 * i:10 * i + 10], T.pabs[:, H * i + 15:H * i + H:16], C16, 3.0, A.add, A.mult, ["pabs%d" % i, "c16"], ["pabu%d" % i])
+        else:
+            ts(T.cu[:], T.cs[:, 15:480:16], C16, 3.0, A.add, A.mult, ["cs0", "cs1", "cs2", "c16"], ["cu"])
+
+    def table(x):
+        what, p, b = x[0], int(x[1]), int(x[2])
+        u, i = 4 * p + b, int(what in "bv")
+        c, ck = window(p, b).indirect(T.pabu[:, 10 * i:10 * i + 10]), ["w%dz" % p, "w%d%d" % (p, b), "pabu%d" % i]
+        if what in "ab":
+            act(term(u, 1 + i), c, ck, ["e3%d%d" % (u, 1 + i)])
+        elif what == "s":
+            scan(T["w%d" % (p + 1)][:, 512 * b + 14:512 * b + 494], T.m3[:], T.e3[:, 480 * u:480 * u + 480], 0.0, A.mult, A.add,
+                 ["m3"] + ["e3%d%d" % (u, k) for k in range(3)], ["w%d%d" % (p + 1, b)])
+        elif what == "t":
+            tt(third(T.tq, b), c, plane(0, b) if p else third(T.tx, b), A.add if p else A.subtract,
+               ck + ["w0%d" % b if p else "tx%d" % b], ["tq%d" % b])
+        else:
+            tt(plane(p + 1, b), c, third(T.tq, b), A.add, ck + ["tq%d" % b], ["w%d%d" % (p + 1, b)])
+
+    def read(x):
+        if x[0] == "r":
+            b, a, c = int(x[2]), int(x[3]), int(x[4])
+            (cp if x[1] == "V" else act)(T.gt[:, 640 * a + b:640 * c:4], window(2, b).indirect(T.cu[:, 10 * a:10 * c]),
+                                         ["w2z", "w2%d" % b, "cu"], ["gt%d%d" % (k, b) for k in range(a, c)])
+        elif x[0] == "q":
+            k = int(x[1])
+            qz(third(T.qz, k), third(T.sz, k), third(T.gt, k, 640, 640), ["gt%d%d" % (k, b) for b in range(4)], ["qz%d" % k])
+            decode(0, (2, 3, 0, 1), third(T.qz, k), third(T.sz, k), "qz%d" % k, k == 0, k == 2)
+        else:
+            shrink(x[1], T.ft[:, int(x[2]):640:4], int(x[2]), ["ft" + x[2]])
 
     def store(h, qs):
         lo = H * h
@@ -459,7 +498,6 @@ def rank_program(g, core, T, topo):
         if t == 0:
             late_fills()
             key_tile()
-        centre()
         signs(0)
         if t == 0:
             digits()
@@ -471,8 +509,7 @@ def rank_program(g, core, T, topo):
             mx(3, T.qv[:], T.sv[:], half(0)[0], half(0)[1], ["qv", "qx0"])
         writers_addresses(1, hu)
         writers_digits(hu)
-        counts(0, None)
-        peel(0, hu, None)
+        peel(0, hu, None, TH if t == 0 else H)
         if t == 0:
             owner_rows(0)
         cells()
@@ -481,18 +518,15 @@ def rank_program(g, core, T, topo):
             owner_rows(1)
         else:
             writers_numbers(t)
-        counts(1, 1)
         peel(1, hu, 1)
         if t == 0:
             owner_rows(2)
         choices()
         if t == 0:
             owner_rows(3)
-            act(T.e1[:], T.ez[:], ["ez"], ["e1"], scale=0.015625)
         else:
-            writers_copies()
+            writers_copies(o)
         gap()
-        counts(2, 0)
         peel(2, hu, 0)
         if t == 0:
             owner_rows(4)
@@ -513,87 +547,26 @@ def rank_program(g, core, T, topo):
         send([(lo[:], so[:])], "ro%d" % t, "so%d" % t, ["so%d" % t])
         if t == 0:
             writers_numbers(0)
-            writers_copies()
+            writers_copies(o)
             gap(len(spare))
         if t == 1:
             qz(T.qv[:], T.sv[:], T.vt[:], ["vt"], ["qv"])
         okey, lkey = "ot%d" % t, "lo%d" % t
         event("ro%d" % t, nin, (), [lkey])
         cp(ot[:].indirect(lo[:, 0:10]), T.idrow[:], [lkey, "idrow"], [okey])
-        for f, i, a, b, key in ((cp, 0, 0, 6, "pab0"), (act, 0, 6, 10, "pab2"), (cp, 1, 0, 4, "pab1"), (act, 1, 4, 10, "pab3")):
-            at = 20 - 10 * i
-            f(T.pab[:, H * i + 16 * a:H * i + 16 * b], ot[:, 0:192].indirect(lo[:, at + a:at + b]), [okey, lkey], [key])
-
-        def asked(k):
-            act(third(T.cg, k), ot[:, 64 * k:64 * k + 64].indirect(lst(T[hr], k)), [okey, hr], ["cg%d" % k])
-
-        def compose(k):
-            scan(third(T.cs, k), T.d16[:], third(T.cg, k), 0.0, A.add, A.min, ["d16", "cg%d" % k], ["cs%d" % k])
-
-        asked(0)
-        asked(1)
-        for i in range(2):
-            scan(third(T.pabs, i), T.d16[:], third(T.pab, i), 0.0, A.add, A.min, ["d16", "pab%d" % i, "pab%d" % (i + 2)], ["pabs%d" % i])
-        for i in range(2):
-            ts(T.pabu[:, 10 * i:10 * i + 10], T.pabs[:, H * i + 15:H * i + H:16], C16, None, A.add, None, ["pabs%d" % i, "c16"], ["pabu%d" % i])
-        ts(T.pabu[:, 20:40], T.pabs[:, 15:320:16], C16, 3.0, A.add, A.mult, ["pabs0", "pabs1", "c16"], ["pabu2"])
-
-        def cell(s, b, i):
-            if s and b < 2:
-                return T.o3[:, 512 * b + 16:512 * b + 497].indirect(T.pabu[:, 20 + 10 * i:30 + 10 * i]), ["o3z", "o3%d" % b, "pabu2"]
-            buf = "v1" if s else "tw"
-            return third(T[buf], b, H + 1, PL).indirect(T.pabu[:, 10 * i:10 * i + 10]), [buf + "z", buf + "%d" % b, "pabu%d" % i]
-
-        for what, s, b in [(x[0], int(x[1]), int(x[2])) for x in TABLE.split()]:
-            x, xk = cell(s, b, 1 if what in "bv" else 0)
-            i = 2 * s + b
-            if what in "ab" and (b == 0 or s == 0):
-                act(term(i, 1 + "ab".index(what)), x, xk, ["e3%d%d" % (i, 1 + "ab".index(what))])
-            elif what == "a":
-                act(third(T.ga, b), x, xk, ["ga%d" % b])
-            elif what == "s":
-                add3(i)
-            elif what == "c":
-                act(T.v2[:, b:640:4], sums(i), ["o3%d" % i], ["v2%d" % b])
-            elif what == "p":
-                tt(third(T.tq, b), third(T.ga, b), bank(4 + b), A.add, ["ga%d" % b, "B%d" % (4 + b)], ["tq%d" % b])
-            elif what == "t":
-                tt(third(T.tq, b), x, third(T.tx, b - 2), A.add if s else A.subtract, xk + ["tx%d" % b], ["tq%d" % b])
+        for x in (LISTS + " " + TABLE + " " + READ).split():
+            if x[0] in "abstv":
+                table(x)
+            elif x[0] in "rqe":
+                read(x)
             else:
-                tt(T.v2[:, b:640:4] if s else third(T.v1, b, H, PL), x, third(T.tq, b), A.add, xk + ["tq%d" % b], ["v%d%d" % (s + 1, b)])
-        asked(2)
-        decode(4, (0, 3, 2, 1), half(o)[0], half(o)[1], "qx%d" % o, False, False)
-        compose(0)
-        compose(1)
-        qz(T.qz[:], T.sz[:], T.v2[:], ["v20", "v21", "v22", "v23"], ["qz"])
-        decode(0, range(4), T.qz[:], T.sz[:], "qz", True)
-        compose(2)
-        ts(T.cu[:], T.cs[:, 15:480:16], C16, None, A.add, None, ["cs0", "cs1", "cs2", "c16"], ["cu"])
-
-        def read(k, b):
-            return third(T.et, b, H + 1, PL).indirect(T.cu[:, 10 * k:10 * k + 10]), ["etz", "et%d" % b, "cu"]
-
-        for what, b in [(x[0], int(x[1])) for x in READ.split()]:
-            if what in "cC":
-                (cp if what == "c" else act)(third(T.et, b, H, PL), bank(b), ["B%d" % b], ["et%d" % b])
-            elif what in "gG":
-                (cp if what == "g" else act)(third(T.ga, b), read(0, b)[0], read(0, b)[1], ["ga%d" % b])
-            elif what == "t":
-                tt(third(T.tq, b), read(1, b)[0], third(T.ga, b), A.add, read(1, b)[1] + ["ga%d" % b], ["tq%d" % b])
-            elif what == "f":
-                tt(T.ft[:, b:640:4], read(2, b)[0], third(T.tq, b), A.add, read(2, b)[1] + ["tq%d" % b], ["ft%d" % b])
-            elif what == "K":
-                act(term(3, b), read(b, 3)[0], read(b, 3)[1], ["e33%d" % b])
-            elif what == "s":
-                add3(3)
-            else:
-                cp(T.ft[:, 3:640:4], sums(3), ["o33"], ["ft3"])
+                lists(x, ot, lo, hr, [okey, lkey])
         qz(T.qg[:], T.sq[:], T.ft[:], ["ft0", "ft1", "ft2", "ft3"], ["qg"])
         for b in (2, 0, 3, 1):
             mx(4 + b, T.qw[:, 128 * b:128 * b + 128], T.sw[:, 128 * b:128 * b + 128], T.qg[:], T.sq[:], ["qw", "sw", "qg"], start=False)
         for b in (0, 1):
-            ts(T.xn[:, b:640:4], bank(4 + b), 0.015625, None, A.mult, None, ["B%d" % (4 + b)], ["xn%d" % b])
-            act(T.xn[:, b + 2:640:4], bank(6 + b), ["B%d" % (6 + b)], ["xn%d" % (b + 2)], scale=0.015625)
+            shrink("V", T.xn[:, b:640:4], 4 + b, ["xn%d" % b])
+            shrink("A", T.xn[:, b + 2:640:4], 6 + b, ["xn%d" % (b + 2)])
         if t == R - 1:
             for grp in sorted(last.values(), key=lambda x: -x["id"]):
                 wait("G", grp)

from concourse.mybir import dt, AluOpType as A, ActivationFunctionType as AF

H, R = 160, 3
TH = 180
SC, S0 = 448, 7 * 53
BIG, M = float(2 ** 20), float(2 ** 16)
BIG2, M2 = 1024.0, 256.0
U, HUGE, TINY = float(13 * 2 ** 16), float(2 ** 60), float(2 ** -60)
SMALL = 0.015625
MID = [27 * sum(64 ** e for e in range(d, 4)) for d in range(4)]
WEIGH = [(U, U, U, 0.0), (4.0, 2.0, 1.0, 0.0)]
F32, BF, I32, U16, QC, U8 = "float32", "bfloat16", "int32", "uint16", "float8_e4m3fn_x4", "uint8"

SCRATCH = {"ps": ("psum", [128, 4096], F32)}
for _d, _l in (
    (BF, "xt 1280 ut 512 vt 512 rowg 128 same 128 ck 512 cv 1024 ez 520 wtab 64 lone 64 sg 512 wm 540 dec 540 cut 20 "
         "z60 60 fl 720 d16 160 idrow 160 ot0 352 ot1 352 ot2 352 pab 320 pabs 320 cg 480 cs 480 "
         "w0 2048 w1 2048 w2 2048 tx 640 e3 3840 m3 480 gt 1920 ft 640 xn 640"),
    (F32, "hcf 4 pc 10 jrow 17 pw0 16 pw1 16 zr 16 pa1 16 pa2 16 pat4 16 d4 64 cl 10 sp 10 k64 48 crow 48 ks 48 hb 48 "
          "sc 1344 tab 120 vs 160 r4 4 r6 6 r7 6 th0 80 thr 80 dh 80 mm 80 sel 80 tq 640 yb 320"),
    (I32, "hci 4 pi 1 pci 4 yk 48 hd 48 dg 32"),
    (U16, "opt 10 opm 10 oq 4 lk 4 lv 6 hu0 48 hu1 48 hu2 48 hu3 48 du 32 so0 30 so1 30 so2 30 lo0 30 lo1 30 lo2 30 pabu 20 cu 30"),
    (QC, "qx 320 qu 128 qv 128 qw 512 qck 128 qcv 256 qe 512 qs 128 qf 180 qg 160 qz 480 lq0 160 lq1 160 lq2 160"),
    (U8, "sx 320 su 128 sv 128 sw 512 sck 128 scv 256 se 512 ss 128 sf 180 sq 160 sz 480 ls0 160 ls1 160 ls2 160"),
):
    _w = _l.split()
    for _i in range(0, len(_w), 2):
        SCRATCH[_w[_i]] = ("sbuf", [128, int(_w[_i + 1])], _d)

PEEL = ("s2 s0 t2 s1 t0 l2 t1 f0 f1", "d2 d1 d0 s2 s1 t2 s0 t1 l2 t0 f1 f0")
MODE = "VVSSSSVV"
LISTS = "PA0610 PV0006 kA2 kA0 PV1020 S0 S1 U0 m2 kA1 m0 U1"
TABLE = "a02 t00 m1 b02 t01 v00 s02 b03 a03 a10 v01 s03 b10 t12 u s10 a11 t13 b11 v12 s11"
READ = "rA003 v13 rA201 rV101 rV213 rA301 q0 rA312 rV123 rA112 q1 rA323 q2 eA2 eV3 eA0 eV1"

POOL = {"V": 40, "A": 24, "P": 16, "G": 24}
NDMA = 16
SEMAPHORES = ([q + "%d" % i for q in POOL for i in range(POOL[q])] + ["D%d" % i for i in range(NDMA)]
              + [s + "%d" % t for t in range(R) for s in ("ro", "rq", "so", "sq")])


def rank_program(g, core, T, topo):
    rank = T.rank_of(core)
    if rank is None:
        return
    n = len(T.cores)
    nxt, prv = T.cores[(rank + 1) % n], T.cores[(rank - 1) % n]
    rid, pid = topo.addr(nxt)[0], topo.addr(nxt)[1]
    mask, nout, nin = topo.mask(core, nxt), len(topo.engines(core, nxt)), len(topo.engines(prv, core))

    Q = {"V": g.vector, "A": g.scalar, "P": g.tensor, "G": g, "S": g.sync}
    known = {q: set() for q in Q}
    lastw, readers, last, count = {}, {}, {}, {}
    nid, ndma = [0], [0]

    def wait(q, grp):
        if grp["id"] in known[q]:
            return
        Q[q].wait_ge(T.sem[grp["sem"]], grp["val"])
        grp["closed"] = True
        known[q] |= grp["known"]
        known[q].add(grp["id"])

    def need(q, r, w, join=None, acc=False):
        deps = []
        for k in r:
            if k in lastw:
                deps.append(lastw[k])
            if k[0] == "B":
                deps += [x for x in readers.get(k, []) if x["q"] != q]
        for k in w:
            if k in lastw and not (acc and lastw[k]["q"] == q):
                deps.append(lastw[k])
            deps += readers.get(k, [])
        for d in sorted(deps, key=lambda x: -x["id"]):
            if d is not join:
                wait(q, d)

    def op(q, fn, r=(), w=(), join=None, dma=False, acc=False):
        need(q, r, w, join, acc)
        if join is not None and not join["closed"]:
            grp = join
        else:
            if dma:
                sem = "D%d" % ndma[0]
                ndma[0] += 1
            else:
                names = [q + "%d" % i for i in range(POOL[q])]
                free = [s for s in names if s not in last or last[s]["id"] in known[q]]
                if not free:
                    old = min(names, key=lambda s: last[s]["id"])
                    wait(q, last[old])
                    free = [old]
                sem = free[0]
                if sem in last:
                    last[sem]["closed"] = True
            nid[0] += 1
            grp = {"id": nid[0], "sem": sem, "val": count.get(sem, 0), "known": set(), "closed": False, "q": q}
            last[sem] = grp
        inc = 16 if dma else 1
        fn().then_inc(T.sem[grp["sem"]], inc)
        grp["val"] += inc
        count[grp["sem"]] = grp["val"]
        grp["known"] |= known[q]
        for k in r:
            readers.setdefault(k, []).append(grp)
        for k in w:
            lastw[k] = grp
            readers[k] = []
        return grp

    def event(sem, val, r, w):
        nid[0] += 1
        grp = {"id": nid[0], "sem": sem, "val": val, "known": set(), "closed": True, "q": "X"}
        last[sem] = grp
        for k in r:
            readers.setdefault(k, []).append(grp)
        for k in w:
            lastw[k] = grp

    def send(pairs, there, here, r):
        need("G", r, ())
        for dst, src in pairs:
            g.remote_dma(dst, src, T.sem[there], T.sem[here], pid, rid, mask)
        event(here, nout * len(pairs), r, ())

    V, S = g.vector, g.scalar

    def bank(b, w=H):
        return T.ps[:, 512 * b:512 * b + w]

    def ts(out, in0, s1, s2, o0, o1, r, w, join=None):
        if o1 is None:
            return op("V", lambda: V.tensor_scalar(out, in0, s1, None, o0), r, w, join)
        return op("V", lambda: V.tensor_scalar(out, in0, s1, s2, o0, o1), r, w, join)

    def tt(out, a, b, o, r, w, join=None):
        return op("V", lambda: V.tensor_tensor(out, a, b, o), r, w, join)

    def cp(out, a, r, w, join=None):
        return op("V", lambda: V.tensor_copy(out, a), r, w, join)

    def ms(out, c, w, join=None):
        return op("V", lambda: V.memset(out, c), (), w, join)

    def scan(out, d0, d1, init, o0, o1, r, w, join=None):
        return op("V", lambda: V.tensor_tensor_scan(out, d0, d1, init, o0, o1), r, w, join)

    def qz(c, s, t, r, w, join=None):
        return op("V", lambda: V.quantize_mx(c, s, t), r, w, join)

    def act(out, a, r, w, scale=1.0, join=None):
        return op("A", lambda: S.activation(out, a, AF.Copy, scale=scale), r, w, join)

    def shrink(e, out, b, w):
        if e == "V":
            return ts(out, bank(b), SMALL, None, A.mult, None, ["B%d" % b], w)
        return act(out, bank(b), ["B%d" % b], w, scale=SMALL)

    def mx(b, lc, ls, rc, rs, r, start=True, stop=True, w=H):
        return op("P", lambda: g.tensor.matmul_mx(bank(b, w), lc, ls, rc, rs, start, stop), r, ["B%d" % b], acc=not start)

    def dma(q, out, a, r, w, join=None):
        return op(q, lambda: Q[q].dma_start(out, a), r, w, join, dma=True)

    def iota(out, pat, base, cm, w, flt=True, join=None):
        if flt:
            return op("G", lambda: g.iota(out, pat, base, cm, allow_small_or_imprecise_dtypes=True), (), w, join)
        return op("G", lambda: g.iota(out, pat, base, cm), (), w, join)

    def fill(out, n, c, w, join=None):
        return iota(out, [[0, n]], c, 0, w, join=join)

    def half(h):
        return T.qx[:, H * h:H * h + H], T.sx[:, H * h:H * h + H]

    def part(c, s, b):
        return c[:, 128 * b:128 * b + 128], s[:, 128 * b:128 * b + 128]

    def third(buf, k, w=H, step=H):
        return buf[:, step * k:step * k + w]

    def lst(buf, k):
        return buf[:, 16 * k:16 * k + 10]

    PM, PG, PT, PA, C16, A16 = [T.pc[:, j:j + 1] for j in range(6)]

    dma("S", T.ut[:], T.u[:], (), ["ut"])
    dma("S", T.xt[:, 0:640], T.x[:, 0:640], (), ["xt0"])
    dma("A", T.hci[:, 0:3], T.hc[:], (), ["hci"])
    dma("S", T.xt[:, 640:1280], T.x[:, 640:1280], (), ["xt1"])
    j = dma("S", T.qw[:].bitcast(dt.uint8), T.wc[:], (), ["qw"])
    dma("S", T.sw[:], T.ws[:], (), ["sw"], join=j)
    dma("S", T.vt[:], T.v[:], (), ["vt"])

    iota(T.pi[:], [[0, 1]], 0, 1, ["pi"], flt=False)
    iota(T.jrow[:], [[1, 17]], -1, 0, ["jrow"])
    iota(T.rowg[:], [[1, 8], [0, 16]], 0, 0, ["rowg"])
    fill(T.sg[:, H:512], 512 - H, 0, ["sgz"])
    iota(T.r4[:], [[7, 4]], 6, 0, ["r4"])
    fill(T.z60[:], 60, 0, ["z60"])
    j = None
    for k in range(3):
        at = SC * k + S0
        j = fill(T.sc[:, at + 58:at + 70:2], 6, 0, ["scz"], j)
        for d in range(4):
            j = fill(T.sc[:, at + 14 * d + 4:at + 14 * d + 14:4], 3, MID[d], (), j)

    def peel_fills():
        j = fill(T.fl[:, 3:640:4], H, 0, ["flz"])
        fill(T.fl[:, 640:720], 80, 0, (), j)
        j = iota(T.cl[:], [[16, 10]], 192, 0, ["cl"])
        iota(T.k64[:], [[64, 3], [0, 16]], 0, 0, ["k64"], join=j)
        fill(T.ez[:], 520, 64, ["ez"])
        iota(T.r6[:], [[64, 6]], 15, 0, ["r6"])
        op("G", lambda: g.affine_select(T.ez[:], T.ez[:], [[-1, 520]], A.is_equal, 0.0, 3, 4), ["ez"], ["ez"])

    def late_fills():
        j = None
        for at, c in ((slice(0, 80, 4), 1000), (slice(1, 80, 4), 4), (slice(2, 40, 4), 2), (slice(42, 80, 4), 1000),
                      (slice(3, 40, 4), 1), (slice(43, 80, 4), 2)):
            j = fill(T.th0[:, at], len(range(80)[at]), c, ["th0"], j)
        j = iota(T.idrow[:], [[1, H]], 0, 0, ["idrow"])
        for b in ("w0", "w1", "w2"):
            fill(T[b][:, 496:2048:512], 4, 0, [b + "z"], j)
        fill(T.ot0[:, 0:192], 192, H, ["ot0"], j)
        j = fill(T.m3[:, 0:480:3], H, 0, ["m3"])
        for e in (1, 2):
            fill(T.m3[:, e:480:3], H, 1, (), j)
        for t in (1, 2):
            fill(T["ot%d" % t][:, 0:192], 192, H, ["ot%d" % t])

    j = ms(T.ck[:], 0.0, ["ck"])
    ms(T.zr[:], 0.0, ["zr"], j)
    j = ts(T.pci[:, 0:1], T.pi[:], 15, None, A.bitwise_and, None, ["pi"], ["pci0"])
    ts(T.pci[:, 1:2], T.pi[:], 4, None, A.logical_shift_right, None, ["pi"], ["pci1"], j)
    ts(T.pci[:, 2:3], T.pi[:], 3, None, A.bitwise_and, None, ["pi"], ["pci2"], j)
    ts(T.pci[:, 3:4], T.pi[:], 2, 3, A.logical_shift_right, A.bitwise_and, ["pi"], ["pci3"], j)
    cut = [0.0] + [s * 1.5 * 2 ** (23 + 6 * d) for d in (1, 2, 3) for s in (1, -1)]
    j = ms(T.cut[:, 0:2], cut[0], ["cut"])
    for e in (1, 2):
        ms(T.cut[:, 3 * e - 1:3 * e + 2], cut[e], (), j)
    cp(T.pc[:, 0:4], T.pci[:], ["pci0"], ["pc"])
    for e in (3, 4, 5, 6):
        ms(T.cut[:, 3 * e - 1:3 * e + 2], cut[e], (), j)
    j = None
    for b in ("wm", "dec"):
        for k in range(3):
            j = act(T[b][:, TH * k + H:TH * k + TH], T.cut[:], ["cut"], [b + "z"] * (k == 0), join=j)
    j = ts(T.pw0[:], T.jrow[:, 1:17], PM, 1.0, A.is_le, A.add, ["jrow", "pc"], ["pw0"])
    j2 = ts(T.pa1[:], T.jrow[:, 1:17], PA, BIG, A.is_equal, A.mult, ["jrow", "pc"], ["pa1"])
    ts(T.pa2[:], T.jrow[:, 0:16], PA, -M, A.is_equal, A.mult, ["jrow", "pc"], ["pa2"], j2)
    ts(T.opt[:], T.rowg[:, 0:10], 0.0, PT, A.mult, A.add, ["rowg", "pc"], ["opt"], j2)
    scan(T.pw1[:], T.pw0[:], T.zr[:], 0.5, A.mult, A.add, ["pw0", "zr"], ["pw1"])
    ts(T.opm[:], T.rowg[:, 0:10], 0.0, PM, A.mult, A.add, ["rowg", "pc"], ["opm"])
    ts(T.same[:], T.rowg[:], PG, None, A.is_equal, None, ["rowg", "pc"], ["same"])
    tt(T.pat4[:], T.pa1[:], T.pa2[:], A.add, ["pa1", "pa2"], ["pat4"])
    act(T.d4[:], T.pat4[:].indirect(T.opt[:, 0:4]), ["pat4", "opt"], ["d4"])
    for i in range(2):
        j = None
        for t in range(4):
            j = act(T.cv[:, 512 * i + t:512 * i + 512:4], T.same[:], ["same"], ["cv%d" % i], scale=WEIGH[i][t], join=j)
    qz(T.qu[:], T.su[:], T.ut[:], ["ut"], ["qu"])
    qz(half(0)[0], half(0)[1], T.xt[:, 0:640], ["xt0"], ["qx0"])

    def key_tile():
        j = None
        for t in range(4):
            j = ts(T.ck[:, 5 * t:512:16], T.rowg[:, t:128:4], PG, T.pw1[:, 15:16], A.is_equal, A.mult,
                   ["rowg", "pc", "pw1", "ck"], ["ck%d" % t], j)
        j = cp(T.hcf[:, 0:3], T.hci[:, 0:3], ["hci"], ["hcf"])
        ts(T.lk[:], T.opm[:, 0:4], 9.0, 4.0, A.min, A.mult, ["opm"], ["lk"], j)
        qz(T.qck[:], T.sck[:], T.ck[:], ["ck0"], ["qck"])

    def digits():
        j = None
        for d in range(4):
            j = ts(T.wtab[:, 16 * d:16 * d + 16], T.jrow[:, 1:17], PM, float(64 ** d), A.is_equal, A.mult,
                   ["jrow", "pc"], ["wtab%d" % d], j)

    def address_rows():
        ts(T.wtab[:], T.wtab[:], TINY, None, A.max, None, ["wtab0"], ["wtab"])
        j = None
        for k in range(3):
            j = ts(T.crow[:, 16 * k:16 * k + 16], T.zr[:], T.hcf[:, k:k + 1], None, A.add, None, ["zr", "hcf"], ["crow%d" % k], j)
        j = cp(T.oq[:], T.r4[:], ["r4"], ["oq"])
        for k in range(3):
            j = ms(T.sc[:, SC * k + S0:SC * k + S0 + 70:14], HUGE, ["sch"], j)

    def flag_tile(i):
        qz(part(T.qcv, T.scv, i)[0], part(T.qcv, T.scv, i)[1], T.cv[:, 512 * i:512 * i + 512], ["cv%d" % i], ["qcv%d" % i])

    def owner_rows(step):
        if step == 0:
            j = ts(T.pa1[:], T.jrow[:, 1:17], PM, BIG2, A.is_equal, A.mult, ["jrow", "pc"], ["pa1"])
            ts(T.pa2[:], T.jrow[:, 0:16], PM, -M2, A.is_equal, A.mult, ["jrow", "pc"], ["pa2"], j)
        elif step == 1:
            j = ts(T.sp[:], T.cl[:], PM, None, A.add, None, ["cl", "pc"], ["sp"])
            ts(C16, PM, 15.0, M2, A.is_lt, A.mult, ["pc"], ["c16"], j)
            ts(A16, PA, 16.0, None, A.mult, None, ["pc"], ["a16"], j)
            tt(T.pat4[:], T.pa1[:], T.pa2[:], A.add, ["pa1", "pa2"], ["pat4"])
            act(T.d16[:], T.pat4[:].indirect(T.opm[:]), ["pat4", "opm"], ["d16"])
        elif step == 2:
            ts(T.r7[:], T.r6[:], A16, 160.0, A.add, A.is_ge, ["r6", "a16"], ["r7"])
        elif step == 3:
            ts(T.r7[:], T.r7[:], -160.0, A16, A.mult, A.add, ["r7", "a16"], ["r7"])
        elif step == 4:
            tt(T.r7[:], T.r7[:], T.r6[:], A.add, ["r7", "r6"], ["r7"])
        else:
            j = cp(T.lv[:], T.r7[:], ["r7"], ["lv"])
            ts(T.thr[:], T.th0[:], C16, None, A.subtract, None, ["th0", "c16"], ["thr"], j)

    def units(b):
        qz(part(T.qe, T.se, b)[0], part(T.qe, T.se, b)[1], T.ez[:, 3 - b:515 - b], ["ez"], ["qe%d" % b])

    DH = ["dh0", "dh1"]
    WM = [["wm0", "wm3"], ["wm1"], ["wm2", "wm4"]]

    def scores(h, b):
        mx(b, T.qu[:], T.su[:], half(h)[0], half(h)[1], ["qu", "qx%d" % h])

    def signs(b):
        ts(T.sg[:, 0:H], bank(b), 0.0, None, A.is_gt, None, ["B%d" % b], ["sg"])

    def keys(kb):
        qz(T.qs[:], T.ss[:], T.sg[:], ["sg", "sgz"], ["qs"])
        mx(kb, T.qck[:], T.sck[:], T.qs[:], T.ss[:], ["qck", "qs"], w=128)

    def addresses(kb, hu):
        return [lambda: scan(T.ks[:, 5:45], T.d4[:, 0:40], bank(kb, 40), 0.0, A.add, A.min, ["d4", "B%d" % kb], ["ks"]),
                lambda: tt(T.yk[:], T.ks[:, 8:45].indirect(T.lk[:, 0:3]), T.crow[:], A.mult, ["ks", "lk", "crow0"], ["yk"]),
                lambda: ts(T.hd[:], T.yk[:], 8, 63, A.logical_shift_right, A.bitwise_and, ["yk"], ["hd"]),
                lambda: cp(T[hu][:], T.hd[:], ["hd"], [hu])]

    def writers_addresses(kb, hu):
        steps = addresses(kb, hu)
        for step in (steps[0], gap, steps[1], gap, steps[2]):
            step()
        ts(T.dg[:], T.yk[:, 0:32], 12, 3, A.logical_shift_right, A.bitwise_and, ["yk"], ["dg"])
        steps[3]()
        gap()
        ts(T.du[:], T.dg[:], 7.0, 6.0, A.mult, A.add, ["dg"], ["du"])

    def writers_digits(hu):
        for f, k, a, b, key in ((cp, 2, 0, 6, "wm2"), (act, 2, 6, 10, "wm4"), (cp, 0, 0, 6, "wm0"), (act, 0, 6, 10, "wm3"), (act, 1, 0, 10, "wm1")):
            f(T.wm[:, TH * k + 16 * a:TH * k + 16 * b], T.wtab[:].indirect(T[hu][:, 16 * k + a:16 * k + b]), ["wtab", hu], [key])

    def first_readers():
        qz(half(1)[0], half(1)[1], T.xt[:, 640:1280], ["xt1"], ["qx1"])
        scores(1, 3)

    ra = addresses(3, "hu3")
    un = [lambda b=b: units(b) for b in range(4)]
    ft = [lambda i=i: flag_tile(i) for i in range(2)]
    spare = [ft[0], ft[1], first_readers, lambda: signs(3), lambda: keys(3), ra[0]] + un + [ra[1], ra[2], ra[3]]

    def gap(n=1):
        for i in range(min(n, len(spare))):
            spare.pop(0)()

    def decode(b0, order, c, s, key, start=True, stop=True):
        for b in order:
            mx(b0 + b, part(T.qe, T.se, b)[0], part(T.qe, T.se, b)[1], c, s, ["qe%d" % b, key], start, stop)

    def plane(s, b):
        return T["w%d" % s][:, 512 * b + 16:512 * b + 496:3]

    def window(s, b):
        return T["w%d" % s][:, 512 * b + 16:512 * b + 497]

    def term(u, k):
        return T.e3[:, 480 * u + k:480 * u + 480:3]

    def writers_numbers(t):
        event("rq%d" % t, 2 * nin, (), ["lq%d" % t])
        decode(4, range(4), T["lq%d" % t][:], T["ls%d" % t][:], "lq%d" % t)
        for b in range(4):
            shrink("A", plane(0, b), 4 + b, ["w0%d" % b])

    def writers_copies(o):
        for u in range(8):
            b = u % 4
            if MODE[u] == "S":
                act(term(u, 0), bank(4 + b), ["B%d" % (4 + b)], ["e3%d0" % u], scale=SMALL if u > 3 else -SMALL)
            elif u < 4:
                shrink("A", third(T.tx, b), 4 + b, ["tx%d" % b])
        decode(4, range(4), half(o)[0], half(o)[1], "qx%d" % o, True, False)

    def cells():
        tt(T.hb[:], T.hd[:], T.k64[:], A.add, ["hd", "k64"], ["hb"])

    def choices():
        h = [lst(T.hb, k) for k in range(3)]
        j = None
        for at, x, y in ((0, h[0], h[1]), (1, h[1], h[2]), (2, h[2], T.sp[:]), (40, h[1], h[0]), (42, h[2], h[1])):
            j = tt(T.dh[:, at:at + 37:4], x, y, A.subtract, ["hb", "sp"], ["dh0"], j)
        j = None
        for at, x in ((3, T.sp[:]), (41, h[0]), (43, h[1])):
            j = act(T.dh[:, at:at + 37:4], x, ["hb", "sp"], ["dh1"], join=j)

    def peel(p, hu, b, wide=H):
        src = "dec" if p else "wm"
        for what, k in [(x[0], int(x[1])) for x in PEEL[p > 0].split()]:
            x, xk = (third(T.dec, k, H, TH), ["dec%d" % k]) if p else (third(T.wm, k, H, TH), WM[k])
            if what == "d":
                tt(x, third(T.wm, k, H, TH), bank(b), A.max, WM[k] + ["B%d" % b], xk)
            elif what == "s":
                j = None
                for c in range(3):
                    at = SC * k + 2 * (2 * c + 1)
                    off, key = (T.ps[:, 512 * b + c:512 * b + TH:3], "B%d" % b) if p else (T.z60[:], "z60")
                    j = scan(T.sc[:, at:at + 7 * 59 + 1:7], T[src][:, TH * k + c:TH * k + TH:3], off, float(-MID[0]),
                             A.add, A.subtract, [key, src + "z"] + xk, ["sc%d" % k], j)
            elif what == "t":
                at = SC * k + S0
                scan(third(T.tab, k, 28, 40), T.sc[:, at:at + 56:2], T.sc[:, at + 14:at + 70:2], 0.0, A.add, A.subtract,
                     ["sch", "scz", "sc%d" % k], ["tab%d" % k])
            elif what == "l":
                tt(T.lone[:], third(T.tab, k, 28, 40).indirect(T.oq[:]), T.wtab[:], A.is_equal, ["tab%d" % k, "oq", "wtab"], ["lone"])
                act(T.fl[:, k:640:4], T.lone[:].indirect(lst(T[hu], k)), ["lone", hu], ["fl%d" % k])
            else:
                tt(T.fl[:, k:640:4], third(T.tab, k, 28, 40).indirect(lst(T.du, k)), x, A.is_equal, ["tab%d" % k, "du"] + xk, ["fl%d" % k])
        gap()
        qz(T.qf[:, 0:wide], T.sf[:, 0:wide], T.fl[:, 0:4 * wide], ["fl0", "fl1", "fl2", "flz"], ["qf"])
        for i, bk in enumerate((1, 0, 2)):
            if i >= p:
                c, n = (1, H) if i == 2 else (0, TH)
                mx(bk, part(T.qcv, T.scv, c)[0], part(T.qcv, T.scv, c)[1], T.qf[:, 0:n], T.sf[:, 0:n], ["qcv%d" % c, "qf"],
                   start=p == 0, stop=p == i, w=n)

    def lists(x, ot, lo, hr, keys):
        e = {"V": cp, "A": act}.get(x[1:2])
        if x[0] == "P":
            a, b = int(x[2:4]), int(x[4:6])
            at = 20 - 20 * (a // 10)
            e(T.pab[:, 16 * a:16 * b], ot[:, 0:192].indirect(lo[:, at + a:at + b]), keys, ["pab%d" % a])
        elif x[0] == "k":
            k = int(x[2])
            e(third(T.cg, k), ot[:, 64 * k:64 * k + 64].indirect(lst(T[hr], k)), [keys[0], hr], ["cg%d" % k])
        elif x[0] == "S":
            i = int(x[1])
            scan(third(T.pabs, i), T.d16[:], third(T.pab, i), 0.0, A.add, A.min,
                 ["d16"] + ["pab%d" % a for a in range(10 * i, 10 * i + 10)], ["pabs%d" % i])
        elif x[0] == "m":
            k = int(x[1])
            scan(third(T.cs, k), T.d16[:], third(T.cg, k), 0.0, A.add, A.min, ["d16", "cg%d" % k], ["cs%d" % k])
        elif x[0] == "U":
            i = int(x[1])
            ts(T.pabu[:, 10 * i:10 * i + 10], T.pabs[:, H * i + 15:H * i + H:16], C16, 3.0, A.add, A.mult, ["pabs%d" % i, "c16"], ["pabu%d" % i])
        else:
            ts(T.cu[:], T.cs[:, 15:480:16], C16, 3.0, A.add, A.mult, ["cs0", "cs1", "cs2", "c16"], ["cu"])

    def table(x):
        what, p, b = x[0], int(x[1]), int(x[2])
        u, i = 4 * p + b, int(what in "bv")
        c, ck = window(p, b).indirect(T.pabu[:, 10 * i:10 * i + 10]), ["w%dz" % p, "w%d%d" % (p, b), "pabu%d" % i]
        if what in "ab":
            act(term(u, 1 + i), c, ck, ["e3%d%d" % (u, 1 + i)])
        elif what == "s":
            scan(T["w%d" % (p + 1)][:, 512 * b + 14:512 * b + 494], T.m3[:], T.e3[:, 480 * u:480 * u + 480], 0.0, A.mult, A.add,
                 ["m3"] + ["e3%d%d" % (u, k) for k in range(3)], ["w%d%d" % (p + 1, b)])
        elif what == "t":
            tt(third(T.tq, b), c, plane(0, b) if p else third(T.tx, b), A.add if p else A.subtract,
               ck + ["w0%d" % b if p else "tx%d" % b], ["tq%d" % b])
        else:
            tt(plane(p + 1, b), c, third(T.tq, b), A.add, ck + ["tq%d" % b], ["w%d%d" % (p + 1, b)])

    def read(x):
        if x[0] == "r":
            b, a, c = int(x[2]), int(x[3]), int(x[4])
            (cp if x[1] == "V" else act)(T.gt[:, 640 * a + b:640 * c:4], window(2, b).indirect(T.cu[:, 10 * a:10 * c]),
                                         ["w2z", "w2%d" % b, "cu"], ["gt%d%d" % (k, b) for k in range(a, c)])
        elif x[0] == "q":
            k = int(x[1])
            qz(third(T.qz, k), third(T.sz, k), third(T.gt, k, 640, 640), ["gt%d%d" % (k, b) for b in range(4)], ["qz%d" % k])
            decode(0, (2, 3, 0, 1), third(T.qz, k), third(T.sz, k), "qz%d" % k, k == 0, k == 2)
        else:
            shrink(x[1], T.ft[:, int(x[2]):640:4], int(x[2]), ["ft" + x[2]])

    def store(h, qs):
        lo = H * h
        j = dma(qs[0], T.oc[:, 4 * lo:4 * lo + 4 * H], half(h)[0].bitcast(dt.uint8), ["qx%d" % h], ())
        js = {qs[0]: j}
        for k in range(4):
            q = qs[1 + k]
            js[q] = dma(q, T.osc[4 * k:4 * k + 4, lo:lo + H], T.sx[32 * k:32 * k + 4, lo:lo + H], ["qx%d" % h], (), js.get(q))
        return js

    for t in range(R):
        w, o = t % 2, 1 - t % 2
        hu, hr = "hu%d" % t, "hu%d" % ((t - 1) % 4)
        ot, so, lo = T["ot%d" % t], T["so%d" % t], T["lo%d" % t]
        scores(w, 0)
        if t == 0:
            peel_fills()
        send([(T["lq%d" % t][:].bitcast(dt.uint8), half(w)[0].bitcast(dt.uint8)), (T["ls%d" % t][:], half(w)[1])],
             "rq%d" % t, "sq%d" % t, ["qx%d" % w])
        if t == 0:
            late_fills()
            key_tile()
        signs(0)
        if t == 0:
            digits()
        keys(1)
        if t == 0:
            address_rows()
        if t == 2:
            store(0, "SSSSS")
            mx(3, T.qv[:], T.sv[:], half(0)[0], half(0)[1], ["qv", "qx0"])
        writers_addresses(1, hu)
        writers_digits(hu)
        peel(0, hu, None, TH if t == 0 else H)
        if t == 0:
            owner_rows(0)
        cells()
        gap()
        if t == 0:
            owner_rows(1)
        else:
            writers_numbers(t)
        peel(1, hu, 1)
        if t == 0:
            owner_rows(2)
        choices()
        if t == 0:
            owner_rows(3)
        else:
            writers_copies(o)
        gap()
        peel(2, hu, 0)
        if t == 0:
            owner_rows(4)
        gap(2)
        if t == 0:
            owner_rows(5)
        if t == 2:
            act(T.yb[:, 0:H], bank(3), ["B3"], ["yb0"])
            dma("S", T.y[:, 0:H], T.yb[:, 0:H], ["yb0"], ())
        scan(T.vs[:], T.d16[:], bank(2), 0.0, A.add, A.min, ["d16", "B2"], ["vs"])
        gap()
        tt(T.mm[:], T.vs[:].indirect(T.lv[:, 0:5]), T.thr[:], A.is_ge, ["vs", "lv", "thr"], ["mm"])
        gap()
        scan(T.sel[:], T.mm[:], T.dh[:], 0.0, A.mult, A.add, ["mm"] + DH, ["sel"])
        gap()
        j = cp(so[:, 0:20], T.sel[:, 3:80:4], ["sel"], ["so%d" % t])
        cp(so[:, 20:30], T.sel[:, 41:80:4], ["sel"], (), j)
        send([(lo[:], so[:])], "ro%d" % t, "so%d" % t, ["so%d" % t])
        if t == 0:
            writers_numbers(0)
            writers_copies(o)
            gap(len(spare))
        if t == 1:
            qz(T.qv[:], T.sv[:], T.vt[:], ["vt"], ["qv"])
        okey, lkey = "ot%d" % t, "lo%d" % t
        event("ro%d" % t, nin, (), [lkey])
        cp(ot[:].indirect(lo[:, 0:10]), T.idrow[:], [lkey, "idrow"], [okey])
        for x in (LISTS + " " + TABLE + " " + READ).split():
            if x[0] in "abstv":
                table(x)
            elif x[0] in "rqe":
                read(x)
            else:
                lists(x, ot, lo, hr, [okey, lkey])
        qz(T.qg[:], T.sq[:], T.ft[:], ["ft0", "ft1", "ft2", "ft3"], ["qg"])
        for b in (2, 0, 3, 1):
            mx(4 + b, T.qw[:, 128 * b:128 * b + 128], T.sw[:, 128 * b:128 * b + 128], T.qg[:], T.sq[:], ["qw", "sw", "qg"], start=False)
        for b in (0, 1):
            shrink("V", T.xn[:, b:640:4], 4 + b, ["xn%d" % b])
            shrink("A", T.xn[:, b + 2:640:4], 6 + b, ["xn%d" % (b + 2)])
        if t == R - 1:
            for grp in sorted(last.values(), key=lambda x: -x["id"]):
                wait("G", grp)
        qz(half(o)[0], half(o)[1], T.xn[:], ["xn0", "xn1", "xn2", "xn3"], ["qx%d" % o])

    mx(0, T.qv[:], T.sv[:], half(1)[0], half(1)[1], ["qv", "qx1"])
    js = store(1, "SSAAA")
    cp(T.yb[:, H:2 * H], bank(0), ["B0"], ["yb1"])
    dma("S", T.y[:, H:2 * H], T.yb[:, H:2 * H], ["yb1"], (), js["S"])
    for q in js:
        wait(q, js[q])
